import numpy as np
import ml_dtypes


def mxq(x, axis, fmt="e4m3"):
    dtype, down = {"e4m3": (ml_dtypes.float8_e4m3fn, 7), "e5m2": (ml_dtypes.float8_e5m2, 14)}[fmt]
    v = np.moveaxis(np.asarray(x, np.float32).astype(ml_dtypes.bfloat16).astype(np.float64), axis, -1)
    blocks = v.reshape(v.shape[:-1] + (-1, 32))
    amax = np.abs(blocks).max(-1, keepdims=True)
    byte = np.maximum(np.where(amax > 0, np.frexp(amax)[1] - 1 + 127, 0) - down, 1)
    scale = np.exp2(byte - 127.0)
    codes = (blocks / scale).astype(np.float32).astype(dtype).astype(np.float64)
    return np.moveaxis((codes * scale).reshape(v.shape), -1, axis)


WIDE = False


def mx_kscale(k):
    if not WIDE:
        return np.ones(k)
    levels = np.array([10, -10, 5, -5, 0])
    if k % 512:
        return np.exp2(np.random.permutation(np.resize(levels, k // 32))).repeat(32)
    a = np.empty((k // 512, 16))
    for p in range(k // 512):
        a[p, :8] = np.random.permutation(np.resize(levels, 8))
        for g in range(8):
            far = levels[np.abs(levels - a[p, g]) >= 10]
            a[p, g + 8] = far[np.random.randint(len(far))]
    return np.exp2(a.ravel()).repeat(32)


def f64(x):
    return np.asarray(x).astype(np.float64)


def striped(idx):
    return np.tile(idx.reshape(-1, 16).T, (8, 1)).astype(np.uint16)


def unstriped(offs):
    return offs[:16].T.reshape(-1).astype(np.int64)


E2M1 = np.array([0.0, 0.5, 1.0, 1.5, 2.0, 3.0, 4.0, 6.0, -0.0, -0.5, -1.0, -1.5, -2.0, -3.0, -4.0, -6.0])


def pack_weight(w, fmt):
    k, n = w.shape
    w = f64(np.asarray(w, np.float32).astype(ml_dtypes.bfloat16)).reshape(k // 32, 32, n)
    amax = np.abs(w).max(1)
    if fmt == "e4m3":
        byte = np.frexp(amax)[1] - 1 + 127 - 7
    else:
        mant, ex = np.frexp(amax / 6.0)
        byte = np.where(mant > 0.5, ex, ex - 1) + 127
    byte = np.clip(np.where(amax > 0, byte, 1), 1, 254)
    scaled = (w * np.exp2(127.0 - byte)[:, None, :]).reshape(k, n).astype(np.float32)
    by_word = np.ascontiguousarray(scaled.reshape(k // 512, 128, 4, n).transpose(0, 1, 3, 2))
    if fmt == "e4m3":
        words = by_word.astype(ml_dtypes.float8_e4m3fn).view(np.uint8)
    else:
        c = by_word.astype(ml_dtypes.float4_e2m1fn).view(np.uint8) & 0xF
        words = (c[..., 0::2] | (c[..., 1::2] << 4)).reshape(k // 512, 128, 2 * n)
    return np.ascontiguousarray(words), np.ascontiguousarray(byte.astype(np.uint8).reshape(k // 512, 16, n))


def unpack_weight(words, scales, fmt):
    g, _, n = scales.shape
    words = np.ascontiguousarray(words).reshape(g, 128, n, -1)
    if fmt == "e4m3":
        vals = words.view(ml_dtypes.float8_e4m3fn).astype(np.float64)
    else:
        nib = np.empty((g, 128, n, 4), np.uint8)
        nib[..., 0::2] = words & 0xF
        nib[..., 1::2] = words >> 4
        vals = E2M1[nib]
    vals = vals * np.repeat(np.exp2(scales.astype(np.float64) - 127.0), 8, axis=1)[..., None]
    return vals.transpose(0, 1, 3, 2).reshape(g * 512, n)


def relu2(v):
    return np.maximum(v, 0.0) ** 2


K, T, E, C, H, N = 1024, 1024, 4, 256, 512, 384


def by_expert(wq, xq):
    return np.concatenate([wq[e].T @ xq[:, e * C:(e + 1) * C] for e in range(E)], axis=1)


def setup_inputs():
    n = np.random.standard_normal
    s = mx_kscale(K)[:, None]
    u = mx_kscale(H)
    x = pack_weight(n((K, T)) * s, "e4m3")
    return {
        "x_words": x[0],
        "x_scales": x[1],
        "w1": (n((E, K, H)) / np.sqrt(K) / s[None] * u[None, None, :]).astype(np.float32),
        "w2": (n((E, H, N)) / np.sqrt(H) / u[None, :, None] ** 2).astype(np.float32),
        "gate": np.tile(np.random.uniform(0.2, 1.0, E * C), (N, 1)).astype(np.float32),
        "offs": striped(np.random.permutation(T)[:E * C]),
    }


def reference(x_words, x_scales, w1, w2, gate, offs):
    idx = unstriped(offs)
    xq = unpack_weight(x_words, x_scales, "e4m3")[:, idx]
    h = relu2(by_expert(mxq(f64(w1), 1, "e4m3"), xq))
    y = by_expert(mxq(f64(w2), 1, "e4m3"), mxq(h, 0, "e4m3"))
    out = np.zeros((N, T))
    out[:, idx] = f64(gate) * y
    return out

@@ -1,0 +1,405 @@
+from contextlib import ExitStack
+
+import concourse.mybir as mybir
+
+K, T, E, C, H, N = 1024, 1024, 4, 256, 512, 384
+FLOPS = 2 * E * C * (K * H + H * N)
+
+F32 = mybir.dt.float32
+BF16 = mybir.dt.bfloat16
+I32 = mybir.dt.int32
+U32 = mybir.dt.uint32
+U16 = mybir.dt.uint16
+U8 = mybir.dt.uint8
+FP8X4 = mybir.dt.float8_e4m3fn_x4
+ACT = mybir.ActivationFunctionType
+ALU = mybir.AluOpType
+
+P = 128
+PACK = 4
+K_PASS = P * PACK
+PASSES = K // K_PASS
+HALF = 128
+NB = N // P
+GROUP = 16
+STREAM_BUFS = 32
+HEAD_BUFS = 16
+
+
+def tile_moe_pkd_mlp_relu2_kernel(tc, x_words, x_scales, w1, w2, gate, offs, out):
+    nc = tc.nc
+    with ExitStack() as ctx:
+        keep = ctx.enter_context(tc.tile_pool(name="keep", bufs=1))
+        ring = ctx.enter_context(tc.tile_pool(name="ring", bufs=STREAM_BUFS))
+        psum = ctx.enter_context(tc.psum_pool(name="psum", bufs=4))
+
+        offsets = keep.tile([P, E * C // GROUP], U16, name="offsets")
+        nc.sync.dma_start(offsets[:], offs)
+
+        def stream(shape, dtype):
+            return ring.tile(shape, dtype, name="stream", align_bytes=64)
+
+        def head(shape, dtype):
+            return ring.tile(shape, dtype, name="head", align_bytes=64, bufs=HEAD_BUFS)
+
+        def slots(s0, s1):
+            return offsets[:, s0 // GROUP : s1 // GROUP]
+
+        xs_win = keep.tile([P, T], U8, name="xs_win", align_bytes=64)
+        nc.vector.memset(xs_win[:].bitcast(I32), 0)
+        for q in range(4):
+            nc.sync.dma_start(
+                out=xs_win[32 * q : 32 * q + 4 * PASSES, :].bitcast(I32),
+                in_=x_scales[:, 4 * q : 4 * q + 4, :].bitcast(I32),
+            )
+
+        xw_win = [keep.tile([P, T], I32, name="xw_win%d" % g, align_bytes=64) for g in range(PASSES)]
+        raw1 = {}
+        raw2 = {}
+        gates = {}
+
+        def load_x(g):
+            nc.sync.dma_start(out=xw_win[g][:], in_=x_words[g].rearrange("p t r -> p (t r)").bitcast(I32))
+
+        def load_w1(e, g, c0, c1):
+            rows = w1[e, g * K_PASS : (g + 1) * K_PASS, :].rearrange("(p j) c -> p j c", j=PACK)
+            t = keep.tile([P, PACK, c1 - c0], F32, name="raw1_%d_%d_%d" % (e, g, c0))
+            nc.sync.dma_start(out=t[:], in_=rows[:, :, c0:c1])
+            raw1.setdefault((e, g), []).append((c0, c1, t))
+
+        def load_w2(e):
+            raw2[e] = keep.tile([P, PACK, N], F32, name="raw2_%d" % e)
+            nc.sync.dma_start(out=raw2[e][:], in_=w2[e].rearrange("(p j) c -> p j c", j=PACK))
+
+        def load_gate(e, b):
+            gates[e, b] = keep.tile([P, C], F32, name="gate%d_%d" % (e, b))
+            nc.sync.dma_start(out=gates[e, b][:], in_=gate[b * P : (b + 1) * P, e * C : (e + 1) * C])
+
+        xw = {}
+        xs = {}
+
+        def gather_scales(e):
+            xs[e] = head([P, C], U8)
+            nc.vector.tensor_copy(xs[e][:], xs_win[:].indirect(slots(e * C, (e + 1) * C)))
+
+        def gather_words(e, g):
+            xw[e, g] = head([P, C], U32)
+            nc.vector.tensor_copy(xw[e, g][:], xw_win[g][:].bitcast(U32).indirect(slots(e * C, (e + 1) * C)))
+
+        def cast(engine, dst, src):
+            if engine == "vector":
+                nc.vector.tensor_copy(out=dst, in_=src)
+            elif engine == "gpsimd":
+                nc.gpsimd.tensor_scalar(out=dst, in0=src, scalar1=1.0, scalar2=0.0, op0=ALU.mult, op1=ALU.add)
+            else:
+                nc.scalar.activation(out=dst, in_=src, func=ACT.Copy)
+
+        w1b = {}
+        w1c = {}
+        w1s = {}
+
+        def cast_w1(e, g, u, c0, c1, engine):
+            if (e, g, u) not in w1b:
+                w1b[e, g, u] = stream([P, 2 * P * PACK], BF16)
+            dst = w1b[e, g, u][:].rearrange("p (t m j) -> p m j t", t=2, j=PACK)
+            for r0, r1, raw in raw1[e, g]:
+                if r0 <= c0 and c1 <= r1:
+                    src = raw[:].rearrange("p j (m t) -> p m j t", t=PACK)
+                    cast(
+                        engine,
+                        dst[:, c0 // PACK : c1 // PACK],
+                        src[:, (c0 - r0) // PACK : (c1 - r0) // PACK, :, 2 * u : 2 * u + 2],
+                    )
+
+        def quant_w1(e, g, u):
+            w1c[e, g, u] = keep.tile([P, 2 * P], U32, name="w1c%d_%d_%d" % (e, g, u), align_bytes=64)
+            w1s[e, g, u] = (head if e == 0 else stream)([P, 2 * P], U8)
+            nc.vector.quantize_mx(out=w1c[e, g, u][:].bitcast(FP8X4), scales=w1s[e, g, u][:], in_=w1b[e, g, u][:])
+
+        w2b = {}
+        w2c = {}
+        w2s = {}
+
+        def cast_w2(e, c0, c1, engine):
+            w2b[e, c0] = stream([P, (c1 - c0) * PACK], BF16)
+            cast(
+                engine,
+                w2b[e, c0][:].rearrange("p (c i j) -> p c j i", i=4, j=PACK),
+                raw2[e][:, :, c0:c1].rearrange("p j (c i) -> p c j i", i=4),
+            )
+
+        def quant_w2(e, c0, c1):
+            codes = keep.tile([P, c1 - c0], U32, name="w2c%d_%d" % (e, c0), align_bytes=64)
+            scales = stream([P, c1 - c0], U8)
+            nc.vector.quantize_mx(out=codes[:].bitcast(FP8X4), scales=scales[:], in_=w2b[e, c0][:])
+            for b in range(c0 // P, c1 // P):
+                w2c[e, b] = codes[:, b * P - c0 : (b + 1) * P - c0]
+                w2s[e, b] = scales[:, b * P - c0 : (b + 1) * P - c0]
+
+        acc1 = {}
+        relus = {}
+        hb = {}
+        hc = {}
+        hs = {}
+
+        def mm1(e, s0):
+            acc = psum.tile([P, PACK, HALF], F32, name="acc1")
+            acc1[e, s0] = acc
+            for t in range(PACK):
+                for g in range(PASSES):
+                    nc.tensor.matmul_mx(
+                        out=acc[:, t, :],
+                        lhsT=w1c[e, g, t // 2][:, t % 2 * P : (t % 2 + 1) * P].bitcast(FP8X4),
+                        lhsT_scale=w1s[e, g, t // 2][:, t % 2 * P : (t % 2 + 1) * P],
+                        rhs=xw[e, g][:, s0 : s0 + HALF].bitcast(FP8X4),
+                        rhs_scale=xs[e][4 * g : P, s0 : s0 + HALF],
+                        start=(g == 0),
+                        stop=(g == PASSES - 1),
+                    )
+
+        def relu(e, s0, engine):
+            relus[e, s0] = stream([P, HALF, PACK], F32)
+            src = acc1[e, s0][:].rearrange("p t s -> p s t")
+            if engine == "vector":
+                nc.vector.tensor_scalar(out=relus[e, s0][:], in0=src, scalar1=0.0, scalar2=None, op0=ALU.max)
+            else:
+                nc.scalar.activation(out=relus[e, s0][:], in_=src, func=ACT.Relu)
+
+        def square(e, s0):
+            hb[e, s0] = stream([P, HALF * PACK], BF16)
+            nc.scalar.activation(
+                out=hb[e, s0][:],
+                in_=relus[e, s0][:].rearrange("p s t -> p (s t)"),
+                func=ACT.Square,
+            )
+
+        def quant_h(e, s0):
+            s1 = s0 + HALF
+            if e not in hc:
+                hc[e] = keep.tile([P, C], U32, name="hc%d" % e, align_bytes=64)
+                hs[e] = stream([P, C], U8)
+            nc.vector.quantize_mx(
+                out=hc[e][:, s0:s1].bitcast(FP8X4), scales=hs[e][:, s0:s1], in_=hb[e, s0][:]
+            )
+
+        acc2 = {}
+        ys = {}
+
+        def mm2(e, b, s0, s1):
+            acc = psum.tile([P, s1 - s0], F32, name="acc2")
+            acc2[e, b, s0] = acc
+            nc.tensor.matmul_mx(
+                out=acc[:],
+                lhsT=w2c[e, b].bitcast(FP8X4),
+                lhsT_scale=w2s[e, b],
+                rhs=hc[e][:, s0:s1].bitcast(FP8X4),
+                rhs_scale=hs[e][:, s0:s1],
+                start=True,
+                stop=True,
+            )
+
+        def evac(e, b, s0, s1, gated):
+            ys[e, b, s0] = stream([P, s1 - s0], F32)
+            if gated:
+                nc.vector.tensor_tensor(ys[e, b, s0][:], acc2[e, b, s0][:], gates[e, b][:, s0:s1], ALU.mult)
+            else:
+                nc.scalar.activation(out=ys[e, b, s0][:], in_=acc2[e, b, s0][:], func=ACT.Copy)
+
+        def gating(e, b, s0, s1):
+            plain = ys[e, b, s0]
+            ys[e, b, s0] = stream([P, s1 - s0], F32)
+            nc.gpsimd.tensor_tensor(ys[e, b, s0][:], plain[:], gates[e, b][:, s0:s1], ALU.mult)
+
+        windows = [keep.tile([P, T], F32, name="window%d" % b) for b in range(NB)]
+
+        def scatter(e, b, s0, s1, gated):
+            dst = windows[b][:].indirect(slots(e * C + s0, e * C + s1))
+            if gated:
+                nc.vector.tensor_copy(dst, ys[e, b, s0][:])
+            else:
+                nc.vector.tensor_tensor(dst, ys[e, b, s0][:], gates[e, b][:, s0:s1], ALU.mult)
+
+        def store(b):
+            nc.sync.dma_start(out=out[b * P : (b + 1) * P, :], in_=windows[b][:])
+
+        load_w1(0, 0, 0, 256)
+        load_x(0)
+        load_w1(0, 0, 256, 512)
+        load_w1(0, 1, 0, 256)
+        load_w1(0, 1, 256, 512)
+        load_x(1)
+        load_w2(0)
+        load_w1(1, 0, 0, 512)
+        load_w1(1, 1, 0, 512)
+        load_gate(0, 1)
+        load_w1(2, 0, 0, 512)
+        load_gate(0, 2)
+        load_gate(0, 0)
+        load_gate(1, 0)
+        load_w2(1)
+        load_w1(2, 1, 0, 512)
+        load_w2(2)
+        load_gate(1, 2)
+        load_w1(3, 1, 0, 512)
+        load_gate(2, 1)
+        load_w1(3, 0, 0, 512)
+        load_gate(1, 1)
+        load_gate(3, 2)
+        load_gate(2, 0)
+        load_w2(3)
+        load_gate(3, 1)
+        load_gate(2, 2)
+        load_gate(3, 0)
+        gather_scales(0)
+        gather_scales(1)
+        gather_scales(2)
+        gather_scales(3)
+        cast_w1(0, 0, 0, 0, 256, "scalar")
+        cast_w1(0, 0, 1, 0, 256, "scalar")
+        gather_words(0, 0)
+        gather_words(1, 0)
+        gather_words(2, 0)
+        gather_words(3, 0)
+        cast_w1(0, 0, 0, 256, 512, "scalar")
+        cast_w1(0, 0, 1, 256, 512, "scalar")
+        quant_w1(0, 0, 0)
+        quant_w1(0, 0, 1)
+        cast_w1(0, 1, 0, 0, 256, "scalar")
+        cast_w1(0, 1, 1, 0, 256, "scalar")
+        cast_w1(0, 1, 0, 256, 512, "scalar")
+        cast_w1(0, 1, 1, 256, 512, "vector")
+        quant_w1(0, 1, 0)
+        quant_w1(0, 1, 1)
+        gather_words(0, 1)
+        gather_words(1, 1)
+        gather_words(2, 1)
+        gather_words(3, 1)
+        cast_w2(0, 0, 256, "scalar")
+        mm1(0, 0)
+        mm1(0, 128)
+        relu(0, 0, "vector")
+        quant_w2(0, 0, 256)
+        cast_w2(0, 256, 384, "vector")
+        relu(0, 128, "scalar")
+        cast_w1(1, 0, 1, 0, 512, "vector")
+        square(0, 0)
+        square(0, 128)
+        quant_w2(0, 256, 384)
+        quant_w1(1, 0, 1)
+        quant_h(0, 128)
+        cast_w1(1, 1, 0, 0, 512, "vector")
+        quant_h(0, 0)
+        cast_w1(1, 0, 0, 0, 512, "scalar")
+        mm2(0, 1, 0, 128)
+        mm2(0, 1, 128, 256)
+        quant_w1(1, 0, 0)
+        evac(0, 1, 0, 128, False)
+        mm2(0, 2, 128, 256)
+        quant_w1(1, 1, 0)
+        evac(0, 2, 128, 256, False)
+        scatter(0, 1, 0, 128, False)
+        cast_w1(1, 1, 1, 0, 512, "scalar")
+        mm2(0, 0, 128, 256)
+        mm2(0, 2, 0, 128)
+        quant_w1(1, 1, 1)
+        evac(0, 1, 128, 256, False)
+        mm1(1, 0)
+        evac(0, 0, 128, 256, False)
+        cast_w1(2, 0, 1, 0, 512, "scalar")
+        mm1(1, 128)
+        scatter(0, 0, 128, 256, False)
+        scatter(0, 2, 128, 256, False)
+        quant_w1(2, 0, 1)
+        relu(1, 128, "vector")
+        cast_w1(2, 0, 0, 0, 512, "scalar")
+        relu(1, 0, "scalar")
+        cast_w2(1, 256, 384, "vector")
+        quant_w1(2, 0, 0)
+        evac(0, 2, 0, 128, False)
+        cast_w2(1, 0, 256, "scalar")
+        mm2(0, 0, 0, 128)
+        quant_w2(1, 0, 256)
+        square(1, 128)
+        square(1, 0)
+        cast_w1(2, 1, 1, 0, 512, "vector")
+        quant_w2(1, 256, 384)
+        quant_h(1, 128)
+        quant_h(1, 0)
+        mm2(1, 2, 0, 256)
+        evac(0, 0, 0, 128, False)
+        quant_w1(2, 1, 1)
+        cast_w1(2, 1, 0, 0, 512, "scalar")
+        evac(1, 2, 0, 256, False)
+        quant_w1(2, 1, 0)
+        cast_w2(2, 0, 256, "scalar")
+        quant_w2(2, 0, 256)
+        mm2(1, 0, 0, 256)
+        mm1(2, 0)
+        cast_w2(2, 256, 384, "scalar")
+        evac(1, 0, 0, 256, False)
+        cast_w1(3, 1, 0, 0, 512, "vector")
+        relu(2, 0, "scalar")
+        mm1(2, 128)
+        quant_w2(2, 256, 384)
+        mm2(1, 1, 0, 256)
+        relu(2, 128, "scalar")
+        square(2, 0)
+        square(2, 128)
+        quant_h(2, 0)
+        evac(1, 1, 0, 256, False)
+        cast_w1(3, 0, 1, 0, 512, "scalar")
+        scatter(0, 0, 0, 128, False)
+        quant_w1(3, 1, 0)
+        quant_w1(3, 0, 1)
+        cast_w1(3, 0, 0, 0, 512, "scalar")
+        quant_w1(3, 0, 0)
+        quant_h(2, 128)
+        mm2(2, 2, 0, 256)
+        mm2(2, 0, 0, 256)
+        evac(2, 0, 0, 256, False)
+        cast_w1(3, 1, 1, 0, 512, "scalar")
+        mm2(2, 1, 0, 256)
+        evac(2, 1, 0, 256, False)
+        scatter(0, 1, 128, 256, False)
+        scatter(1, 0, 0, 256, False)
+        scatter(0, 2, 0, 128, False)
+        quant_w1(3, 1, 1)
+        evac(2, 2, 0, 256, False)
+        mm1(3, 0)
+        mm1(3, 128)
+        cast_w2(3, 0, 256, "scalar")
+        quant_w2(3, 0, 256)
+        scatter(1, 2, 0, 256, False)
+        relu(3, 0, "scalar")
+        relu(3, 128, "scalar")
+        square(3, 0)
+        cast_w2(3, 256, 384, "scalar")
+        scatter(1, 1, 0, 256, False)
+        quant_h(3, 0)
+        mm2(3, 0, 0, 128)
+        scatter(2, 2, 0, 256, False)
+        scatter(2, 1, 0, 256, False)
+        quant_w2(3, 256, 384)
+        square(3, 128)
+        quant_h(3, 128)
+        evac(3, 0, 0, 128, False)
+        mm2(3, 2, 0, 128)
+        mm2(3, 1, 0, 128)
+        evac(3, 2, 0, 128, False)
+        mm2(3, 0, 128, 256)
+        scatter(2, 0, 0, 256, False)
+        mm2(3, 2, 128, 256)
+        mm2(3, 1, 128, 256)
+        evac(3, 0, 128, 256, False)
+        scatter(3, 2, 0, 128, False)
+        evac(3, 2, 128, 256, False)
+        scatter(3, 0, 0, 128, False)
+        scatter(3, 0, 128, 256, False)
+        scatter(3, 2, 128, 256, False)
+        evac(3, 1, 128, 256, False)
+        store(0)
+        evac(3, 1, 0, 128, False)
+        scatter(3, 1, 0, 128, False)
+        store(2)
+        scatter(3, 1, 128, 256, False)
+        store(1)

@@ -47,11 +47,13 @@ def tile_moe_pkd_mlp_relu2_kernel(tc, x_words, x_scales, w1, w2, gate, offs, out
 
         xs_win = keep.tile([P, T], U8, name="xs_win", align_bytes=64)
         nc.vector.memset(xs_win[:].bitcast(I32), 0)
-        for q in range(4):
-            nc.sync.dma_start(
-                out=xs_win[32 * q : 32 * q + 4 * PASSES, :].bitcast(I32),
-                in_=x_scales[:, 4 * q : 4 * q + 4, :].bitcast(I32),
-            )
+
+        def load_scales():
+            for q in range(4):
+                nc.sync.dma_start(
+                    out=xs_win[32 * q : 32 * q + 4 * PASSES, :].bitcast(I32),
+                    in_=x_scales[:, 4 * q : 4 * q + 4, :].bitcast(I32),
+                )
 
         xw_win = [keep.tile([P, T], I32, name="xw_win%d" % g, align_bytes=64) for g in range(PASSES)]
         raw1 = {}
@@ -222,184 +224,179 @@ def tile_moe_pkd_mlp_relu2_kernel(tc, x_words, x_scales, w1, w2, gate, offs, out
         def store(b):
             nc.sync.dma_start(out=out[b * P : (b + 1) * P, :], in_=windows[b][:])
 
-        load_w1(0, 0, 0, 256)
         load_x(0)
-        load_w1(0, 0, 256, 512)
-        load_w1(0, 1, 0, 256)
-        load_w1(0, 1, 256, 512)
         load_x(1)
+        load_w1(0, 0, 0, 512)
+        load_w1(0, 1, 0, 512)
+        load_scales()
+        load_w1(1, 1, 0, 512)
         load_w2(0)
         load_w1(1, 0, 0, 512)
-        load_w1(1, 1, 0, 512)
-        load_gate(0, 1)
-        load_w1(2, 0, 0, 512)
-        load_gate(0, 2)
-        load_gate(0, 0)
-        load_gate(1, 0)
         load_w2(1)
-        load_w1(2, 1, 0, 512)
-        load_w2(2)
+        load_gate(0, 1)
+        load_gate(0, 0)
         load_gate(1, 2)
+        load_gate(0, 2)
+        load_w1(2, 0, 0, 512)
+        load_w1(2, 1, 0, 512)
+        load_gate(1, 0)
+        load_w2(2)
         load_w1(3, 1, 0, 512)
-        load_gate(2, 1)
         load_w1(3, 0, 0, 512)
         load_gate(1, 1)
-        load_gate(3, 2)
-        load_gate(2, 0)
         load_w2(3)
+        load_gate(2, 0)
+        load_gate(2, 1)
+        load_gate(3, 2)
         load_gate(3, 1)
-        load_gate(2, 2)
         load_gate(3, 0)
-        gather_scales(0)
-        gather_scales(1)
-        gather_scales(2)
-        gather_scales(3)
-        cast_w1(0, 0, 0, 0, 256, "scalar")
-        cast_w1(0, 0, 1, 0, 256, "scalar")
+        load_gate(2, 2)
+        cast_w1(0, 0, 0, 0, 512, "vector")
         gather_words(0, 0)
         gather_words(1, 0)
+        gather_words(3, 1)
+        cast_w1(0, 0, 1, 0, 512, "scalar")
+        cast_w1(0, 1, 0, 0, 512, "vector")
         gather_words(2, 0)
-        gather_words(3, 0)
-        cast_w1(0, 0, 0, 256, 512, "scalar")
-        cast_w1(0, 0, 1, 256, 512, "scalar")
+        gather_words(2, 1)
+        gather_words(1, 1)
+        gather_words(0, 1)
         quant_w1(0, 0, 0)
+        gather_scales(0)
+        cast_w1(0, 1, 1, 0, 512, "scalar")
+        cast_w1(1, 1, 1, 0, 512, "vector")
+        cast_w1(1, 1, 0, 0, 512, "scalar")
+        cast_w2(0, 0, 256, "vector")
         quant_w1(0, 0, 1)
-        cast_w1(0, 1, 0, 0, 256, "scalar")
-        cast_w1(0, 1, 1, 0, 256, "scalar")
-        cast_w1(0, 1, 0, 256, 512, "scalar")
-        cast_w1(0, 1, 1, 256, 512, "vector")
         quant_w1(0, 1, 0)
         quant_w1(0, 1, 1)
-        gather_words(0, 1)
-        gather_words(1, 1)
-        gather_words(2, 1)
-        gather_words(3, 1)
-        cast_w2(0, 0, 256, "scalar")
+        quant_w1(1, 1, 0)
+        quant_w2(0, 0, 256)
+        gather_scales(2)
         mm1(0, 0)
         mm1(0, 128)
-        relu(0, 0, "vector")
-        quant_w2(0, 0, 256)
-        cast_w2(0, 256, 384, "vector")
         relu(0, 128, "scalar")
-        cast_w1(1, 0, 1, 0, 512, "vector")
-        square(0, 0)
+        cast_w1(1, 0, 0, 0, 512, "vector")
+        cast_w2(0, 256, 384, "scalar")
+        relu(0, 0, "scalar")
         square(0, 128)
-        quant_w2(0, 256, 384)
-        quant_w1(1, 0, 1)
         quant_h(0, 128)
-        cast_w1(1, 1, 0, 0, 512, "vector")
-        quant_h(0, 0)
-        cast_w1(1, 0, 0, 0, 512, "scalar")
-        mm2(0, 1, 0, 128)
-        mm2(0, 1, 128, 256)
+        cast_w1(1, 0, 1, 0, 512, "scalar")
         quant_w1(1, 0, 0)
-        evac(0, 1, 0, 128, False)
-        mm2(0, 2, 128, 256)
-        quant_w1(1, 1, 0)
-        evac(0, 2, 128, 256, False)
-        scatter(0, 1, 0, 128, False)
-        cast_w1(1, 1, 1, 0, 512, "scalar")
-        mm2(0, 0, 128, 256)
-        mm2(0, 2, 0, 128)
         quant_w1(1, 1, 1)
-        evac(0, 1, 128, 256, False)
-        mm1(1, 0)
-        evac(0, 0, 128, 256, False)
-        cast_w1(2, 0, 1, 0, 512, "scalar")
+        quant_w1(1, 0, 1)
+        mm2(0, 1, 128, 256)
+        square(0, 0)
+        evac(0, 1, 128, 256, True)
+        gather_scales(1)
+        quant_w2(0, 256, 384)
+        gather_words(3, 0)
         mm1(1, 128)
-        scatter(0, 0, 128, 256, False)
-        scatter(0, 2, 128, 256, False)
-        quant_w1(2, 0, 1)
-        relu(1, 128, "vector")
-        cast_w1(2, 0, 0, 0, 512, "scalar")
-        relu(1, 0, "scalar")
-        cast_w2(1, 256, 384, "vector")
-        quant_w1(2, 0, 0)
-        evac(0, 2, 0, 128, False)
+        mm2(0, 0, 128, 256)
+        mm1(1, 0)
+        quant_h(0, 0)
+        mm2(0, 2, 0, 128)
+        evac(0, 0, 128, 256, True)
         cast_w2(1, 0, 256, "scalar")
+        mm2(0, 2, 128, 256)
+        relu(1, 128, "scalar")
+        cast_w2(1, 256, 384, "vector")
         mm2(0, 0, 0, 128)
-        quant_w2(1, 0, 256)
+        relu(1, 0, "scalar")
+        evac(0, 2, 0, 128, True)
+        evac(0, 0, 0, 128, True)
+        evac(0, 2, 128, 256, True)
         square(1, 128)
         square(1, 0)
-        cast_w1(2, 1, 1, 0, 512, "vector")
-        quant_w2(1, 256, 384)
-        quant_h(1, 128)
+        cast_w1(2, 0, 0, 0, 512, "scalar")
+        scatter(0, 0, 128, 256, True)
+        mm2(0, 1, 0, 128)
+        quant_w2(1, 0, 256)
+        scatter(0, 2, 0, 128, True)
+        cast_w1(2, 0, 1, 0, 512, "scalar")
+        scatter(0, 1, 128, 256, True)
+        scatter(0, 0, 0, 128, True)
+        gather_scales(3)
+        evac(0, 1, 0, 128, True)
         quant_h(1, 0)
+        quant_h(1, 128)
+        cast_w1(2, 1, 1, 0, 512, "scalar")
+        quant_w2(1, 256, 384)
+        quant_w1(2, 0, 0)
+        cast_w1(2, 1, 0, 0, 512, "vector")
         mm2(1, 2, 0, 256)
-        evac(0, 0, 0, 128, False)
-        quant_w1(2, 1, 1)
-        cast_w1(2, 1, 0, 0, 512, "scalar")
-        evac(1, 2, 0, 256, False)
-        quant_w1(2, 1, 0)
-        cast_w2(2, 0, 256, "scalar")
-        quant_w2(2, 0, 256)
+        scatter(0, 2, 128, 256, True)
         mm2(1, 0, 0, 256)
+        quant_w1(2, 0, 1)
+        quant_w1(2, 1, 0)
+        evac(1, 0, 0, 256, True)
+        cast_w2(2, 0, 256, "scalar")
+        cast_w2(2, 256, 384, "vector")
+        quant_w1(2, 1, 1)
+        evac(1, 2, 0, 256, True)
         mm1(2, 0)
-        cast_w2(2, 256, 384, "scalar")
-        evac(1, 0, 0, 256, False)
-        cast_w1(3, 1, 0, 0, 512, "vector")
-        relu(2, 0, "scalar")
+        cast_w1(3, 1, 1, 0, 512, "vector")
         mm1(2, 128)
-        quant_w2(2, 256, 384)
-        mm2(1, 1, 0, 256)
+        relu(2, 0, "scalar")
         relu(2, 128, "scalar")
-        square(2, 0)
+        cast_w1(3, 1, 0, 0, 512, "vector")
         square(2, 128)
-        quant_h(2, 0)
-        evac(1, 1, 0, 256, False)
-        cast_w1(3, 0, 1, 0, 512, "scalar")
-        scatter(0, 0, 0, 128, False)
-        quant_w1(3, 1, 0)
-        quant_w1(3, 0, 1)
+        quant_w1(3, 1, 1)
+        quant_w2(2, 0, 256)
+        square(2, 0)
         cast_w1(3, 0, 0, 0, 512, "scalar")
+        quant_w1(3, 1, 0)
+        mm2(1, 1, 0, 256)
+        quant_w2(2, 256, 384)
+        quant_h(2, 0)
+        cast_w1(3, 0, 1, 0, 512, "scalar")
+        scatter(0, 1, 0, 128, True)
+        evac(1, 1, 0, 256, True)
+        scatter(1, 2, 0, 256, True)
         quant_w1(3, 0, 0)
         quant_h(2, 128)
-        mm2(2, 2, 0, 256)
+        scatter(1, 1, 0, 256, True)
         mm2(2, 0, 0, 256)
-        evac(2, 0, 0, 256, False)
-        cast_w1(3, 1, 1, 0, 512, "scalar")
         mm2(2, 1, 0, 256)
-        evac(2, 1, 0, 256, False)
-        scatter(0, 1, 128, 256, False)
-        scatter(1, 0, 0, 256, False)
-        scatter(0, 2, 0, 128, False)
-        quant_w1(3, 1, 1)
-        evac(2, 2, 0, 256, False)
+        evac(2, 1, 0, 256, True)
+        quant_w1(3, 0, 1)
         mm1(3, 0)
-        mm1(3, 128)
+        mm2(2, 2, 0, 256)
         cast_w2(3, 0, 256, "scalar")
-        quant_w2(3, 0, 256)
-        scatter(1, 2, 0, 256, False)
-        relu(3, 0, "scalar")
-        relu(3, 128, "scalar")
-        square(3, 0)
         cast_w2(3, 256, 384, "scalar")
-        scatter(1, 1, 0, 256, False)
+        mm1(3, 128)
+        evac(2, 2, 0, 256, True)
+        relu(3, 0, "scalar")
+        evac(2, 0, 0, 256, True)
+        relu(3, 128, "scalar")
+        scatter(1, 0, 0, 256, True)
+        square(3, 0)
         quant_h(3, 0)
-        mm2(3, 0, 0, 128)
-        scatter(2, 2, 0, 256, False)
-        scatter(2, 1, 0, 256, False)
-        quant_w2(3, 256, 384)
+        scatter(2, 1, 0, 256, True)
         square(3, 128)
+        scatter(2, 0, 0, 256, True)
         quant_h(3, 128)
-        evac(3, 0, 0, 128, False)
-        mm2(3, 2, 0, 128)
-        mm2(3, 1, 0, 128)
-        evac(3, 2, 0, 128, False)
+        quant_w2(3, 0, 256)
+        quant_w2(3, 256, 384)
+        mm2(3, 0, 0, 128)
+        evac(3, 0, 0, 128, True)
         mm2(3, 0, 128, 256)
-        scatter(2, 0, 0, 256, False)
-        mm2(3, 2, 128, 256)
+        scatter(2, 2, 0, 256, True)
         mm2(3, 1, 128, 256)
-        evac(3, 0, 128, 256, False)
-        scatter(3, 2, 0, 128, False)
-        evac(3, 2, 128, 256, False)
-        scatter(3, 0, 0, 128, False)
-        scatter(3, 0, 128, 256, False)
-        scatter(3, 2, 128, 256, False)
-        evac(3, 1, 128, 256, False)
+        scatter(3, 0, 0, 128, True)
+        evac(3, 0, 128, 256, True)
+        mm2(3, 1, 0, 128)
+        mm2(3, 2, 0, 128)
+        evac(3, 1, 0, 128, True)
+        evac(3, 1, 128, 256, True)
+        scatter(3, 0, 128, 256, True)
         store(0)
-        evac(3, 1, 0, 128, False)
-        scatter(3, 1, 0, 128, False)
-        store(2)
-        scatter(3, 1, 128, 256, False)
+        scatter(3, 1, 128, 256, True)
+        mm2(3, 2, 128, 256)
+        evac(3, 2, 128, 256, True)
+        evac(3, 2, 0, 128, True)
+        scatter(3, 1, 0, 128, True)
+        scatter(3, 2, 0, 128, True)
         store(1)
+        scatter(3, 2, 128, 256, True)
+        store(2)

@@ -22,8 +22,9 @@ PASSES = K // K_PASS
 HALF = 128
 NB = N // P
 GROUP = 16
-STREAM_BUFS = 32
-HEAD_BUFS = 16
+STREAM_BUFS = 30
+HEAD_BUFS = 23
+SIDE_BUFS = 2
 
 
 def tile_moe_pkd_mlp_relu2_kernel(tc, x_words, x_scales, w1, w2, gate, offs, out):
@@ -41,6 +42,9 @@ def tile_moe_pkd_mlp_relu2_kernel(tc, x_words, x_scales, w1, w2, gate, offs, out
 
         def head(shape, dtype):
             return ring.tile(shape, dtype, name="head", align_bytes=64, bufs=HEAD_BUFS)
+
+        def side(shape, dtype):
+            return ring.tile(shape, dtype, name="side", align_bytes=64, bufs=SIDE_BUFS)
 
         def slots(s0, s1):
             return offsets[:, s0 // GROUP : s1 // GROUP]
@@ -102,7 +106,7 @@ def tile_moe_pkd_mlp_relu2_kernel(tc, x_words, x_scales, w1, w2, gate, offs, out
 
         def cast_w1(e, g, u, c0, c1, engine):
             if (e, g, u) not in w1b:
-                w1b[e, g, u] = stream([P, 2 * P * PACK], BF16)
+                w1b[e, g, u] = (side if engine == "gpsimd" else stream)([P, 2 * P * PACK], BF16)
             dst = w1b[e, g, u][:].rearrange("p (t m j) -> p m j t", t=2, j=PACK)
             for r0, r1, raw in raw1[e, g]:
                 if r0 <= c0 and c1 <= r1:
@@ -115,7 +119,7 @@ def tile_moe_pkd_mlp_relu2_kernel(tc, x_words, x_scales, w1, w2, gate, offs, out
 
         def quant_w1(e, g, u):
             w1c[e, g, u] = keep.tile([P, 2 * P], U32, name="w1c%d_%d_%d" % (e, g, u), align_bytes=64)
-            w1s[e, g, u] = (head if e == 0 else stream)([P, 2 * P], U8)
+            w1s[e, g, u] = (head if e <= 1 else stream)([P, 2 * P], U8)
             nc.vector.quantize_mx(out=w1c[e, g, u][:].bitcast(FP8X4), scales=w1s[e, g, u][:], in_=w1b[e, g, u][:])
 
         w2b = {}
@@ -123,7 +127,7 @@ def tile_moe_pkd_mlp_relu2_kernel(tc, x_words, x_scales, w1, w2, gate, offs, out
         w2s = {}
 
         def cast_w2(e, c0, c1, engine):
-            w2b[e, c0] = stream([P, (c1 - c0) * PACK], BF16)
+            w2b[e, c0] = (side if engine == "gpsimd" else stream)([P, (c1 - c0) * PACK], BF16)
             cast(
                 engine,
                 w2b[e, c0][:].rearrange("p (c i j) -> p c j i", i=4, j=PACK),
@@ -132,7 +136,7 @@ def tile_moe_pkd_mlp_relu2_kernel(tc, x_words, x_scales, w1, w2, gate, offs, out
 
         def quant_w2(e, c0, c1):
             codes = keep.tile([P, c1 - c0], U32, name="w2c%d_%d" % (e, c0), align_bytes=64)
-            scales = stream([P, c1 - c0], U8)
+            scales = (head if e == 0 else stream)([P, c1 - c0], U8)
             nc.vector.quantize_mx(out=codes[:].bitcast(FP8X4), scales=scales[:], in_=w2b[e, c0][:])
             for b in range(c0 // P, c1 // P):
                 w2c[e, b] = codes[:, b * P - c0 : (b + 1) * P - c0]
@@ -179,7 +183,7 @@ def tile_moe_pkd_mlp_relu2_kernel(tc, x_words, x_scales, w1, w2, gate, offs, out
             s1 = s0 + HALF
             if e not in hc:
                 hc[e] = keep.tile([P, C], U32, name="hc%d" % e, align_bytes=64)
-                hs[e] = stream([P, C], U8)
+                hs[e] = (head if e == 0 else stream)([P, C], U8)
             nc.vector.quantize_mx(
                 out=hc[e][:, s0:s1].bitcast(FP8X4), scales=hs[e][:, s0:s1], in_=hb[e, s0][:]
             )
@@ -225,178 +229,189 @@ def tile_moe_pkd_mlp_relu2_kernel(tc, x_words, x_scales, w1, w2, gate, offs, out
             nc.sync.dma_start(out=out[b * P : (b + 1) * P, :], in_=windows[b][:])
 
         load_x(0)
-        load_x(1)
-        load_w1(0, 0, 0, 512)
-        load_w1(0, 1, 0, 512)
         load_scales()
-        load_w1(1, 1, 0, 512)
+        load_x(1)
+        load_w1(0, 1, 0, 512)
+        load_w1(0, 0, 0, 512)
         load_w2(0)
         load_w1(1, 0, 0, 512)
+        load_w1(1, 1, 0, 512)
         load_w2(1)
-        load_gate(0, 1)
         load_gate(0, 0)
-        load_gate(1, 2)
         load_gate(0, 2)
         load_w1(2, 0, 0, 512)
+        load_gate(0, 1)
+        load_w2(2)
         load_w1(2, 1, 0, 512)
         load_gate(1, 0)
-        load_w2(2)
+        load_gate(2, 2)
+        load_gate(1, 2)
         load_w1(3, 1, 0, 512)
-        load_w1(3, 0, 0, 512)
         load_gate(1, 1)
+        load_w1(3, 0, 0, 512)
+        load_gate(3, 2)
         load_w2(3)
         load_gate(2, 0)
         load_gate(2, 1)
-        load_gate(3, 2)
         load_gate(3, 1)
         load_gate(3, 0)
-        load_gate(2, 2)
-        cast_w1(0, 0, 0, 0, 512, "vector")
-        gather_words(0, 0)
         gather_words(1, 0)
-        gather_words(3, 1)
-        cast_w1(0, 0, 1, 0, 512, "scalar")
-        cast_w1(0, 1, 0, 0, 512, "vector")
-        gather_words(2, 0)
+        gather_scales(1)
+        cast_w1(0, 0, 1, 0, 512, "vector")
+        gather_words(0, 0)
         gather_words(2, 1)
-        gather_words(1, 1)
-        gather_words(0, 1)
-        quant_w1(0, 0, 0)
+        gather_words(3, 0)
+        cast_w1(0, 1, 0, 0, 512, "gpsimd")
         gather_scales(0)
         cast_w1(0, 1, 1, 0, 512, "scalar")
-        cast_w1(1, 1, 1, 0, 512, "vector")
-        cast_w1(1, 1, 0, 0, 512, "scalar")
-        cast_w2(0, 0, 256, "vector")
-        quant_w1(0, 0, 1)
+        gather_words(2, 0)
+        gather_words(0, 1)
+        gather_words(1, 1)
+        cast_w1(1, 0, 1, 0, 512, "gpsimd")
         quant_w1(0, 1, 0)
         quant_w1(0, 1, 1)
-        quant_w1(1, 1, 0)
-        quant_w2(0, 0, 256)
-        gather_scales(2)
-        mm1(0, 0)
-        mm1(0, 128)
-        relu(0, 128, "scalar")
-        cast_w1(1, 0, 0, 0, 512, "vector")
-        cast_w2(0, 256, 384, "scalar")
-        relu(0, 0, "scalar")
-        square(0, 128)
-        quant_h(0, 128)
-        cast_w1(1, 0, 1, 0, 512, "scalar")
-        quant_w1(1, 0, 0)
-        quant_w1(1, 1, 1)
-        quant_w1(1, 0, 1)
-        mm2(0, 1, 128, 256)
-        square(0, 0)
-        evac(0, 1, 128, 256, True)
-        gather_scales(1)
-        quant_w2(0, 256, 384)
-        gather_words(3, 0)
-        mm1(1, 128)
-        mm2(0, 0, 128, 256)
-        mm1(1, 0)
-        quant_h(0, 0)
-        mm2(0, 2, 0, 128)
-        evac(0, 0, 128, 256, True)
-        cast_w2(1, 0, 256, "scalar")
-        mm2(0, 2, 128, 256)
-        relu(1, 128, "scalar")
-        cast_w2(1, 256, 384, "vector")
-        mm2(0, 0, 0, 128)
-        relu(1, 0, "scalar")
-        evac(0, 2, 0, 128, True)
-        evac(0, 0, 0, 128, True)
-        evac(0, 2, 128, 256, True)
-        square(1, 128)
-        square(1, 0)
-        cast_w1(2, 0, 0, 0, 512, "scalar")
-        scatter(0, 0, 128, 256, True)
-        mm2(0, 1, 0, 128)
-        quant_w2(1, 0, 256)
-        scatter(0, 2, 0, 128, True)
-        cast_w1(2, 0, 1, 0, 512, "scalar")
-        scatter(0, 1, 128, 256, True)
-        scatter(0, 0, 0, 128, True)
+        cast_w1(0, 0, 0, 0, 512, "scalar")
+        quant_w1(0, 0, 1)
+        quant_w1(0, 0, 0)
+        gather_words(3, 1)
         gather_scales(3)
-        evac(0, 1, 0, 128, True)
-        quant_h(1, 0)
-        quant_h(1, 128)
-        cast_w1(2, 1, 1, 0, 512, "scalar")
-        quant_w2(1, 256, 384)
-        quant_w1(2, 0, 0)
-        cast_w1(2, 1, 0, 0, 512, "vector")
-        mm2(1, 2, 0, 256)
-        scatter(0, 2, 128, 256, True)
-        mm2(1, 0, 0, 256)
+        mm1(0, 128)
+        mm1(0, 0)
+        cast_w2(0, 0, 256, "scalar")
+        cast_w2(0, 256, 384, "scalar")
+        cast_w1(1, 0, 0, 0, 512, "scalar")
+        quant_w2(0, 0, 256)
+        quant_w1(1, 0, 0)
+        relu(0, 128, "vector")
+        relu(0, 0, "vector")
+        cast_w1(1, 1, 1, 0, 512, "vector")
+        quant_w2(0, 256, 384)
+        cast_w1(2, 0, 1, 0, 512, "gpsimd")
+        square(0, 0)
+        quant_h(0, 0)
+        mm2(0, 0, 0, 128)
+        quant_w1(1, 0, 1)
+        square(0, 128)
+        cast_w1(1, 1, 0, 0, 512, "scalar")
+        quant_h(0, 128)
+        mm2(0, 2, 0, 256)
+        quant_w1(1, 1, 1)
+        cast_w1(2, 1, 1, 0, 512, "gpsimd")
+        quant_w1(1, 1, 0)
+        cast_w2(1, 0, 256, "scalar")
+        mm2(0, 1, 0, 256)
+        evac(0, 0, 0, 128, True)
+        cast_w1(3, 1, 1, 0, 512, "gpsimd")
+        mm2(0, 0, 128, 256)
+        mm1(1, 128)
+        mm1(1, 0)
+        cast_w2(1, 256, 384, "scalar")
+        evac(0, 0, 128, 256, True)
+        evac(0, 2, 0, 256, True)
+        relu(1, 128, "scalar")
+        evac(0, 1, 0, 256, False)
+        square(1, 128)
+        relu(1, 0, "scalar")
+        quant_w2(1, 0, 256)
+        cast_w1(2, 0, 0, 0, 512, "scalar")
         quant_w1(2, 0, 1)
-        quant_w1(2, 1, 0)
-        evac(1, 0, 0, 256, True)
+        square(1, 0)
+        quant_w1(2, 0, 0)
+        quant_h(1, 128)
+        quant_w2(1, 256, 384)
+        gating(0, 1, 0, 256)
+        cast_w1(2, 1, 0, 0, 512, "scalar")
+        quant_h(1, 0)
+        mm2(1, 2, 0, 256)
+        mm2(1, 0, 0, 128)
+        mm2(1, 1, 0, 256)
+        cast_w2(2, 256, 384, "scalar")
+        evac(1, 0, 0, 128, False)
+        mm2(1, 0, 128, 256)
+        evac(1, 1, 0, 256, False)
         cast_w2(2, 0, 256, "scalar")
-        cast_w2(2, 256, 384, "vector")
-        quant_w1(2, 1, 1)
         evac(1, 2, 0, 256, True)
+        evac(1, 0, 128, 256, True)
+        gather_scales(2)
+        quant_w1(2, 1, 0)
+        gating(1, 0, 0, 128)
+        quant_w1(2, 1, 1)
         mm1(2, 0)
-        cast_w1(3, 1, 1, 0, 512, "vector")
+        scatter(0, 1, 0, 256, True)
+        cast_w1(3, 0, 1, 0, 512, "gpsimd")
         mm1(2, 128)
+        gating(1, 1, 0, 256)
+        quant_w1(3, 1, 1)
+        scatter(0, 0, 0, 128, True)
         relu(2, 0, "scalar")
         relu(2, 128, "scalar")
-        cast_w1(3, 1, 0, 0, 512, "vector")
-        square(2, 128)
-        quant_w1(3, 1, 1)
-        quant_w2(2, 0, 256)
         square(2, 0)
-        cast_w1(3, 0, 0, 0, 512, "scalar")
-        quant_w1(3, 1, 0)
-        mm2(1, 1, 0, 256)
-        quant_w2(2, 256, 384)
+        quant_w2(2, 0, 256)
+        square(2, 128)
         quant_h(2, 0)
-        cast_w1(3, 0, 1, 0, 512, "scalar")
-        scatter(0, 1, 0, 128, True)
-        evac(1, 1, 0, 256, True)
-        scatter(1, 2, 0, 256, True)
-        quant_w1(3, 0, 0)
+        mm2(2, 0, 0, 128)
+        scatter(0, 0, 128, 256, True)
         quant_h(2, 128)
-        scatter(1, 1, 0, 256, True)
-        mm2(2, 0, 0, 256)
-        mm2(2, 1, 0, 256)
-        evac(2, 1, 0, 256, True)
+        mm2(2, 0, 128, 256)
+        cast_w1(3, 0, 0, 0, 512, "scalar")
         quant_w1(3, 0, 1)
-        mm1(3, 0)
+        quant_w1(3, 0, 0)
+        quant_w2(2, 256, 384)
+        mm2(2, 1, 0, 256)
         mm2(2, 2, 0, 256)
+        cast_w1(3, 1, 0, 0, 512, "scalar")
+        scatter(1, 1, 0, 256, True)
         cast_w2(3, 0, 256, "scalar")
+        evac(2, 0, 0, 128, True)
+        scatter(0, 2, 0, 256, True)
+        quant_w1(3, 1, 0)
+        evac(2, 2, 0, 256, False)
+        mm1(3, 0)
+        scatter(1, 0, 128, 256, True)
         cast_w2(3, 256, 384, "scalar")
-        mm1(3, 128)
-        evac(2, 2, 0, 256, True)
-        relu(3, 0, "scalar")
-        evac(2, 0, 0, 256, True)
-        relu(3, 128, "scalar")
-        scatter(1, 0, 0, 256, True)
-        square(3, 0)
-        quant_h(3, 0)
-        scatter(2, 1, 0, 256, True)
-        square(3, 128)
-        scatter(2, 0, 0, 256, True)
-        quant_h(3, 128)
+        evac(2, 0, 128, 256, True)
         quant_w2(3, 0, 256)
+        relu(3, 0, "scalar")
+        evac(2, 1, 0, 256, False)
+        mm1(3, 128)
+        gating(2, 2, 0, 256)
+        scatter(1, 0, 0, 128, True)
+        square(3, 0)
         quant_w2(3, 256, 384)
-        mm2(3, 0, 0, 128)
-        evac(3, 0, 0, 128, True)
-        mm2(3, 0, 128, 256)
-        scatter(2, 2, 0, 256, True)
-        mm2(3, 1, 128, 256)
-        scatter(3, 0, 0, 128, True)
-        evac(3, 0, 128, 256, True)
+        quant_h(3, 0)
+        relu(3, 128, "scalar")
         mm2(3, 1, 0, 128)
+        mm2(3, 0, 0, 128)
+        gating(2, 1, 0, 256)
+        scatter(1, 2, 0, 256, True)
+        evac(3, 1, 0, 128, False)
+        square(3, 128)
+        quant_h(3, 128)
         mm2(3, 2, 0, 128)
-        evac(3, 1, 0, 128, True)
-        evac(3, 1, 128, 256, True)
-        scatter(3, 0, 128, 256, True)
-        store(0)
-        scatter(3, 1, 128, 256, True)
+        evac(3, 0, 0, 128, False)
+        scatter(2, 0, 0, 128, True)
+        mm2(3, 1, 128, 256)
+        evac(3, 1, 128, 256, False)
         mm2(3, 2, 128, 256)
-        evac(3, 2, 128, 256, True)
-        evac(3, 2, 0, 128, True)
+        gating(3, 1, 0, 128)
+        gating(3, 0, 0, 128)
+        mm2(3, 0, 128, 256)
+        gating(3, 1, 128, 256)
+        evac(3, 2, 128, 256, False)
+        evac(3, 2, 0, 128, False)
+        scatter(2, 0, 128, 256, True)
+        scatter(2, 1, 0, 256, True)
+        scatter(3, 0, 0, 128, True)
+        evac(3, 0, 128, 256, False)
         scatter(3, 1, 0, 128, True)
-        scatter(3, 2, 0, 128, True)
+        scatter(3, 1, 128, 256, True)
+        gating(3, 2, 128, 256)
+        gating(3, 0, 128, 256)
+        scatter(3, 0, 128, 256, True)
+        gating(3, 2, 0, 128)
+        scatter(2, 2, 0, 256, True)
         store(1)
+        scatter(3, 2, 0, 128, True)
+        store(0)
         scatter(3, 2, 128, 256, True)
         store(2)

@@ -23,8 +23,10 @@ HALF = 128
 NB = N // P
 GROUP = 16
 STREAM_BUFS = 30
-HEAD_BUFS = 23
+HEAD_BUFS = 18
+RAW_BUFS = 6
 SIDE_BUFS = 2
+WHOLE = (1, 2)
 
 
 def tile_moe_pkd_mlp_relu2_kernel(tc, x_words, x_scales, w1, w2, gate, offs, out):
@@ -69,7 +71,7 @@ def tile_moe_pkd_mlp_relu2_kernel(tc, x_words, x_scales, w1, w2, gate, offs, out
 
         def load_w1(e, g, c0, c1):
             rows = w1[e, g * K_PASS : (g + 1) * K_PASS, :].rearrange("(p j) c -> p j c", j=PACK)
-            t = keep.tile([P, PACK, c1 - c0], F32, name="raw1_%d_%d_%d" % (e, g, c0))
+            t = ring.tile([P, PACK, c1 - c0], F32, name="raw1", bufs=RAW_BUFS)
             nc.sync.dma_start(out=t[:], in_=rows[:, :, c0:c1])
             raw1.setdefault((e, g), []).append((c0, c1, t))
 
@@ -84,13 +86,17 @@ def tile_moe_pkd_mlp_relu2_kernel(tc, x_words, x_scales, w1, w2, gate, offs, out
         xw = {}
         xs = {}
 
-        def gather_scales(e):
-            xs[e] = head([P, C], U8)
-            nc.vector.tensor_copy(xs[e][:], xs_win[:].indirect(slots(e * C, (e + 1) * C)))
+        def gather_scales(e, e1):
+            tile = head([P, (e1 - e) * C], U8)
+            nc.vector.tensor_copy(tile[:], xs_win[:].indirect(slots(e * C, e1 * C)))
+            for n in range(e, e1):
+                xs[n] = tile[:, (n - e) * C : (n - e + 1) * C]
 
-        def gather_words(e, g):
-            xw[e, g] = head([P, C], U32)
-            nc.vector.tensor_copy(xw[e, g][:], xw_win[g][:].bitcast(U32).indirect(slots(e * C, (e + 1) * C)))
+        def gather_words(e, e1, g):
+            tile = head([P, (e1 - e) * C], U32)
+            nc.vector.tensor_copy(tile[:], xw_win[g][:].bitcast(U32).indirect(slots(e * C, e1 * C)))
+            for n in range(e, e1):
+                xw[n, g] = tile[:, (n - e) * C : (n - e + 1) * C]
 
         def cast(engine, dst, src):
             if engine == "vector":
@@ -107,15 +113,14 @@ def tile_moe_pkd_mlp_relu2_kernel(tc, x_words, x_scales, w1, w2, gate, offs, out
         def cast_w1(e, g, u, c0, c1, engine):
             if (e, g, u) not in w1b:
                 w1b[e, g, u] = (side if engine == "gpsimd" else stream)([P, 2 * P * PACK], BF16)
-            dst = w1b[e, g, u][:].rearrange("p (t m j) -> p m j t", t=2, j=PACK)
-            for r0, r1, raw in raw1[e, g]:
-                if r0 <= c0 and c1 <= r1:
-                    src = raw[:].rearrange("p j (m t) -> p m j t", t=PACK)
-                    cast(
-                        engine,
-                        dst[:, c0 // PACK : c1 // PACK],
-                        src[:, (c0 - r0) // PACK : (c1 - r0) // PACK, :, 2 * u : 2 * u + 2],
-                    )
+            raw = raw1[e, g][0][2]
+            if engine == "gpsimd":
+                dst = w1b[e, g, u][:].rearrange("p (t m j) -> p m t j", t=2, j=PACK)
+                src = raw[:].rearrange("p j (m t) -> p m t j", t=PACK)[:, :, 2 * u : 2 * u + 2, :]
+            else:
+                dst = w1b[e, g, u][:].rearrange("p (t m j) -> p m j t", t=2, j=PACK)
+                src = raw[:].rearrange("p j (m t) -> p m j t", t=PACK)[:, :, :, 2 * u : 2 * u + 2]
+            cast(engine, dst, src)
 
         def quant_w1(e, g, u):
             w1c[e, g, u] = keep.tile([P, 2 * P], U32, name="w1c%d_%d_%d" % (e, g, u), align_bytes=64)
@@ -128,11 +133,13 @@ def tile_moe_pkd_mlp_relu2_kernel(tc, x_words, x_scales, w1, w2, gate, offs, out
 
         def cast_w2(e, c0, c1, engine):
             w2b[e, c0] = (side if engine == "gpsimd" else stream)([P, (c1 - c0) * PACK], BF16)
-            cast(
-                engine,
-                w2b[e, c0][:].rearrange("p (c i j) -> p c j i", i=4, j=PACK),
-                raw2[e][:, :, c0:c1].rearrange("p j (c i) -> p c j i", i=4),
-            )
+            if engine == "gpsimd":
+                dst = w2b[e, c0][:].rearrange("p (c j) -> p c j", j=PACK)
+                src = raw2[e][:, :, c0:c1].rearrange("p j c -> p c j")
+            else:
+                dst = w2b[e, c0][:].rearrange("p (c i j) -> p c j i", i=4, j=PACK)
+                src = raw2[e][:, :, c0:c1].rearrange("p j (c i) -> p c j i", i=4)
+            cast(engine, dst, src)
 
         def quant_w2(e, c0, c1):
             codes = keep.tile([P, c1 - c0], U32, name="w2c%d_%d" % (e, c0), align_bytes=64)
@@ -172,20 +179,24 @@ def tile_moe_pkd_mlp_relu2_kernel(tc, x_words, x_scales, w1, w2, gate, offs, out
                 nc.scalar.activation(out=relus[e, s0][:], in_=src, func=ACT.Relu)
 
         def square(e, s0):
-            hb[e, s0] = stream([P, HALF * PACK], BF16)
+            if e in WHOLE:
+                if e not in hb:
+                    hb[e] = stream([P, C * PACK], BF16)
+                hb[e, s0] = hb[e][:, s0 * PACK : (s0 + HALF) * PACK]
+            else:
+                hb[e, s0] = stream([P, HALF * PACK], BF16)[:]
             nc.scalar.activation(
-                out=hb[e, s0][:],
+                out=hb[e, s0],
                 in_=relus[e, s0][:].rearrange("p s t -> p (s t)"),
                 func=ACT.Square,
             )
 
-        def quant_h(e, s0):
-            s1 = s0 + HALF
+        def quant_h(e, s0, s1):
             if e not in hc:
                 hc[e] = keep.tile([P, C], U32, name="hc%d" % e, align_bytes=64)
                 hs[e] = (head if e == 0 else stream)([P, C], U8)
             nc.vector.quantize_mx(
-                out=hc[e][:, s0:s1].bitcast(FP8X4), scales=hs[e][:, s0:s1], in_=hb[e, s0][:]
+                out=hc[e][:, s0:s1].bitcast(FP8X4), scales=hs[e][:, s0:s1], in_=hb[e][:] if e in WHOLE else hb[e, s0]
             )
 
         acc2 = {}
@@ -229,189 +240,168 @@ def tile_moe_pkd_mlp_relu2_kernel(tc, x_words, x_scales, w1, w2, gate, offs, out
             nc.sync.dma_start(out=out[b * P : (b + 1) * P, :], in_=windows[b][:])
 
         load_x(0)
-        load_scales()
         load_x(1)
-        load_w1(0, 1, 0, 512)
         load_w1(0, 0, 0, 512)
-        load_w2(0)
-        load_w1(1, 0, 0, 512)
+        load_scales()
+        load_w1(0, 1, 0, 512)
         load_w1(1, 1, 0, 512)
-        load_w2(1)
-        load_gate(0, 0)
-        load_gate(0, 2)
-        load_w1(2, 0, 0, 512)
-        load_gate(0, 1)
-        load_w2(2)
+        load_w1(1, 0, 0, 512)
+        load_w2(0)
         load_w1(2, 1, 0, 512)
+        load_gate(0, 0)
+        load_gate(0, 1)
+        load_gate(0, 2)
+        load_w2(1)
+        load_w1(2, 0, 0, 512)
         load_gate(1, 0)
-        load_gate(2, 2)
         load_gate(1, 2)
-        load_w1(3, 1, 0, 512)
         load_gate(1, 1)
         load_w1(3, 0, 0, 512)
+        load_w1(3, 1, 0, 512)
+        load_w2(2)
         load_gate(3, 2)
-        load_w2(3)
-        load_gate(2, 0)
-        load_gate(2, 1)
         load_gate(3, 1)
+        load_gate(2, 0)
+        load_gate(2, 2)
         load_gate(3, 0)
-        gather_words(1, 0)
-        gather_scales(1)
-        cast_w1(0, 0, 1, 0, 512, "vector")
-        gather_words(0, 0)
-        gather_words(2, 1)
-        gather_words(3, 0)
-        cast_w1(0, 1, 0, 0, 512, "gpsimd")
-        gather_scales(0)
-        cast_w1(0, 1, 1, 0, 512, "scalar")
-        gather_words(2, 0)
-        gather_words(0, 1)
-        gather_words(1, 1)
-        cast_w1(1, 0, 1, 0, 512, "gpsimd")
-        quant_w1(0, 1, 0)
-        quant_w1(0, 1, 1)
-        cast_w1(0, 0, 0, 0, 512, "scalar")
-        quant_w1(0, 0, 1)
+        load_gate(2, 1)
+        load_w2(3)
+        gather_words(2, 4, 0)
+        cast_w1(0, 0, 1, 0, 512, "scalar")
+        cast_w1(0, 0, 0, 0, 512, "gpsimd")
+        gather_words(3, 4, 1)
+        gather_words(1, 3, 1)
+        gather_words(0, 2, 0)
+        cast_w1(0, 1, 1, 0, 512, "vector")
+        gather_scales(0, 1)
+        cast_w1(1, 1, 1, 0, 512, "gpsimd")
+        gather_words(0, 1, 1)
+        cast_w1(0, 1, 0, 0, 512, "scalar")
         quant_w1(0, 0, 0)
-        gather_words(3, 1)
-        gather_scales(3)
-        mm1(0, 128)
-        mm1(0, 0)
-        cast_w2(0, 0, 256, "scalar")
-        cast_w2(0, 256, 384, "scalar")
-        cast_w1(1, 0, 0, 0, 512, "scalar")
-        quant_w2(0, 0, 256)
-        quant_w1(1, 0, 0)
-        relu(0, 128, "vector")
-        relu(0, 0, "vector")
-        cast_w1(1, 1, 1, 0, 512, "vector")
-        quant_w2(0, 256, 384)
-        cast_w1(2, 0, 1, 0, 512, "gpsimd")
-        square(0, 0)
-        quant_h(0, 0)
-        mm2(0, 0, 0, 128)
-        quant_w1(1, 0, 1)
-        square(0, 128)
         cast_w1(1, 1, 0, 0, 512, "scalar")
-        quant_h(0, 128)
-        mm2(0, 2, 0, 256)
-        quant_w1(1, 1, 1)
-        cast_w1(2, 1, 1, 0, 512, "gpsimd")
+        quant_w1(0, 0, 1)
+        quant_w1(0, 1, 0)
+        cast_w1(1, 0, 0, 0, 512, "vector")
+        quant_w1(0, 1, 1)
+        mm1(0, 0)
+        cast_w1(1, 0, 1, 0, 512, "vector")
+        gather_scales(1, 4)
         quant_w1(1, 1, 0)
-        cast_w2(1, 0, 256, "scalar")
-        mm2(0, 1, 0, 256)
-        evac(0, 0, 0, 128, True)
-        cast_w1(3, 1, 1, 0, 512, "gpsimd")
-        mm2(0, 0, 128, 256)
-        mm1(1, 128)
+        quant_w1(1, 0, 0)
+        relu(0, 0, "scalar")
+        mm1(0, 128)
+        quant_w1(1, 1, 1)
+        relu(0, 128, "scalar")
+        cast_w2(0, 256, 384, "vector")
+        square(0, 128)
+        square(0, 0)
+        cast_w2(0, 0, 256, "scalar")
+        quant_h(0, 0, 128)
+        quant_w2(0, 0, 256)
+        mm2(0, 0, 0, 128)
+        quant_h(0, 128, 256)
+        cast_w1(2, 1, 1, 0, 512, "scalar")
+        quant_w2(0, 256, 384)
+        quant_w1(1, 0, 1)
         mm1(1, 0)
-        cast_w2(1, 256, 384, "scalar")
-        evac(0, 0, 128, 256, True)
-        evac(0, 2, 0, 256, True)
-        relu(1, 128, "scalar")
-        evac(0, 1, 0, 256, False)
-        square(1, 128)
-        relu(1, 0, "scalar")
-        quant_w2(1, 0, 256)
-        cast_w1(2, 0, 0, 0, 512, "scalar")
-        quant_w1(2, 0, 1)
-        square(1, 0)
-        quant_w1(2, 0, 0)
-        quant_h(1, 128)
-        quant_w2(1, 256, 384)
-        gating(0, 1, 0, 256)
-        cast_w1(2, 1, 0, 0, 512, "scalar")
-        quant_h(1, 0)
-        mm2(1, 2, 0, 256)
-        mm2(1, 0, 0, 128)
-        mm2(1, 1, 0, 256)
-        cast_w2(2, 256, 384, "scalar")
-        evac(1, 0, 0, 128, False)
-        mm2(1, 0, 128, 256)
-        evac(1, 1, 0, 256, False)
-        cast_w2(2, 0, 256, "scalar")
-        evac(1, 2, 0, 256, True)
-        evac(1, 0, 128, 256, True)
-        gather_scales(2)
-        quant_w1(2, 1, 0)
-        gating(1, 0, 0, 128)
-        quant_w1(2, 1, 1)
-        mm1(2, 0)
-        scatter(0, 1, 0, 256, True)
-        cast_w1(3, 0, 1, 0, 512, "gpsimd")
-        mm1(2, 128)
-        gating(1, 1, 0, 256)
-        quant_w1(3, 1, 1)
+        mm2(0, 1, 0, 256)
+        mm2(0, 2, 0, 256)
+        cast_w1(2, 1, 0, 0, 512, "gpsimd")
+        mm2(0, 0, 128, 256)
+        evac(0, 0, 0, 128, True)
+        evac(0, 1, 0, 256, True)
+        evac(0, 0, 128, 256, False)
+        gating(0, 0, 128, 256)
+        mm1(1, 128)
+        evac(0, 2, 0, 256, False)
         scatter(0, 0, 0, 128, True)
-        relu(2, 0, "scalar")
-        relu(2, 128, "scalar")
-        square(2, 0)
-        quant_w2(2, 0, 256)
-        square(2, 128)
-        quant_h(2, 0)
-        mm2(2, 0, 0, 128)
-        scatter(0, 0, 128, 256, True)
-        quant_h(2, 128)
-        mm2(2, 0, 128, 256)
-        cast_w1(3, 0, 0, 0, 512, "scalar")
-        quant_w1(3, 0, 1)
-        quant_w1(3, 0, 0)
-        quant_w2(2, 256, 384)
-        mm2(2, 1, 0, 256)
-        mm2(2, 2, 0, 256)
-        cast_w1(3, 1, 0, 0, 512, "scalar")
-        scatter(1, 1, 0, 256, True)
-        cast_w2(3, 0, 256, "scalar")
-        evac(2, 0, 0, 128, True)
+        cast_w2(1, 0, 256, "gpsimd")
+        relu(1, 0, "scalar")
+        relu(1, 128, "scalar")
+        gating(0, 2, 0, 256)
+        cast_w2(1, 256, 384, "scalar")
+        quant_w2(1, 256, 384)
+        square(1, 128)
+        square(1, 0)
+        cast_w1(2, 0, 0, 0, 512, "scalar")
+        cast_w1(2, 0, 1, 0, 512, "scalar")
+        quant_h(1, 0, 256)
+        quant_w2(1, 0, 256)
+        mm2(1, 2, 0, 256)
+        mm2(1, 0, 0, 256)
+        quant_w1(2, 0, 0)
+        quant_w1(2, 1, 1)
+        scatter(0, 1, 0, 256, True)
+        quant_w1(2, 1, 0)
+        mm2(1, 1, 0, 256)
+        evac(1, 0, 0, 256, True)
+        evac(1, 2, 0, 256, False)
+        quant_w1(2, 0, 1)
+        mm1(2, 0)
+        cast_w1(3, 0, 0, 0, 512, "gpsimd")
+        mm1(2, 128)
         scatter(0, 2, 0, 256, True)
+        gating(1, 2, 0, 256)
+        evac(1, 1, 0, 256, True)
+        cast_w1(3, 0, 1, 0, 512, "scalar")
+        relu(2, 0, "scalar")
+        scatter(0, 0, 128, 256, True)
+        relu(2, 128, "scalar")
+        square(2, 128)
+        square(2, 0)
+        cast_w2(2, 256, 384, "scalar")
+        cast_w2(2, 0, 256, "scalar")
+        quant_h(2, 0, 256)
+        quant_w1(3, 0, 1)
+        cast_w1(3, 1, 1, 0, 512, "gpsimd")
+        quant_w2(2, 256, 384)
+        mm2(2, 2, 0, 256)
+        quant_w1(3, 0, 0)
+        quant_w2(2, 0, 256)
+        mm2(2, 0, 0, 256)
+        cast_w1(3, 1, 0, 0, 512, "scalar")
+        quant_w1(3, 1, 1)
+        evac(2, 0, 0, 256, False)
+        evac(2, 2, 0, 256, True)
+        mm2(2, 1, 0, 256)
+        scatter(1, 2, 0, 256, True)
+        scatter(1, 0, 0, 256, True)
         quant_w1(3, 1, 0)
-        evac(2, 2, 0, 256, False)
+        cast_w2(3, 256, 384, "gpsimd")
+        gating(2, 0, 0, 256)
         mm1(3, 0)
-        scatter(1, 0, 128, 256, True)
-        cast_w2(3, 256, 384, "scalar")
-        evac(2, 0, 128, 256, True)
+        cast_w2(3, 0, 256, "scalar")
         quant_w2(3, 0, 256)
         relu(3, 0, "scalar")
-        evac(2, 1, 0, 256, False)
-        mm1(3, 128)
-        gating(2, 2, 0, 256)
-        scatter(1, 0, 0, 128, True)
         square(3, 0)
-        quant_w2(3, 256, 384)
-        quant_h(3, 0)
+        mm1(3, 128)
+        quant_h(3, 0, 128)
+        evac(2, 1, 0, 256, False)
         relu(3, 128, "scalar")
-        mm2(3, 1, 0, 128)
+        scatter(1, 1, 0, 256, True)
+        scatter(2, 0, 0, 256, True)
         mm2(3, 0, 0, 128)
-        gating(2, 1, 0, 256)
-        scatter(1, 2, 0, 256, True)
-        evac(3, 1, 0, 128, False)
+        quant_w2(3, 256, 384)
         square(3, 128)
-        quant_h(3, 128)
+        quant_h(3, 128, 256)
         mm2(3, 2, 0, 128)
         evac(3, 0, 0, 128, False)
-        scatter(2, 0, 0, 128, True)
-        mm2(3, 1, 128, 256)
-        evac(3, 1, 128, 256, False)
-        mm2(3, 2, 128, 256)
-        gating(3, 1, 0, 128)
-        gating(3, 0, 0, 128)
-        mm2(3, 0, 128, 256)
-        gating(3, 1, 128, 256)
-        evac(3, 2, 128, 256, False)
-        evac(3, 2, 0, 128, False)
-        scatter(2, 0, 128, 256, True)
-        scatter(2, 1, 0, 256, True)
-        scatter(3, 0, 0, 128, True)
-        evac(3, 0, 128, 256, False)
-        scatter(3, 1, 0, 128, True)
-        scatter(3, 1, 128, 256, True)
-        gating(3, 2, 128, 256)
-        gating(3, 0, 128, 256)
-        scatter(3, 0, 128, 256, True)
-        gating(3, 2, 0, 128)
         scatter(2, 2, 0, 256, True)
-        store(1)
-        scatter(3, 2, 0, 128, True)
-        store(0)
+        evac(3, 2, 0, 128, False)
+        scatter(2, 1, 0, 256, False)
+        mm2(3, 0, 128, 256)
+        evac(3, 0, 128, 256, True)
+        mm2(3, 2, 128, 256)
+        mm2(3, 1, 0, 256)
+        evac(3, 2, 128, 256, False)
+        gating(3, 2, 128, 256)
+        evac(3, 1, 0, 256, False)
+        scatter(3, 2, 0, 128, False)
+        gating(3, 1, 0, 256)
+        scatter(3, 1, 0, 256, True)
         scatter(3, 2, 128, 256, True)
+        scatter(3, 0, 0, 128, False)
+        scatter(3, 0, 128, 256, True)
+        store(0)
         store(2)
+        store(1)

@@ -79,9 +79,11 @@ def tile_moe_pkd_mlp_relu2_kernel(tc, x_words, x_scales, w1, w2, gate, offs, out
             raw2[e] = keep.tile([P, PACK, N], F32, name="raw2_%d" % e)
             nc.sync.dma_start(out=raw2[e][:], in_=w2[e].rearrange("(p j) c -> p j c", j=PACK))
 
-        def load_gate(e, b):
-            gates[e, b] = keep.tile([P, C], F32, name="gate%d_%d" % (e, b))
-            nc.sync.dma_start(out=gates[e, b][:], in_=gate[b * P : (b + 1) * P, e * C : (e + 1) * C])
+        def load_gate(e):
+            tile = keep.tile([P, NB, C], F32, name="gate%d" % e)
+            nc.sync.dma_start(out=tile[:], in_=gate[:, e * C : (e + 1) * C].rearrange("(b p) c -> p b c", p=P))
+            for b in range(NB):
+                gates[e, b] = tile[:, b, :]
 
         xw = {}
         xs = {}
@@ -247,161 +249,149 @@ def tile_moe_pkd_mlp_relu2_kernel(tc, x_words, x_scales, w1, w2, gate, offs, out
         load_w1(1, 1, 0, 512)
         load_w1(1, 0, 0, 512)
         load_w2(0)
+        load_gate(0)
         load_w1(2, 1, 0, 512)
-        load_gate(0, 0)
-        load_gate(0, 1)
-        load_gate(0, 2)
         load_w2(1)
         load_w1(2, 0, 0, 512)
-        load_gate(1, 0)
-        load_gate(1, 2)
-        load_gate(1, 1)
+        load_gate(1)
         load_w1(3, 0, 0, 512)
-        load_w1(3, 1, 0, 512)
         load_w2(2)
-        load_gate(3, 2)
-        load_gate(3, 1)
-        load_gate(2, 0)
-        load_gate(2, 2)
-        load_gate(3, 0)
-        load_gate(2, 1)
+        load_w1(3, 1, 0, 512)
+        load_gate(2)
         load_w2(3)
+        load_gate(3)
+        cast_w1(0, 0, 0, 0, 512, "scalar")
+        cast_w1(0, 1, 0, 0, 512, "vector")
         gather_words(2, 4, 0)
-        cast_w1(0, 0, 1, 0, 512, "scalar")
-        cast_w1(0, 0, 0, 0, 512, "gpsimd")
         gather_words(3, 4, 1)
-        gather_words(1, 3, 1)
         gather_words(0, 2, 0)
-        cast_w1(0, 1, 1, 0, 512, "vector")
-        gather_scales(0, 1)
-        cast_w1(1, 1, 1, 0, 512, "gpsimd")
         gather_words(0, 1, 1)
-        cast_w1(0, 1, 0, 0, 512, "scalar")
-        quant_w1(0, 0, 0)
-        cast_w1(1, 1, 0, 0, 512, "scalar")
-        quant_w1(0, 0, 1)
-        quant_w1(0, 1, 0)
-        cast_w1(1, 0, 0, 0, 512, "vector")
-        quant_w1(0, 1, 1)
-        mm1(0, 0)
-        cast_w1(1, 0, 1, 0, 512, "vector")
+        gather_scales(0, 1)
         gather_scales(1, 4)
-        quant_w1(1, 1, 0)
-        quant_w1(1, 0, 0)
+        quant_w1(0, 0, 0)
+        cast_w1(0, 0, 1, 0, 512, "scalar")
+        quant_w1(0, 1, 0)
+        cast_w1(0, 1, 1, 0, 512, "scalar")
+        quant_w1(0, 1, 1)
+        cast_w1(1, 1, 1, 0, 512, "scalar")
+        quant_w1(0, 0, 1)
+        mm1(0, 0)
         relu(0, 0, "scalar")
+        cast_w1(1, 1, 0, 0, 512, "vector")
+        gather_words(1, 3, 1)
         mm1(0, 128)
+        cast_w1(1, 0, 0, 0, 512, "vector")
         quant_w1(1, 1, 1)
         relu(0, 128, "scalar")
-        cast_w2(0, 256, 384, "vector")
-        square(0, 128)
         square(0, 0)
-        cast_w2(0, 0, 256, "scalar")
         quant_h(0, 0, 128)
+        quant_w1(1, 0, 0)
+        square(0, 128)
+        quant_w1(1, 1, 0)
+        cast_w1(1, 0, 1, 0, 512, "scalar")
+        cast_w2(0, 0, 256, "vector")
         quant_w2(0, 0, 256)
-        mm2(0, 0, 0, 128)
+        cast_w1(2, 1, 0, 0, 512, "gpsimd")
+        quant_w1(1, 0, 1)
         quant_h(0, 128, 256)
+        cast_w2(1, 0, 256, "gpsimd")
+        mm1(1, 0)
+        mm1(1, 128)
+        cast_w2(0, 256, 384, "scalar")
+        mm2(0, 0, 0, 128)
+        evac(0, 0, 0, 128, False)
+        gating(0, 0, 0, 128)
+        mm2(0, 0, 128, 256)
+        relu(1, 0, "scalar")
         cast_w1(2, 1, 1, 0, 512, "scalar")
         quant_w2(0, 256, 384)
-        quant_w1(1, 0, 1)
-        mm1(1, 0)
-        mm2(0, 1, 0, 256)
-        mm2(0, 2, 0, 256)
-        cast_w1(2, 1, 0, 0, 512, "gpsimd")
-        mm2(0, 0, 128, 256)
-        evac(0, 0, 0, 128, True)
-        evac(0, 1, 0, 256, True)
-        evac(0, 0, 128, 256, False)
-        gating(0, 0, 128, 256)
-        mm1(1, 128)
-        evac(0, 2, 0, 256, False)
-        scatter(0, 0, 0, 128, True)
-        cast_w2(1, 0, 256, "gpsimd")
-        relu(1, 0, "scalar")
         relu(1, 128, "scalar")
-        gating(0, 2, 0, 256)
+        cast_w1(3, 0, 0, 0, 512, "gpsimd")
+        mm2(0, 1, 0, 256)
+        evac(0, 0, 128, 256, True)
+        evac(0, 1, 0, 256, True)
+        square(1, 0)
+        mm2(0, 2, 0, 256)
+        square(1, 128)
+        evac(0, 2, 0, 256, True)
+        quant_h(1, 0, 256)
         cast_w2(1, 256, 384, "scalar")
         quant_w2(1, 256, 384)
-        square(1, 128)
-        square(1, 0)
-        cast_w1(2, 0, 0, 0, 512, "scalar")
-        cast_w1(2, 0, 1, 0, 512, "scalar")
-        quant_h(1, 0, 256)
         quant_w2(1, 0, 256)
-        mm2(1, 2, 0, 256)
-        mm2(1, 0, 0, 256)
-        quant_w1(2, 0, 0)
-        quant_w1(2, 1, 1)
-        scatter(0, 1, 0, 256, True)
         quant_w1(2, 1, 0)
+        quant_w1(2, 1, 1)
+        mm2(1, 0, 0, 256)
+        cast_w1(2, 0, 0, 0, 512, "scalar")
+        quant_w1(2, 0, 0)
+        cast_w1(2, 0, 1, 0, 512, "scalar")
         mm2(1, 1, 0, 256)
-        evac(1, 0, 0, 256, True)
+        mm2(1, 2, 0, 256)
         evac(1, 2, 0, 256, False)
-        quant_w1(2, 0, 1)
-        mm1(2, 0)
-        cast_w1(3, 0, 0, 0, 512, "gpsimd")
-        mm1(2, 128)
         scatter(0, 2, 0, 256, True)
-        gating(1, 2, 0, 256)
+        cast_w2(2, 256, 384, "gpsimd")
+        evac(1, 0, 0, 256, True)
         evac(1, 1, 0, 256, True)
+        quant_w1(2, 0, 1)
+        gating(1, 2, 0, 256)
         cast_w1(3, 0, 1, 0, 512, "scalar")
-        relu(2, 0, "scalar")
         scatter(0, 0, 128, 256, True)
+        mm1(2, 128)
+        scatter(0, 1, 0, 256, True)
         relu(2, 128, "scalar")
-        square(2, 128)
-        square(2, 0)
-        cast_w2(2, 256, 384, "scalar")
         cast_w2(2, 0, 256, "scalar")
-        quant_h(2, 0, 256)
-        quant_w1(3, 0, 1)
-        cast_w1(3, 1, 1, 0, 512, "gpsimd")
-        quant_w2(2, 256, 384)
-        mm2(2, 2, 0, 256)
+        mm1(2, 0)
         quant_w1(3, 0, 0)
         quant_w2(2, 0, 256)
-        mm2(2, 0, 0, 256)
+        relu(2, 0, "scalar")
+        square(2, 128)
+        square(2, 0)
+        quant_w2(2, 256, 384)
+        quant_h(2, 0, 256)
+        cast_w1(3, 1, 1, 0, 512, "vector")
         cast_w1(3, 1, 0, 0, 512, "scalar")
+        quant_w1(3, 0, 1)
+        quant_w1(3, 1, 0)
+        mm2(2, 0, 0, 256)
+        scatter(0, 0, 0, 128, True)
+        mm2(2, 2, 0, 256)
         quant_w1(3, 1, 1)
         evac(2, 0, 0, 256, False)
-        evac(2, 2, 0, 256, True)
-        mm2(2, 1, 0, 256)
-        scatter(1, 2, 0, 256, True)
-        scatter(1, 0, 0, 256, True)
-        quant_w1(3, 1, 0)
-        cast_w2(3, 256, 384, "gpsimd")
-        gating(2, 0, 0, 256)
         mm1(3, 0)
-        cast_w2(3, 0, 256, "scalar")
-        quant_w2(3, 0, 256)
-        relu(3, 0, "scalar")
-        square(3, 0)
-        mm1(3, 128)
-        quant_h(3, 0, 128)
-        evac(2, 1, 0, 256, False)
-        relu(3, 128, "scalar")
-        scatter(1, 1, 0, 256, True)
-        scatter(2, 0, 0, 256, True)
-        mm2(3, 0, 0, 128)
+        scatter(1, 0, 0, 256, True)
+        evac(2, 2, 0, 256, False)
+        cast_w2(3, 256, 384, "scalar")
         quant_w2(3, 256, 384)
-        square(3, 128)
-        quant_h(3, 128, 256)
+        scatter(2, 0, 0, 256, False)
+        cast_w2(3, 0, 256, "scalar")
+        mm2(2, 1, 0, 256)
+        relu(3, 0, "scalar")
+        mm1(3, 128)
+        quant_w2(3, 0, 256)
+        scatter(1, 2, 0, 256, True)
+        square(3, 0)
+        quant_h(3, 0, 128)
+        mm2(3, 0, 0, 128)
+        evac(2, 1, 0, 256, False)
         mm2(3, 2, 0, 128)
-        evac(3, 0, 0, 128, False)
-        scatter(2, 2, 0, 256, True)
+        relu(3, 128, "scalar")
+        square(3, 128)
         evac(3, 2, 0, 128, False)
-        scatter(2, 1, 0, 256, False)
-        mm2(3, 0, 128, 256)
-        evac(3, 0, 128, 256, True)
-        mm2(3, 2, 128, 256)
-        mm2(3, 1, 0, 256)
-        evac(3, 2, 128, 256, False)
-        gating(3, 2, 128, 256)
-        evac(3, 1, 0, 256, False)
-        scatter(3, 2, 0, 128, False)
-        gating(3, 1, 0, 256)
-        scatter(3, 1, 0, 256, True)
-        scatter(3, 2, 128, 256, True)
+        evac(3, 0, 0, 128, False)
+        quant_h(3, 128, 256)
         scatter(3, 0, 0, 128, False)
-        scatter(3, 0, 128, 256, True)
+        mm2(3, 2, 128, 256)
+        mm2(3, 0, 128, 256)
+        scatter(1, 1, 0, 256, True)
+        evac(3, 2, 128, 256, False)
+        mm2(3, 1, 0, 256)
+        evac(3, 0, 128, 256, False)
+        evac(3, 1, 0, 256, False)
+        scatter(3, 0, 128, 256, False)
+        scatter(2, 2, 0, 256, False)
         store(0)
+        scatter(2, 1, 0, 256, False)
+        scatter(3, 1, 0, 256, False)
+        scatter(3, 2, 0, 128, False)
+        scatter(3, 2, 128, 256, False)
         store(2)
         store(1)

@@ -19,14 +19,11 @@ P = 128
 PACK = 4
 K_PASS = P * PACK
 PASSES = K // K_PASS
-HALF = 128
 NB = N // P
 GROUP = 16
-STREAM_BUFS = 30
-HEAD_BUFS = 18
+STREAM_BUFS = 20
+HELD_BUFS = 29
 RAW_BUFS = 6
-SIDE_BUFS = 2
-WHOLE = (1, 2)
 
 
 def tile_moe_pkd_mlp_relu2_kernel(tc, x_words, x_scales, w1, w2, gate, offs, out):
@@ -42,17 +39,22 @@ def tile_moe_pkd_mlp_relu2_kernel(tc, x_words, x_scales, w1, w2, gate, offs, out
         def stream(shape, dtype):
             return ring.tile(shape, dtype, name="stream", align_bytes=64)
 
-        def head(shape, dtype):
-            return ring.tile(shape, dtype, name="head", align_bytes=64, bufs=HEAD_BUFS)
+        def held(shape, dtype):
+            return ring.tile(shape, dtype, name="held", align_bytes=64, bufs=HELD_BUFS)
 
-        def side(shape, dtype):
-            return ring.tile(shape, dtype, name="side", align_bytes=64, bufs=SIDE_BUFS)
+        def single(name):
+            return lambda shape, dtype: ring.tile(shape, dtype, name=name, align_bytes=64, bufs=1)
+
+        relay = [single("relay%d" % i) for i in range(2)]
+
+        def wide(shape, dtype):
+            return ring.tile(shape, dtype, name="wide", align_bytes=64, bufs=4)
 
         def slots(s0, s1):
             return offsets[:, s0 // GROUP : s1 // GROUP]
 
         xs_win = keep.tile([P, T], U8, name="xs_win", align_bytes=64)
-        nc.vector.memset(xs_win[:].bitcast(I32), 0)
+        nc.gpsimd.memset(xs_win[:].bitcast(I32), 0)
 
         def load_scales():
             for q in range(4):
@@ -64,41 +66,45 @@ def tile_moe_pkd_mlp_relu2_kernel(tc, x_words, x_scales, w1, w2, gate, offs, out
         xw_win = [keep.tile([P, T], I32, name="xw_win%d" % g, align_bytes=64) for g in range(PASSES)]
         raw1 = {}
         raw2 = {}
+        raw2_first = {}
         gates = {}
 
         def load_x(g):
             nc.sync.dma_start(out=xw_win[g][:], in_=x_words[g].rearrange("p t r -> p (t r)").bitcast(I32))
 
-        def load_w1(e, g, c0, c1):
+        def load_w1(e, g):
             rows = w1[e, g * K_PASS : (g + 1) * K_PASS, :].rearrange("(p j) c -> p j c", j=PACK)
-            t = ring.tile([P, PACK, c1 - c0], F32, name="raw1", bufs=RAW_BUFS)
-            nc.sync.dma_start(out=t[:], in_=rows[:, :, c0:c1])
-            raw1.setdefault((e, g), []).append((c0, c1, t))
+            raw1[e, g] = ring.tile([P, PACK, H], F32, name="raw1", bufs=RAW_BUFS)
+            nc.sync.dma_start(out=raw1[e, g][:], in_=rows)
 
-        def load_w2(e):
-            raw2[e] = keep.tile([P, PACK, N], F32, name="raw2_%d" % e)
-            nc.sync.dma_start(out=raw2[e][:], in_=w2[e].rearrange("(p j) c -> p j c", j=PACK))
+        def load_w2(e, b0, b1):
+            raw2[e, b0] = keep.tile([P, PACK, (b1 - b0) * P], F32, name="raw2_%d_%d" % (e, b0))
+            rows = w2[e].rearrange("(p j) c -> p j c", j=PACK)
+            nc.sync.dma_start(out=raw2[e, b0][:], in_=rows[:, :, b0 * P : b1 * P])
+            for b in range(b0, b1):
+                raw2[e, b] = raw2[e, b0]
+                raw2_first[e, b] = b0
 
-        def load_gate(e):
-            tile = keep.tile([P, NB, C], F32, name="gate%d" % e)
-            nc.sync.dma_start(out=tile[:], in_=gate[:, e * C : (e + 1) * C].rearrange("(b p) c -> p b c", p=P))
-            for b in range(NB):
-                gates[e, b] = tile[:, b, :]
+        def load_gate(e0, e1):
+            tile = keep.tile([P, (e1 - e0) * C], F32, name="gate%d" % e0)
+            nc.sync.dma_start(out=tile[:], in_=gate[0:P, e0 * C : e1 * C])
+            for e in range(e0, e1):
+                gates[e] = tile[:, (e - e0) * C : (e - e0 + 1) * C]
 
         xw = {}
         xs = {}
 
-        def gather_scales(e, e1):
-            tile = head([P, (e1 - e) * C], U8)
-            nc.vector.tensor_copy(tile[:], xs_win[:].indirect(slots(e * C, e1 * C)))
-            for n in range(e, e1):
-                xs[n] = tile[:, (n - e) * C : (n - e + 1) * C]
+        def gather_scales(e0, e1):
+            tile = keep.tile([P, (e1 - e0) * C], U8, name="xs%d" % e0, align_bytes=64)
+            nc.vector.tensor_copy(tile[:], xs_win[:].indirect(slots(e0 * C, e1 * C)))
+            for e in range(e0, e1):
+                xs[e] = tile[:, (e - e0) * C : (e - e0 + 1) * C]
 
-        def gather_words(e, e1, g):
-            tile = head([P, (e1 - e) * C], U32)
-            nc.vector.tensor_copy(tile[:], xw_win[g][:].bitcast(U32).indirect(slots(e * C, e1 * C)))
-            for n in range(e, e1):
-                xw[n, g] = tile[:, (n - e) * C : (n - e + 1) * C]
+        def gather_words(e0, e1, g, place):
+            tile = place([P, (e1 - e0) * C], U32)
+            nc.vector.tensor_copy(tile[:], xw_win[g][:].bitcast(U32).indirect(slots(e0 * C, e1 * C)))
+            for e in range(e0, e1):
+                xw[e, g] = tile[:, (e - e0) * C : (e - e0 + 1) * C]
 
         def cast(engine, dst, src):
             if engine == "vector":
@@ -112,286 +118,221 @@ def tile_moe_pkd_mlp_relu2_kernel(tc, x_words, x_scales, w1, w2, gate, offs, out
         w1c = {}
         w1s = {}
 
-        def cast_w1(e, g, u, c0, c1, engine):
-            if (e, g, u) not in w1b:
-                w1b[e, g, u] = (side if engine == "gpsimd" else stream)([P, 2 * P * PACK], BF16)
-            raw = raw1[e, g][0][2]
-            if engine == "gpsimd":
-                dst = w1b[e, g, u][:].rearrange("p (t m j) -> p m t j", t=2, j=PACK)
-                src = raw[:].rearrange("p j (m t) -> p m t j", t=PACK)[:, :, 2 * u : 2 * u + 2, :]
-            else:
-                dst = w1b[e, g, u][:].rearrange("p (t m j) -> p m j t", t=2, j=PACK)
-                src = raw[:].rearrange("p j (m t) -> p m j t", t=PACK)[:, :, :, 2 * u : 2 * u + 2]
-            cast(engine, dst, src)
+        def cast_w1(e, g, u, engine, place=stream):
+            w1b[e, g, u] = place([P, 2 * P * PACK], BF16)
+            walk = "p m t j" if engine == "gpsimd" else "p m j t"
+            dst = w1b[e, g, u][:].rearrange("p (t m j) -> " + walk, t=2, j=PACK)
+            src = raw1[e, g][:].rearrange("p j (m u t) -> p j m u t", u=2, t=2)[:, :, :, u, :]
+            cast(engine, dst, src.rearrange("p j m t -> " + walk))
 
-        def quant_w1(e, g, u):
-            w1c[e, g, u] = keep.tile([P, 2 * P], U32, name="w1c%d_%d_%d" % (e, g, u), align_bytes=64)
-            w1s[e, g, u] = (head if e <= 1 else stream)([P, 2 * P], U8)
+        def quant_w1(e, g, u, place=held):
+            w1c[e, g, u] = place([P, 2 * P], U32)
+            w1s[e, g, u] = stream([P, 2 * P], U8)
             nc.vector.quantize_mx(out=w1c[e, g, u][:].bitcast(FP8X4), scales=w1s[e, g, u][:], in_=w1b[e, g, u][:])
 
         w2b = {}
         w2c = {}
         w2s = {}
 
-        def cast_w2(e, c0, c1, engine):
-            w2b[e, c0] = (side if engine == "gpsimd" else stream)([P, (c1 - c0) * PACK], BF16)
+        def cast_w2(e, b0, b1, engine, place=stream):
+            w2b[e, b0] = place([P, (b1 - b0) * P * PACK], BF16)
+            raw = raw2[e, b0][:, :, (b0 - raw2_first[e, b0]) * P : (b1 - raw2_first[e, b0]) * P]
             if engine == "gpsimd":
-                dst = w2b[e, c0][:].rearrange("p (c j) -> p c j", j=PACK)
-                src = raw2[e][:, :, c0:c1].rearrange("p j c -> p c j")
+                dst = w2b[e, b0][:].rearrange("p (c j) -> p c j", j=PACK)
+                src = raw.rearrange("p j c -> p c j")
             else:
-                dst = w2b[e, c0][:].rearrange("p (c i j) -> p c j i", i=4, j=PACK)
-                src = raw2[e][:, :, c0:c1].rearrange("p j (c i) -> p c j i", i=4)
+                dst = w2b[e, b0][:].rearrange("p (c i j) -> p c j i", i=4, j=PACK)
+                src = raw.rearrange("p j (c i) -> p c j i", i=4)
             cast(engine, dst, src)
 
-        def quant_w2(e, c0, c1):
-            codes = keep.tile([P, c1 - c0], U32, name="w2c%d_%d" % (e, c0), align_bytes=64)
-            scales = (head if e == 0 else stream)([P, c1 - c0], U8)
-            nc.vector.quantize_mx(out=codes[:].bitcast(FP8X4), scales=scales[:], in_=w2b[e, c0][:])
-            for b in range(c0 // P, c1 // P):
-                w2c[e, b] = codes[:, b * P - c0 : (b + 1) * P - c0]
-                w2s[e, b] = scales[:, b * P - c0 : (b + 1) * P - c0]
+        def quant_w2(e, b0, b1):
+            codes = held([P, (b1 - b0) * P], U32)
+            scales = stream([P, (b1 - b0) * P], U8)
+            nc.vector.quantize_mx(out=codes[:].bitcast(FP8X4), scales=scales[:], in_=w2b[e, b0][:])
+            for b in range(b0, b1):
+                w2c[e, b] = codes[:, (b - b0) * P : (b - b0 + 1) * P]
+                w2s[e, b] = scales[:, (b - b0) * P : (b - b0 + 1) * P]
 
         acc1 = {}
-        relus = {}
         hb = {}
         hc = {}
         hs = {}
 
-        def mm1(e, s0):
-            acc = psum.tile([P, PACK, HALF], F32, name="acc1")
-            acc1[e, s0] = acc
+        def mm1(e, g, u):
+            first = (e, 2 * u) not in acc1
+            for t in range(2):
+                if first:
+                    acc1[e, 2 * u + t] = psum.tile([P, C], F32, name="acc1")
+                nc.tensor.matmul_mx(
+                    out=acc1[e, 2 * u + t][:],
+                    lhsT=w1c[e, g, u][:, t * P : (t + 1) * P].bitcast(FP8X4),
+                    lhsT_scale=w1s[e, g, u][:, t * P : (t + 1) * P],
+                    rhs=xw[e, g].bitcast(FP8X4),
+                    rhs_scale=xs[e][4 * g : P, :],
+                    start=first,
+                    stop=not first,
+                )
+
+        relus = {}
+
+        def relu(e):
+            relus[e] = stream([P, PACK, C], F32)
             for t in range(PACK):
-                for g in range(PASSES):
-                    nc.tensor.matmul_mx(
-                        out=acc[:, t, :],
-                        lhsT=w1c[e, g, t // 2][:, t % 2 * P : (t % 2 + 1) * P].bitcast(FP8X4),
-                        lhsT_scale=w1s[e, g, t // 2][:, t % 2 * P : (t % 2 + 1) * P],
-                        rhs=xw[e, g][:, s0 : s0 + HALF].bitcast(FP8X4),
-                        rhs_scale=xs[e][4 * g : P, s0 : s0 + HALF],
-                        start=(g == 0),
-                        stop=(g == PASSES - 1),
-                    )
+                nc.scalar.activation(out=relus[e][:, t, :], in_=acc1[e, t][:], func=ACT.Relu)
 
-        def relu(e, s0, engine):
-            relus[e, s0] = stream([P, HALF, PACK], F32)
-            src = acc1[e, s0][:].rearrange("p t s -> p s t")
-            if engine == "vector":
-                nc.vector.tensor_scalar(out=relus[e, s0][:], in0=src, scalar1=0.0, scalar2=None, op0=ALU.max)
-            else:
-                nc.scalar.activation(out=relus[e, s0][:], in_=src, func=ACT.Relu)
-
-        def square(e, s0):
-            if e in WHOLE:
-                if e not in hb:
-                    hb[e] = stream([P, C * PACK], BF16)
-                hb[e, s0] = hb[e][:, s0 * PACK : (s0 + HALF) * PACK]
-            else:
-                hb[e, s0] = stream([P, HALF * PACK], BF16)[:]
+        def square(e):
+            hb[e] = stream([P, C * PACK], BF16)
             nc.scalar.activation(
-                out=hb[e, s0],
-                in_=relus[e, s0][:].rearrange("p s t -> p (s t)"),
+                out=hb[e][:].rearrange("p (c i t) -> p c t i", i=4, t=PACK),
+                in_=relus[e][:].rearrange("p t (c i) -> p c t i", i=4),
                 func=ACT.Square,
             )
 
-        def quant_h(e, s0, s1):
-            if e not in hc:
-                hc[e] = keep.tile([P, C], U32, name="hc%d" % e, align_bytes=64)
-                hs[e] = (head if e == 0 else stream)([P, C], U8)
-            nc.vector.quantize_mx(
-                out=hc[e][:, s0:s1].bitcast(FP8X4), scales=hs[e][:, s0:s1], in_=hb[e][:] if e in WHOLE else hb[e, s0]
-            )
+        def quant_h(e):
+            hc[e] = held([P, C], U32)
+            hs[e] = stream([P, C], U8)
+            nc.vector.quantize_mx(out=hc[e][:].bitcast(FP8X4), scales=hs[e][:], in_=hb[e][:])
 
         acc2 = {}
         ys = {}
 
-        def mm2(e, b, s0, s1):
-            acc = psum.tile([P, s1 - s0], F32, name="acc2")
-            acc2[e, b, s0] = acc
+        def mm2(e, b):
+            acc2[e, b] = psum.tile([P, C], F32, name="acc2")
             nc.tensor.matmul_mx(
-                out=acc[:],
+                out=acc2[e, b][:],
                 lhsT=w2c[e, b].bitcast(FP8X4),
                 lhsT_scale=w2s[e, b],
-                rhs=hc[e][:, s0:s1].bitcast(FP8X4),
-                rhs_scale=hs[e][:, s0:s1],
+                rhs=hc[e][:].bitcast(FP8X4),
+                rhs_scale=hs[e][:],
                 start=True,
                 stop=True,
             )
 
-        def evac(e, b, s0, s1, gated):
-            ys[e, b, s0] = stream([P, s1 - s0], F32)
-            if gated:
-                nc.vector.tensor_tensor(ys[e, b, s0][:], acc2[e, b, s0][:], gates[e, b][:, s0:s1], ALU.mult)
-            else:
-                nc.scalar.activation(out=ys[e, b, s0][:], in_=acc2[e, b, s0][:], func=ACT.Copy)
+        gated = {}
 
-        def gating(e, b, s0, s1):
-            plain = ys[e, b, s0]
-            ys[e, b, s0] = stream([P, s1 - s0], F32)
-            nc.gpsimd.tensor_tensor(ys[e, b, s0][:], plain[:], gates[e, b][:, s0:s1], ALU.mult)
+        def evac(e, b, engine):
+            ys[e, b] = stream([P, C], F32)
+            gated[e, b] = engine == "vector"
+            if engine == "vector":
+                nc.vector.tensor_tensor(ys[e, b][:], acc2[e, b][:], gates[e], ALU.mult)
+            else:
+                nc.scalar.activation(out=ys[e, b][:], in_=acc2[e, b][:], func=ACT.Copy)
+
+        def gating(e, b, place=stream):
+            plain = ys[e, b]
+            ys[e, b] = place([P, C], F32)
+            gated[e, b] = True
+            nc.gpsimd.tensor_tensor(ys[e, b][:], plain[:], gates[e], ALU.mult)
 
         windows = [keep.tile([P, T], F32, name="window%d" % b) for b in range(NB)]
 
-        def scatter(e, b, s0, s1, gated):
-            dst = windows[b][:].indirect(slots(e * C + s0, e * C + s1))
-            if gated:
-                nc.vector.tensor_copy(dst, ys[e, b, s0][:])
+        def scatter(e, b):
+            dst = windows[b][:].indirect(slots(e * C, (e + 1) * C))
+            if gated[e, b]:
+                nc.vector.tensor_copy(dst, ys[e, b][:])
             else:
-                nc.vector.tensor_tensor(dst, ys[e, b, s0][:], gates[e, b][:, s0:s1], ALU.mult)
+                nc.vector.tensor_tensor(dst, ys[e, b][:], gates[e], ALU.mult)
 
         def store(b):
             nc.sync.dma_start(out=out[b * P : (b + 1) * P, :], in_=windows[b][:])
 
         load_x(0)
-        load_x(1)
-        load_w1(0, 0, 0, 512)
         load_scales()
-        load_w1(0, 1, 0, 512)
-        load_w1(1, 1, 0, 512)
-        load_w1(1, 0, 0, 512)
-        load_w2(0)
-        load_gate(0)
-        load_w1(2, 1, 0, 512)
-        load_w2(1)
-        load_w1(2, 0, 0, 512)
-        load_gate(1)
-        load_w1(3, 0, 0, 512)
-        load_w2(2)
-        load_w1(3, 1, 0, 512)
-        load_gate(2)
-        load_w2(3)
-        load_gate(3)
-        cast_w1(0, 0, 0, 0, 512, "scalar")
-        cast_w1(0, 1, 0, 0, 512, "vector")
-        gather_words(2, 4, 0)
-        gather_words(3, 4, 1)
-        gather_words(0, 2, 0)
-        gather_words(0, 1, 1)
-        gather_scales(0, 1)
-        gather_scales(1, 4)
-        quant_w1(0, 0, 0)
-        cast_w1(0, 0, 1, 0, 512, "scalar")
-        quant_w1(0, 1, 0)
-        cast_w1(0, 1, 1, 0, 512, "scalar")
-        quant_w1(0, 1, 1)
-        cast_w1(1, 1, 1, 0, 512, "scalar")
-        quant_w1(0, 0, 1)
-        mm1(0, 0)
-        relu(0, 0, "scalar")
-        cast_w1(1, 1, 0, 0, 512, "vector")
-        gather_words(1, 3, 1)
-        mm1(0, 128)
-        cast_w1(1, 0, 0, 0, 512, "vector")
-        quant_w1(1, 1, 1)
-        relu(0, 128, "scalar")
-        square(0, 0)
-        quant_h(0, 0, 128)
-        quant_w1(1, 0, 0)
-        square(0, 128)
-        quant_w1(1, 1, 0)
-        cast_w1(1, 0, 1, 0, 512, "scalar")
-        cast_w2(0, 0, 256, "vector")
-        quant_w2(0, 0, 256)
-        cast_w1(2, 1, 0, 0, 512, "gpsimd")
-        quant_w1(1, 0, 1)
-        quant_h(0, 128, 256)
-        cast_w2(1, 0, 256, "gpsimd")
-        mm1(1, 0)
-        mm1(1, 128)
-        cast_w2(0, 256, 384, "scalar")
-        mm2(0, 0, 0, 128)
-        evac(0, 0, 0, 128, False)
-        gating(0, 0, 0, 128)
-        mm2(0, 0, 128, 256)
-        relu(1, 0, "scalar")
-        cast_w1(2, 1, 1, 0, 512, "scalar")
-        quant_w2(0, 256, 384)
-        relu(1, 128, "scalar")
-        cast_w1(3, 0, 0, 0, 512, "gpsimd")
-        mm2(0, 1, 0, 256)
-        evac(0, 0, 128, 256, True)
-        evac(0, 1, 0, 256, True)
-        square(1, 0)
-        mm2(0, 2, 0, 256)
-        square(1, 128)
-        evac(0, 2, 0, 256, True)
-        quant_h(1, 0, 256)
-        cast_w2(1, 256, 384, "scalar")
-        quant_w2(1, 256, 384)
-        quant_w2(1, 0, 256)
-        quant_w1(2, 1, 0)
-        quant_w1(2, 1, 1)
-        mm2(1, 0, 0, 256)
-        cast_w1(2, 0, 0, 0, 512, "scalar")
-        quant_w1(2, 0, 0)
-        cast_w1(2, 0, 1, 0, 512, "scalar")
-        mm2(1, 1, 0, 256)
-        mm2(1, 2, 0, 256)
-        evac(1, 2, 0, 256, False)
-        scatter(0, 2, 0, 256, True)
-        cast_w2(2, 256, 384, "gpsimd")
-        evac(1, 0, 0, 256, True)
-        evac(1, 1, 0, 256, True)
-        quant_w1(2, 0, 1)
-        gating(1, 2, 0, 256)
-        cast_w1(3, 0, 1, 0, 512, "scalar")
-        scatter(0, 0, 128, 256, True)
-        mm1(2, 128)
-        scatter(0, 1, 0, 256, True)
-        relu(2, 128, "scalar")
-        cast_w2(2, 0, 256, "scalar")
-        mm1(2, 0)
-        quant_w1(3, 0, 0)
-        quant_w2(2, 0, 256)
-        relu(2, 0, "scalar")
-        square(2, 128)
-        square(2, 0)
-        quant_w2(2, 256, 384)
-        quant_h(2, 0, 256)
-        cast_w1(3, 1, 1, 0, 512, "vector")
-        cast_w1(3, 1, 0, 0, 512, "scalar")
-        quant_w1(3, 0, 1)
-        quant_w1(3, 1, 0)
-        mm2(2, 0, 0, 256)
-        scatter(0, 0, 0, 128, True)
-        mm2(2, 2, 0, 256)
-        quant_w1(3, 1, 1)
-        evac(2, 0, 0, 256, False)
-        mm1(3, 0)
-        scatter(1, 0, 0, 256, True)
-        evac(2, 2, 0, 256, False)
-        cast_w2(3, 256, 384, "scalar")
-        quant_w2(3, 256, 384)
-        scatter(2, 0, 0, 256, False)
-        cast_w2(3, 0, 256, "scalar")
-        mm2(2, 1, 0, 256)
-        relu(3, 0, "scalar")
-        mm1(3, 128)
-        quant_w2(3, 0, 256)
-        scatter(1, 2, 0, 256, True)
-        square(3, 0)
-        quant_h(3, 0, 128)
-        mm2(3, 0, 0, 128)
-        evac(2, 1, 0, 256, False)
-        mm2(3, 2, 0, 128)
-        relu(3, 128, "scalar")
-        square(3, 128)
-        evac(3, 2, 0, 128, False)
-        evac(3, 0, 0, 128, False)
-        quant_h(3, 128, 256)
-        scatter(3, 0, 0, 128, False)
-        mm2(3, 2, 128, 256)
-        mm2(3, 0, 128, 256)
-        scatter(1, 1, 0, 256, True)
-        evac(3, 2, 128, 256, False)
-        mm2(3, 1, 0, 256)
-        evac(3, 0, 128, 256, False)
-        evac(3, 1, 0, 256, False)
-        scatter(3, 0, 128, 256, False)
-        scatter(2, 2, 0, 256, False)
-        store(0)
-        scatter(2, 1, 0, 256, False)
-        scatter(3, 1, 0, 256, False)
-        scatter(3, 2, 0, 128, False)
-        scatter(3, 2, 128, 256, False)
-        store(2)
-        store(1)
+        load_w1(0, 0)
+        load_w1(0, 1)
+        load_x(1)
+        for e in range(E):
+            load_w2(e, 0, 3)
+            load_gate(e, e + 1)
+            if e + 1 < E:
+                load_w1(e + 1, 0)
+                load_w1(e + 1, 1)
+
+        def prepare(e, g, u, place=held):
+            quant_w1(e, g, u, place)
+            mm1(e, g, u)
+
+        gather_words(0, 2, 0, wide)
+        gather_words(2, 4, 0, wide)
+        gather_scales(0, 2)
+        gather_scales(2, 4)
+        for u in range(2):
+            cast_w1(0, 0, u, "scalar")
+        prepare(0, 0, 0)
+        cast_w1(0, 1, 0, "vector")
+        cast_w1(0, 1, 1, "scalar")
+        prepare(0, 0, 1)
+        gather_words(0, 1, 1, held)
+        prepare(0, 1, 0)
+        prepare(0, 1, 1, wide)
+        gather_words(1, E, 1, wide)
+        relu(0)
+        cast_w2(0, 0, 2, "vector")
+        cast_w2(0, 2, 3, "vector")
+        square(0)
+        quant_w2(0, 0, 2)
+        quant_w2(0, 2, 3)
+        for e in range(2):
+            n = e + 1
+            slot = relay[0]
+            quant_h(e)
+            for b in range(NB):
+                mm2(e, b)
+            if e == 0:
+                cast_w1(n, 0, 0, "scalar")
+                cast_w1(n, 0, 1, "vector")
+                prepare(n, 0, 0)
+            else:
+                cast_w1(n, 1, 0, "scalar")
+                prepare(n, 0, 0)
+                cast_w1(n, 0, 1, "vector")
+            evac(e, 0, "vector")
+            prepare(n, 0, 1)
+            scatter(e, 0)
+            evac(e, 1, "scalar")
+            if e == 0:
+                cast_w1(n, 1, 0, "scalar")
+            cast_w1(n, 1, 1, "scalar", slot)
+            prepare(n, 1, 0)
+            prepare(n, 1, 1)
+            gating(e, 1)
+            scatter(e, 1)
+            evac(e, 2, "scalar")
+            gating(e, 2, slot)
+            scatter(e, 2)
+            cast_w2(n, 0, 2, "scalar")
+            cast_w2(n, 2, 3, "gpsimd")
+            if e == 1:
+                cast_w1(n + 1, 0, 1, "scalar")
+            cast_w1(n + 1, 0, 0, "gpsimd")
+            relu(n)
+            square(n)
+            quant_w2(n, 2, 3)
+            quant_w2(n, 0, 2)
+        quant_h(2)
+        for b in range(NB):
+            mm2(2, b)
+        cast_w1(3, 1, 1, "vector")
+        cast_w1(3, 1, 0, "scalar")
+        prepare(3, 0, 0)
+        prepare(3, 1, 0)
+        prepare(3, 0, 1)
+        prepare(3, 1, 1)
+        for b in range(2):
+            evac(2, b, "scalar")
+            scatter(2, b)
+        cast_w2(3, 0, 2, "scalar")
+        relu(3)
+        cast_w2(3, 2, 3, "scalar")
+        square(3)
+        quant_w2(3, 0, 2)
+        quant_h(3)
+        evac(2, 2, "scalar")
+        quant_w2(3, 2, 3)
+        for b in range(NB):
+            mm2(3, b)
+        scatter(2, 2)
+        for b in range(NB):
+            evac(3, b, "scalar")
+            scatter(3, b)
+            store(b)

@@ -272,67 +272,83 @@ def tile_moe_pkd_mlp_relu2_kernel(tc, x_words, x_scales, w1, w2, gate, offs, out
         square(0)
         quant_w2(0, 0, 2)
         quant_w2(0, 2, 3)
-        for e in range(2):
-            n = e + 1
-            slot = relay[0]
-            quant_h(e)
-            for b in range(NB):
-                mm2(e, b)
-            if e == 0:
-                cast_w1(n, 0, 0, "scalar")
-                cast_w1(n, 0, 1, "vector")
-                prepare(n, 0, 0)
-            else:
-                cast_w1(n, 1, 0, "scalar")
-                prepare(n, 0, 0)
-                cast_w1(n, 0, 1, "vector")
-            evac(e, 0, "vector")
-            prepare(n, 0, 1)
-            scatter(e, 0)
-            evac(e, 1, "scalar")
-            if e == 0:
-                cast_w1(n, 1, 0, "scalar")
-            cast_w1(n, 1, 1, "scalar", slot)
-            prepare(n, 1, 0)
-            prepare(n, 1, 1)
-            gating(e, 1)
-            scatter(e, 1)
-            evac(e, 2, "scalar")
-            gating(e, 2, slot)
-            scatter(e, 2)
-            cast_w2(n, 0, 2, "scalar")
-            cast_w2(n, 2, 3, "gpsimd")
-            if e == 1:
-                cast_w1(n + 1, 0, 1, "scalar")
-            cast_w1(n + 1, 0, 0, "gpsimd")
-            relu(n)
-            square(n)
-            quant_w2(n, 2, 3)
-            quant_w2(n, 0, 2)
-        quant_h(2)
+        quant_h(0)
         for b in range(NB):
-            mm2(2, b)
-        cast_w1(3, 1, 1, "vector")
+            mm2(0, b)
+        cast_w1(1, 0, 0, "scalar")
+        cast_w1(1, 0, 1, "vector")
+        prepare(1, 0, 0)
+        prepare(1, 0, 1)
+        evac(0, 0, "scalar")
+        scatter(0, 0)
+        cast_w1(1, 1, 0, "scalar")
+        cast_w1(1, 1, 1, "scalar")
+        prepare(1, 1, 0)
+        cast_w2(1, 2, 3, "vector")
+        prepare(1, 1, 1)
+        evac(0, 1, "scalar")
+        scatter(0, 1)
+        cast_w2(1, 0, 2, "scalar")
+        evac(0, 2, "scalar")
+        scatter(0, 2)
+        relu(1)
+        square(1)
+        quant_w2(1, 2, 3)
+        quant_w2(1, 0, 2)
+
+        quant_h(1)
+        for b in range(NB):
+            mm2(1, b)
+        cast_w1(2, 1, 0, "scalar")
+        cast_w1(2, 0, 0, "vector")
+        cast_w1(2, 1, 1, "scalar")
+        cast_w1(2, 0, 1, "vector")
+        prepare(2, 0, 0)
+        prepare(2, 0, 1)
+        prepare(2, 1, 0)
+        prepare(2, 1, 1)
+        for b in range(2):
+            evac(1, b, "scalar")
+            scatter(1, b)
+        cast_w2(2, 0, 2, "scalar")
+        relu(2)
+        evac(1, 2, "scalar")
+        scatter(1, 2)
+        square(2)
+        quant_w2(2, 0, 2)
+        quant_h(2)
+        mm2(2, 0)
+        mm2(2, 1)
+        cast_w1(3, 0, 0, "scalar")
         cast_w1(3, 1, 0, "scalar")
+        cast_w1(3, 1, 1, "vector")
         prepare(3, 0, 0)
         prepare(3, 1, 0)
-        prepare(3, 0, 1)
+        cast_w1(3, 0, 1, "vector")
         prepare(3, 1, 1)
-        for b in range(2):
-            evac(2, b, "scalar")
-            scatter(2, b)
-        cast_w2(3, 0, 2, "scalar")
+        prepare(3, 0, 1)
+        evac(2, 0, "scalar")
+        scatter(2, 0)
+        cast_w2(2, 2, 3, "scalar")
+        quant_w2(2, 2, 3)
+        mm2(2, 2)
+        evac(2, 1, "scalar")
+        scatter(2, 1)
+        cast_w2(3, 0, 1, "scalar")
         relu(3)
-        cast_w2(3, 2, 3, "scalar")
         square(3)
-        quant_w2(3, 0, 2)
+        quant_w2(3, 0, 1)
         quant_h(3)
+        mm2(3, 0)
         evac(2, 2, "scalar")
-        quant_w2(3, 2, 3)
-        for b in range(NB):
-            mm2(3, b)
         scatter(2, 2)
+        cast_w2(3, 1, 3, "scalar")
+        evac(3, 0, "scalar")
+        quant_w2(3, 1, 3)
+        mm2(3, 1)
+        mm2(3, 2)
         for b in range(NB):
-            evac(3, b, "scalar")
+            if b:
+                evac(3, b, "scalar")
             scatter(3, b)
             store(b)

@@ -1,6 +1,7 @@
 from contextlib import ExitStack
 
 import concourse.mybir as mybir
+from concourse.masks import make_identity
 
 K, T, E, C, H, N = 1024, 1024, 4, 256, 512, 384
 FLOPS = 2 * E * C * (K * H + H * N)
@@ -21,6 +22,7 @@ K_PASS = P * PACK
 PASSES = K // K_PASS
 NB = N // P
 GROUP = 16
+RUN = E * C // P
 STREAM_BUFS = 20
 HELD_BUFS = 29
 RAW_BUFS = 6
@@ -85,11 +87,24 @@ def tile_moe_pkd_mlp_relu2_kernel(tc, x_words, x_scales, w1, w2, gate, offs, out
                 raw2[e, b] = raw2[e, b0]
                 raw2_first[e, b] = b0
 
-        def load_gate(e0, e1):
-            tile = keep.tile([P, (e1 - e0) * C], F32, name="gate%d" % e0)
-            nc.sync.dma_start(out=tile[:], in_=gate[0:P, e0 * C : e1 * C])
-            for e in range(e0, e1):
-                gates[e] = tile[:, (e - e0) * C : (e - e0 + 1) * C]
+        gate_rows = keep.tile([P, RUN], F32, name="gate_rows")
+        gate_all = keep.tile([P, E * C], F32, name="gate_all")
+        identity = keep.tile([P, P], F32, name="identity")
+        make_identity(nc, identity[:])
+
+        def load_gate():
+            nc.sync.dma_start(out=gate_rows[:], in_=gate[0].rearrange("(p j) -> p j", j=RUN))
+
+        def spread_gate():
+            for j0 in range(0, RUN, PACK):
+                bank = psum.tile([P, PACK, P], F32, name="acc2")
+                for j in range(PACK):
+                    column = gate_rows[:, j0 + j : j0 + j + 1].to_broadcast([P, P])
+                    nc.tensor.transpose(bank[:, j, :], column, identity[:])
+                dst = gate_all[:].rearrange("p (n j) -> p n j", j=RUN)[:, :, j0 : j0 + PACK]
+                nc.scalar.activation(out=dst, in_=bank[:].rearrange("p j n -> p n j"), func=ACT.Copy)
+            for e in range(E):
+                gates[e] = gate_all[:, e * C : (e + 1) * C]
 
         xw = {}
         xs = {}
@@ -118,17 +133,24 @@ def tile_moe_pkd_mlp_relu2_kernel(tc, x_words, x_scales, w1, w2, gate, offs, out
         w1c = {}
         w1s = {}
 
-        def cast_w1(e, g, u, engine, place=stream):
-            w1b[e, g, u] = place([P, 2 * P * PACK], BF16)
-            walk = "p m t j" if engine == "gpsimd" else "p m j t"
-            dst = w1b[e, g, u][:].rearrange("p (t m j) -> " + walk, t=2, j=PACK)
-            src = raw1[e, g][:].rearrange("p j (m u t) -> p j m u t", u=2, t=2)[:, :, :, u, :]
-            cast(engine, dst, src.rearrange("p j m t -> " + walk))
+        def cast_w1(e, g, engine):
+            tile = stream([P, H * PACK], BF16)
+            dst = tile[:].rearrange("p (t m j) -> p m j t", t=PACK, j=PACK)
+            src = raw1[e, g][:].rearrange("p j (m t) -> p m j t", t=PACK)
+            cast(engine, dst, src)
+            for u in range(2):
+                w1b[e, g, u] = tile[:, u * 2 * H : (u + 1) * 2 * H]
+
+        def cast_w1_half(e, g, u, engine):
+            w1b[e, g, u] = stream([P, 2 * H], BF16)[:]
+            dst = w1b[e, g, u].rearrange("p (t m j) -> p m j t", t=2, j=PACK)
+            src = raw1[e, g][:].rearrange("p j (m u t) -> p u m j t", u=2, t=2)
+            cast(engine, dst, src[:, u])
 
         def quant_w1(e, g, u, place=held):
             w1c[e, g, u] = place([P, 2 * P], U32)
             w1s[e, g, u] = stream([P, 2 * P], U8)
-            nc.vector.quantize_mx(out=w1c[e, g, u][:].bitcast(FP8X4), scales=w1s[e, g, u][:], in_=w1b[e, g, u][:])
+            nc.vector.quantize_mx(out=w1c[e, g, u][:].bitcast(FP8X4), scales=w1s[e, g, u][:], in_=w1b[e, g, u])
 
         w2b = {}
         w2c = {}
@@ -236,6 +258,7 @@ def tile_moe_pkd_mlp_relu2_kernel(tc, x_words, x_scales, w1, w2, gate, offs, out
         def store(b):
             nc.sync.dma_start(out=out[b * P : (b + 1) * P, :], in_=windows[b][:])
 
+        load_gate()
         load_x(0)
         load_scales()
         load_w1(0, 0)
@@ -243,7 +266,6 @@ def tile_moe_pkd_mlp_relu2_kernel(tc, x_words, x_scales, w1, w2, gate, offs, out
         load_x(1)
         for e in range(E):
             load_w2(e, 0, 3)
-            load_gate(e, e + 1)
             if e + 1 < E:
                 load_w1(e + 1, 0)
                 load_w1(e + 1, 1)
@@ -252,15 +274,15 @@ def tile_moe_pkd_mlp_relu2_kernel(tc, x_words, x_scales, w1, w2, gate, offs, out
             quant_w1(e, g, u, place)
             mm1(e, g, u)
 
+        spread_gate()
         gather_words(0, 2, 0, wide)
         gather_words(2, 4, 0, wide)
         gather_scales(0, 2)
         gather_scales(2, 4)
-        for u in range(2):
-            cast_w1(0, 0, u, "scalar")
+        cast_w1(0, 0, "scalar")
+        cast_w1_half(0, 1, 0, "vector")
+        cast_w1_half(0, 1, 1, "scalar")
         prepare(0, 0, 0)
-        cast_w1(0, 1, 0, "vector")
-        cast_w1(0, 1, 1, "scalar")
         prepare(0, 0, 1)
         gather_words(0, 1, 1, held)
         prepare(0, 1, 0)
@@ -272,72 +294,52 @@ def tile_moe_pkd_mlp_relu2_kernel(tc, x_words, x_scales, w1, w2, gate, offs, out
         square(0)
         quant_w2(0, 0, 2)
         quant_w2(0, 2, 3)
-        quant_h(0)
-        for b in range(NB):
-            mm2(0, b)
-        cast_w1(1, 0, 0, "scalar")
-        cast_w1(1, 0, 1, "vector")
-        prepare(1, 0, 0)
-        prepare(1, 0, 1)
-        evac(0, 0, "scalar")
-        scatter(0, 0)
-        cast_w1(1, 1, 0, "scalar")
-        cast_w1(1, 1, 1, "scalar")
-        prepare(1, 1, 0)
-        cast_w2(1, 2, 3, "vector")
-        prepare(1, 1, 1)
-        evac(0, 1, "scalar")
-        scatter(0, 1)
-        cast_w2(1, 0, 2, "scalar")
-        evac(0, 2, "scalar")
-        scatter(0, 2)
-        relu(1)
-        square(1)
-        quant_w2(1, 2, 3)
-        quant_w2(1, 0, 2)
-
-        quant_h(1)
-        for b in range(NB):
-            mm2(1, b)
-        cast_w1(2, 1, 0, "scalar")
-        cast_w1(2, 0, 0, "vector")
-        cast_w1(2, 1, 1, "scalar")
-        cast_w1(2, 0, 1, "vector")
-        prepare(2, 0, 0)
-        prepare(2, 0, 1)
-        prepare(2, 1, 0)
-        prepare(2, 1, 1)
-        for b in range(2):
-            evac(1, b, "scalar")
-            scatter(1, b)
-        cast_w2(2, 0, 2, "scalar")
-        relu(2)
-        evac(1, 2, "scalar")
-        scatter(1, 2)
-        square(2)
-        quant_w2(2, 0, 2)
-        quant_h(2)
-        mm2(2, 0)
-        mm2(2, 1)
-        cast_w1(3, 0, 0, "scalar")
-        cast_w1(3, 1, 0, "scalar")
-        cast_w1(3, 1, 1, "vector")
-        prepare(3, 0, 0)
-        prepare(3, 1, 0)
-        cast_w1(3, 0, 1, "vector")
-        prepare(3, 1, 1)
-        prepare(3, 0, 1)
-        evac(2, 0, "scalar")
-        scatter(2, 0)
-        cast_w2(2, 2, 3, "scalar")
-        quant_w2(2, 2, 3)
-        mm2(2, 2)
-        evac(2, 1, "scalar")
-        scatter(2, 1)
-        cast_w2(3, 0, 1, "scalar")
-        relu(3)
-        square(3)
-        quant_w2(3, 0, 1)
+        for e in range(E - 1):
+            n = e + 1
+            quant_h(e)
+            for b in range(NB if e < 2 else 2):
+                mm2(e, b)
+            if e == 0:
+                cast_w1_half(n, 0, 0, "scalar")
+                cast_w1_half(n, 0, 1, "vector")
+            prepare(n, 0, 0)
+            prepare(n, 0, 1)
+            early = (0, 0) if e == 0 else (e - 1, 2)
+            evac(early[0], early[1], "scalar")
+            scatter(early[0], early[1])
+            if e == 0:
+                cast_w1_half(n, 1, 0, "scalar")
+                cast_w1_half(n, 1, 1, "vector")
+            else:
+                cast_w1(n, 1, "scalar")
+            prepare(n, 1, 0)
+            prepare(n, 1, 1)
+            if e == 0:
+                evac(e, 1, "scalar")
+                scatter(e, 1)
+                cast_w2(n, 2, 3, "scalar")
+                cast_w2(n, 0, 2, "scalar")
+            elif e == 1:
+                for b in range(2):
+                    evac(e, b, "scalar")
+                    scatter(e, b)
+                cast_w2(n, 0, 2, "scalar")
+            else:
+                evac(e, 0, "scalar")
+                scatter(e, 0)
+                cast_w2(e, 2, 3, "scalar")
+                quant_w2(e, 2, 3)
+                mm2(e, 2)
+                evac(e, 1, "scalar")
+                scatter(e, 1)
+                cast_w2(n, 0, 1, "scalar")
+            relu(n)
+            if n + 1 < E:
+                cast_w1(n + 1, 0, "vector")
+            square(n)
+            if e == 0:
+                quant_w2(n, 2, 3)
+            quant_w2(n, 0, 2 if e < 2 else 1)
         quant_h(3)
         mm2(3, 0)
         evac(2, 2, "scalar")

@@ -23,9 +23,13 @@ PASSES = K // K_PASS
 NB = N // P
 GROUP = 16
 RUN = E * C // P
+LINE = 4
+LAST = E - 1
 STREAM_BUFS = 20
 HELD_BUFS = 29
+WIDE_BUFS = 4
 RAW_BUFS = 6
+BANKS = 4
 
 
 def tile_moe_pkd_mlp_relu2_kernel(tc, x_words, x_scales, w1, w2, gate, offs, out):
@@ -33,7 +37,7 @@ def tile_moe_pkd_mlp_relu2_kernel(tc, x_words, x_scales, w1, w2, gate, offs, out
     with ExitStack() as ctx:
         keep = ctx.enter_context(tc.tile_pool(name="keep", bufs=1))
         ring = ctx.enter_context(tc.tile_pool(name="ring", bufs=STREAM_BUFS))
-        psum = ctx.enter_context(tc.psum_pool(name="psum", bufs=4))
+        psum = ctx.enter_context(tc.psum_pool(name="psum", bufs=BANKS))
 
         offsets = keep.tile([P, E * C // GROUP], U16, name="offsets")
         nc.sync.dma_start(offsets[:], offs)
@@ -44,16 +48,11 @@ def tile_moe_pkd_mlp_relu2_kernel(tc, x_words, x_scales, w1, w2, gate, offs, out
         def held(shape, dtype):
             return ring.tile(shape, dtype, name="held", align_bytes=64, bufs=HELD_BUFS)
 
-        def single(name):
-            return lambda shape, dtype: ring.tile(shape, dtype, name=name, align_bytes=64, bufs=1)
-
-        relay = [single("relay%d" % i) for i in range(2)]
-
         def wide(shape, dtype):
-            return ring.tile(shape, dtype, name="wide", align_bytes=64, bufs=4)
+            return ring.tile(shape, dtype, name="wide", align_bytes=64, bufs=WIDE_BUFS)
 
-        def slots(s0, s1):
-            return offsets[:, s0 // GROUP : s1 // GROUP]
+        def slots(e0, e1):
+            return offsets[:, e0 * C // GROUP : e1 * C // GROUP]
 
         xs_win = keep.tile([P, T], U8, name="xs_win", align_bytes=64)
         nc.gpsimd.memset(xs_win[:].bitcast(I32), 0)
@@ -68,8 +67,6 @@ def tile_moe_pkd_mlp_relu2_kernel(tc, x_words, x_scales, w1, w2, gate, offs, out
         xw_win = [keep.tile([P, T], I32, name="xw_win%d" % g, align_bytes=64) for g in range(PASSES)]
         raw1 = {}
         raw2 = {}
-        raw2_first = {}
-        gates = {}
 
         def load_x(g):
             nc.sync.dma_start(out=xw_win[g][:], in_=x_words[g].rearrange("p t r -> p (t r)").bitcast(I32))
@@ -79,53 +76,45 @@ def tile_moe_pkd_mlp_relu2_kernel(tc, x_words, x_scales, w1, w2, gate, offs, out
             raw1[e, g] = ring.tile([P, PACK, H], F32, name="raw1", bufs=RAW_BUFS)
             nc.sync.dma_start(out=raw1[e, g][:], in_=rows)
 
-        def load_w2(e, b0, b1):
-            raw2[e, b0] = keep.tile([P, PACK, (b1 - b0) * P], F32, name="raw2_%d_%d" % (e, b0))
-            rows = w2[e].rearrange("(p j) c -> p j c", j=PACK)
-            nc.sync.dma_start(out=raw2[e, b0][:], in_=rows[:, :, b0 * P : b1 * P])
-            for b in range(b0, b1):
-                raw2[e, b] = raw2[e, b0]
-                raw2_first[e, b] = b0
+        def load_w2(e):
+            raw2[e] = keep.tile([P, PACK, N], F32, name="raw2_%d" % e)
+            nc.sync.dma_start(out=raw2[e][:], in_=w2[e].rearrange("(p j) c -> p j c", j=PACK))
 
-        gate_rows = keep.tile([P, RUN], F32, name="gate_rows")
-        gate_all = keep.tile([P, E * C], F32, name="gate_all")
+        gate_row = keep.tile([P, RUN], F32, name="gate_row")
+        gates = keep.tile([P, E * C], F32, name="gates")
         identity = keep.tile([P, P], F32, name="identity")
         make_identity(nc, identity[:])
 
         def load_gate():
-            nc.sync.dma_start(out=gate_rows[:], in_=gate[0].rearrange("(p j) -> p j", j=RUN))
+            nc.sync.dma_start(out=gate_row[:], in_=gate[0].rearrange("(p j) -> p j", j=RUN))
 
         def spread_gate():
-            for j0 in range(0, RUN, PACK):
-                bank = psum.tile([P, PACK, P], F32, name="acc2")
-                for j in range(PACK):
-                    column = gate_rows[:, j0 + j : j0 + j + 1].to_broadcast([P, P])
+            for j0 in range(0, RUN, LINE):
+                bank = psum.tile([P, LINE, P], F32, name="acc2")
+                for j in range(LINE):
+                    column = gate_row[:, j0 + j : j0 + j + 1].to_broadcast([P, P])
                     nc.tensor.transpose(bank[:, j, :], column, identity[:])
-                dst = gate_all[:].rearrange("p (n j) -> p n j", j=RUN)[:, :, j0 : j0 + PACK]
+                dst = gates[:].rearrange("p (n j) -> p n j", j=RUN)[:, :, j0 : j0 + LINE]
                 nc.scalar.activation(out=dst, in_=bank[:].rearrange("p j n -> p n j"), func=ACT.Copy)
-            for e in range(E):
-                gates[e] = gate_all[:, e * C : (e + 1) * C]
 
         xw = {}
         xs = {}
 
         def gather_scales(e0, e1):
             tile = keep.tile([P, (e1 - e0) * C], U8, name="xs%d" % e0, align_bytes=64)
-            nc.vector.tensor_copy(tile[:], xs_win[:].indirect(slots(e0 * C, e1 * C)))
+            nc.vector.tensor_copy(tile[:], xs_win[:].indirect(slots(e0, e1)))
             for e in range(e0, e1):
                 xs[e] = tile[:, (e - e0) * C : (e - e0 + 1) * C]
 
         def gather_words(e0, e1, g, place):
             tile = place([P, (e1 - e0) * C], U32)
-            nc.vector.tensor_copy(tile[:], xw_win[g][:].bitcast(U32).indirect(slots(e0 * C, e1 * C)))
+            nc.vector.tensor_copy(tile[:], xw_win[g][:].bitcast(U32).indirect(slots(e0, e1)))
             for e in range(e0, e1):
                 xw[e, g] = tile[:, (e - e0) * C : (e - e0 + 1) * C]
 
         def cast(engine, dst, src):
             if engine == "vector":
                 nc.vector.tensor_copy(out=dst, in_=src)
-            elif engine == "gpsimd":
-                nc.gpsimd.tensor_scalar(out=dst, in0=src, scalar1=1.0, scalar2=0.0, op0=ALU.mult, op1=ALU.add)
             else:
                 nc.scalar.activation(out=dst, in_=src, func=ACT.Copy)
 
@@ -147,24 +136,34 @@ def tile_moe_pkd_mlp_relu2_kernel(tc, x_words, x_scales, w1, w2, gate, offs, out
             src = raw1[e, g][:].rearrange("p j (m u t) -> p u m j t", u=2, t=2)
             cast(engine, dst, src[:, u])
 
-        def quant_w1(e, g, u, place=held):
+        acc1 = {}
+
+        def first_product(e, g, u, place=held):
             w1c[e, g, u] = place([P, 2 * P], U32)
             w1s[e, g, u] = stream([P, 2 * P], U8)
             nc.vector.quantize_mx(out=w1c[e, g, u][:].bitcast(FP8X4), scales=w1s[e, g, u][:], in_=w1b[e, g, u])
+            opens = (e, 2 * u) not in acc1
+            for t in range(2):
+                if opens:
+                    acc1[e, 2 * u + t] = psum.tile([P, C], F32, name="acc1")
+                nc.tensor.matmul_mx(
+                    out=acc1[e, 2 * u + t][:],
+                    lhsT=w1c[e, g, u][:, t * P : (t + 1) * P].bitcast(FP8X4),
+                    lhsT_scale=w1s[e, g, u][:, t * P : (t + 1) * P],
+                    rhs=xw[e, g].bitcast(FP8X4),
+                    rhs_scale=xs[e][4 * g : P, :],
+                    start=opens,
+                    stop=not opens,
+                )
 
         w2b = {}
         w2c = {}
         w2s = {}
 
-        def cast_w2(e, b0, b1, engine, place=stream):
-            w2b[e, b0] = place([P, (b1 - b0) * P * PACK], BF16)
-            raw = raw2[e, b0][:, :, (b0 - raw2_first[e, b0]) * P : (b1 - raw2_first[e, b0]) * P]
-            if engine == "gpsimd":
-                dst = w2b[e, b0][:].rearrange("p (c j) -> p c j", j=PACK)
-                src = raw.rearrange("p j c -> p c j")
-            else:
-                dst = w2b[e, b0][:].rearrange("p (c i j) -> p c j i", i=4, j=PACK)
-                src = raw.rearrange("p j (c i) -> p c j i", i=4)
+        def cast_w2(e, b0, b1, engine):
+            w2b[e, b0] = stream([P, (b1 - b0) * P * PACK], BF16)
+            dst = w2b[e, b0][:].rearrange("p (c i j) -> p c j i", i=LINE, j=PACK)
+            src = raw2[e][:, :, b0 * P : b1 * P].rearrange("p j (c i) -> p c j i", i=LINE)
             cast(engine, dst, src)
 
         def quant_w2(e, b0, b1):
@@ -175,27 +174,10 @@ def tile_moe_pkd_mlp_relu2_kernel(tc, x_words, x_scales, w1, w2, gate, offs, out
                 w2c[e, b] = codes[:, (b - b0) * P : (b - b0 + 1) * P]
                 w2s[e, b] = scales[:, (b - b0) * P : (b - b0 + 1) * P]
 
-        acc1 = {}
+        relus = {}
         hb = {}
         hc = {}
         hs = {}
-
-        def mm1(e, g, u):
-            first = (e, 2 * u) not in acc1
-            for t in range(2):
-                if first:
-                    acc1[e, 2 * u + t] = psum.tile([P, C], F32, name="acc1")
-                nc.tensor.matmul_mx(
-                    out=acc1[e, 2 * u + t][:],
-                    lhsT=w1c[e, g, u][:, t * P : (t + 1) * P].bitcast(FP8X4),
-                    lhsT_scale=w1s[e, g, u][:, t * P : (t + 1) * P],
-                    rhs=xw[e, g].bitcast(FP8X4),
-                    rhs_scale=xs[e][4 * g : P, :],
-                    start=first,
-                    stop=not first,
-                )
-
-        relus = {}
 
         def relu(e):
             relus[e] = stream([P, PACK, C], F32)
@@ -205,8 +187,8 @@ def tile_moe_pkd_mlp_relu2_kernel(tc, x_words, x_scales, w1, w2, gate, offs, out
         def square(e):
             hb[e] = stream([P, C * PACK], BF16)
             nc.scalar.activation(
-                out=hb[e][:].rearrange("p (c i t) -> p c t i", i=4, t=PACK),
-                in_=relus[e][:].rearrange("p t (c i) -> p c t i", i=4),
+                out=hb[e][:].rearrange("p (c i t) -> p c t i", i=LINE, t=PACK),
+                in_=relus[e][:].rearrange("p t (c i) -> p c t i", i=LINE),
                 func=ACT.Square,
             )
 
@@ -218,7 +200,7 @@ def tile_moe_pkd_mlp_relu2_kernel(tc, x_words, x_scales, w1, w2, gate, offs, out
         acc2 = {}
         ys = {}
 
-        def mm2(e, b):
+        def second_product(e, b):
             acc2[e, b] = psum.tile([P, C], F32, name="acc2")
             nc.tensor.matmul_mx(
                 out=acc2[e, b][:],
@@ -230,127 +212,118 @@ def tile_moe_pkd_mlp_relu2_kernel(tc, x_words, x_scales, w1, w2, gate, offs, out
                 stop=True,
             )
 
-        gated = {}
-
-        def evac(e, b, engine):
+        def evacuate(e, b):
             ys[e, b] = stream([P, C], F32)
-            gated[e, b] = engine == "vector"
-            if engine == "vector":
-                nc.vector.tensor_tensor(ys[e, b][:], acc2[e, b][:], gates[e], ALU.mult)
-            else:
-                nc.scalar.activation(out=ys[e, b][:], in_=acc2[e, b][:], func=ACT.Copy)
-
-        def gating(e, b, place=stream):
-            plain = ys[e, b]
-            ys[e, b] = place([P, C], F32)
-            gated[e, b] = True
-            nc.gpsimd.tensor_tensor(ys[e, b][:], plain[:], gates[e], ALU.mult)
+            nc.scalar.activation(out=ys[e, b][:], in_=acc2[e, b][:], func=ACT.Copy)
 
         windows = [keep.tile([P, T], F32, name="window%d" % b) for b in range(NB)]
 
         def scatter(e, b):
-            dst = windows[b][:].indirect(slots(e * C, (e + 1) * C))
-            if gated[e, b]:
-                nc.vector.tensor_copy(dst, ys[e, b][:])
-            else:
-                nc.vector.tensor_tensor(dst, ys[e, b][:], gates[e], ALU.mult)
+            dst = windows[b][:].indirect(slots(e, e + 1))
+            nc.vector.tensor_tensor(dst, ys[e, b][:], gates[:, e * C : (e + 1) * C], ALU.mult)
 
-        def store(b):
-            nc.sync.dma_start(out=out[b * P : (b + 1) * P, :], in_=windows[b][:])
+        def deliver(e, b):
+            evacuate(e, b)
+            scatter(e, b)
 
-        load_gate()
         load_x(0)
         load_scales()
+        load_gate()
         load_w1(0, 0)
         load_w1(0, 1)
         load_x(1)
         for e in range(E):
-            load_w2(e, 0, 3)
-            if e + 1 < E:
+            load_w2(e)
+            if e < LAST:
                 load_w1(e + 1, 0)
                 load_w1(e + 1, 1)
 
-        def prepare(e, g, u, place=held):
-            quant_w1(e, g, u, place)
-            mm1(e, g, u)
-
         spread_gate()
-        gather_words(0, 2, 0, wide)
-        gather_words(2, 4, 0, wide)
-        gather_scales(0, 2)
-        gather_scales(2, 4)
+        gather_words(0, E // 2, 0, wide)
+        gather_words(E // 2, E, 0, wide)
+        gather_scales(0, E // 2)
+        gather_scales(E // 2, E)
         cast_w1(0, 0, "scalar")
         cast_w1_half(0, 1, 0, "vector")
         cast_w1_half(0, 1, 1, "scalar")
-        prepare(0, 0, 0)
-        prepare(0, 0, 1)
+        first_product(0, 0, 0)
+        first_product(0, 0, 1)
         gather_words(0, 1, 1, held)
-        prepare(0, 1, 0)
-        prepare(0, 1, 1, wide)
+        first_product(0, 1, 0)
+        first_product(0, 1, 1, wide)
         gather_words(1, E, 1, wide)
         relu(0)
         cast_w2(0, 0, 2, "vector")
-        cast_w2(0, 2, 3, "vector")
+        cast_w2(0, 2, NB, "vector")
         square(0)
         quant_w2(0, 0, 2)
-        quant_w2(0, 2, 3)
-        for e in range(E - 1):
-            n = e + 1
-            quant_h(e)
-            for b in range(NB if e < 2 else 2):
-                mm2(e, b)
-            if e == 0:
-                cast_w1_half(n, 0, 0, "scalar")
-                cast_w1_half(n, 0, 1, "vector")
-            prepare(n, 0, 0)
-            prepare(n, 0, 1)
-            early = (0, 0) if e == 0 else (e - 1, 2)
-            evac(early[0], early[1], "scalar")
-            scatter(early[0], early[1])
-            if e == 0:
-                cast_w1_half(n, 1, 0, "scalar")
-                cast_w1_half(n, 1, 1, "vector")
-            else:
-                cast_w1(n, 1, "scalar")
-            prepare(n, 1, 0)
-            prepare(n, 1, 1)
-            if e == 0:
-                evac(e, 1, "scalar")
-                scatter(e, 1)
-                cast_w2(n, 2, 3, "scalar")
-                cast_w2(n, 0, 2, "scalar")
-            elif e == 1:
-                for b in range(2):
-                    evac(e, b, "scalar")
-                    scatter(e, b)
-                cast_w2(n, 0, 2, "scalar")
-            else:
-                evac(e, 0, "scalar")
-                scatter(e, 0)
-                cast_w2(e, 2, 3, "scalar")
-                quant_w2(e, 2, 3)
-                mm2(e, 2)
-                evac(e, 1, "scalar")
-                scatter(e, 1)
-                cast_w2(n, 0, 1, "scalar")
-            relu(n)
-            if n + 1 < E:
-                cast_w1(n + 1, 0, "vector")
-            square(n)
-            if e == 0:
-                quant_w2(n, 2, 3)
-            quant_w2(n, 0, 2 if e < 2 else 1)
-        quant_h(3)
-        mm2(3, 0)
-        evac(2, 2, "scalar")
-        scatter(2, 2)
-        cast_w2(3, 1, 3, "scalar")
-        evac(3, 0, "scalar")
-        quant_w2(3, 1, 3)
-        mm2(3, 1)
-        mm2(3, 2)
+        quant_w2(0, 2, NB)
+
+
+        quant_h(0)
         for b in range(NB):
-            if b:
-                evac(3, b, "scalar")
-            scatter(3, b)
-            store(b)
+            second_product(0, b)
+        for g in range(PASSES):
+            cast_w1_half(1, g, 0, "scalar")
+            cast_w1_half(1, g, 1, "vector")
+            first_product(1, g, 0)
+            first_product(1, g, 1)
+            deliver(0, g)
+        cast_w2(1, 2, NB, "scalar")
+        cast_w2(1, 0, 2, "scalar")
+        relu(1)
+        cast_w1(2, 0, "vector")
+        square(1)
+        quant_w2(1, 2, NB)
+        quant_w2(1, 0, 2)
+
+        quant_h(1)
+        for b in range(NB):
+            second_product(1, b)
+        first_product(2, 0, 0)
+        first_product(2, 0, 1)
+        deliver(0, 2)
+        cast_w1(2, 1, "scalar")
+        first_product(2, 1, 0)
+        first_product(2, 1, 1)
+        deliver(1, 0)
+        deliver(1, 1)
+        cast_w2(2, 0, 2, "scalar")
+        relu(2)
+        cast_w1_half(LAST, 0, 0, "vector")
+        square(2)
+        quant_w2(2, 0, 2)
+
+        quant_h(2)
+        second_product(2, 0)
+        second_product(2, 1)
+        first_product(LAST, 0, 0)
+        deliver(1, 2)
+        cast_w1(LAST, 1, "scalar")
+        cast_w1_half(LAST, 0, 1, "scalar")
+        cast_w2(2, 2, NB, "vector")
+        first_product(LAST, 1, 0)
+        first_product(LAST, 1, 1)
+        first_product(LAST, 0, 1)
+        deliver(2, 0)
+        quant_w2(2, 2, NB)
+        second_product(2, 2)
+        deliver(2, 1)
+        cast_w2(LAST, 0, 1, "scalar")
+        relu(LAST)
+        square(LAST)
+        quant_w2(LAST, 0, 1)
+
+        quant_h(LAST)
+        second_product(LAST, 0)
+        deliver(2, 2)
+        cast_w2(LAST, 1, NB, "scalar")
+        evacuate(LAST, 0)
+        quant_w2(LAST, 1, NB)
+        second_product(LAST, 1)
+        second_product(LAST, 2)
+        for b in range(NB):
+            if b > 0:
+                evacuate(LAST, b)
+            scatter(LAST, b)
+            nc.sync.dma_start(out=out[b * P : (b + 1) * P, :], in_=windows[b][:])

@@ -95,7 +95,7 @@ def tile_moe_pkd_mlp_relu2_kernel(tc, x_words, x_scales, w1, w2, gate, offs, out
                     column = gate_row[:, j0 + j : j0 + j + 1].to_broadcast([P, P])
                     nc.tensor.transpose(bank[:, j, :], column, identity[:])
                 dst = gates[:].rearrange("p (n j) -> p n j", j=RUN)[:, :, j0 : j0 + LINE]
-                nc.scalar.activation(out=dst, in_=bank[:].rearrange("p j n -> p n j"), func=ACT.Copy)
+                nc.scalar.copy(out=dst, in_=bank[:].rearrange("p j n -> p n j"))
 
         xw = {}
         xs = {}
@@ -116,7 +116,7 @@ def tile_moe_pkd_mlp_relu2_kernel(tc, x_words, x_scales, w1, w2, gate, offs, out
             if engine == "vector":
                 nc.vector.tensor_copy(out=dst, in_=src)
             else:
-                nc.scalar.activation(out=dst, in_=src, func=ACT.Copy)
+                nc.scalar.copy(out=dst, in_=src)
 
         w1b = {}
         w1c = {}
@@ -214,7 +214,7 @@ def tile_moe_pkd_mlp_relu2_kernel(tc, x_words, x_scales, w1, w2, gate, offs, out
 
         def evacuate(e, b):
             ys[e, b] = stream([P, C], F32)
-            nc.scalar.activation(out=ys[e, b][:], in_=acc2[e, b][:], func=ACT.Copy)
+            nc.scalar.copy(out=ys[e, b][:], in_=acc2[e, b][:])
 
         windows = [keep.tile([P, T], F32, name="window%d" % b) for b in range(NB)]
 

@@ -24,6 +24,7 @@ NB = N // P
 GROUP = 16
 RUN = E * C // P
 LINE = 4
+PAIR = 2
 LAST = E - 1
 STREAM_BUFS = 20
 HELD_BUFS = 29
@@ -162,8 +163,8 @@ def tile_moe_pkd_mlp_relu2_kernel(tc, x_words, x_scales, w1, w2, gate, offs, out
 
         def cast_w2(e, b0, b1, engine):
             w2b[e, b0] = stream([P, (b1 - b0) * P * PACK], BF16)
-            dst = w2b[e, b0][:].rearrange("p (c i j) -> p c j i", i=LINE, j=PACK)
-            src = raw2[e][:, :, b0 * P : b1 * P].rearrange("p j (c i) -> p c j i", i=LINE)
+            dst = w2b[e, b0][:].rearrange("p (c i j) -> p c j i", i=PAIR, j=PACK)
+            src = raw2[e][:, :, b0 * P : b1 * P].rearrange("p j (c i) -> p c j i", i=PAIR)
             cast(engine, dst, src)
 
         def quant_w2(e, b0, b1):
@@ -187,8 +188,8 @@ def tile_moe_pkd_mlp_relu2_kernel(tc, x_words, x_scales, w1, w2, gate, offs, out
         def square(e):
             hb[e] = stream([P, C * PACK], BF16)
             nc.scalar.activation(
-                out=hb[e][:].rearrange("p (c i t) -> p c t i", i=LINE, t=PACK),
-                in_=relus[e][:].rearrange("p t (c i) -> p c t i", i=LINE),
+                out=hb[e][:].rearrange("p (c i t) -> p c t i", i=PAIR, t=PACK),
+                in_=relus[e][:].rearrange("p t (c i) -> p c t i", i=PAIR),
                 func=ACT.Square,
             )
 

@@ -26,10 +26,10 @@ RUN = E * C // P
 LINE = 4
 PAIR = 2
 LAST = E - 1
-STREAM_BUFS = 20
+STREAM_BUFS = 28
 HELD_BUFS = 29
-WIDE_BUFS = 4
-RAW_BUFS = 6
+WIDE_BUFS = 8
+RAW_BUFS = 5
 BANKS = 4
 
 
@@ -101,8 +101,8 @@ def tile_moe_pkd_mlp_relu2_kernel(tc, x_words, x_scales, w1, w2, gate, offs, out
         xw = {}
         xs = {}
 
-        def gather_scales(e0, e1):
-            tile = keep.tile([P, (e1 - e0) * C], U8, name="xs%d" % e0, align_bytes=64)
+        def gather_scales(e0, e1, place):
+            tile = place([P, (e1 - e0) * C], U8)
             nc.vector.tensor_copy(tile[:], xs_win[:].indirect(slots(e0, e1)))
             for e in range(e0, e1):
                 xs[e] = tile[:, (e - e0) * C : (e - e0 + 1) * C]
@@ -123,14 +123,6 @@ def tile_moe_pkd_mlp_relu2_kernel(tc, x_words, x_scales, w1, w2, gate, offs, out
         w1c = {}
         w1s = {}
 
-        def cast_w1(e, g, engine):
-            tile = stream([P, H * PACK], BF16)
-            dst = tile[:].rearrange("p (t m j) -> p m j t", t=PACK, j=PACK)
-            src = raw1[e, g][:].rearrange("p j (m t) -> p m j t", t=PACK)
-            cast(engine, dst, src)
-            for u in range(2):
-                w1b[e, g, u] = tile[:, u * 2 * H : (u + 1) * 2 * H]
-
         def cast_w1_half(e, g, u, engine):
             w1b[e, g, u] = stream([P, 2 * H], BF16)[:]
             dst = w1b[e, g, u].rearrange("p (t m j) -> p m j t", t=2, j=PACK)
@@ -139,36 +131,42 @@ def tile_moe_pkd_mlp_relu2_kernel(tc, x_words, x_scales, w1, w2, gate, offs, out
 
         acc1 = {}
 
-        def first_product(e, g, u, place=held):
-            w1c[e, g, u] = place([P, 2 * P], U32)
+        def quant_w1(e, g, u):
+            w1c[e, g, u] = held([P, 2 * P], U32)
             w1s[e, g, u] = stream([P, 2 * P], U8)
             nc.vector.quantize_mx(out=w1c[e, g, u][:].bitcast(FP8X4), scales=w1s[e, g, u][:], in_=w1b[e, g, u])
-            opens = (e, 2 * u) not in acc1
+
+        def first_product(e, g, u):
+            quant_w1(e, g, u)
+            multiply_w1(e, g, u)
+
+        def multiply_w1(e, g, u):
+            opens = (e, u) not in acc1
+            if opens:
+                acc1[e, u] = psum.tile([P, 2, C], F32, name="acc1")
             for t in range(2):
-                if opens:
-                    acc1[e, 2 * u + t] = psum.tile([P, C], F32, name="acc1")
                 nc.tensor.matmul_mx(
-                    out=acc1[e, 2 * u + t][:],
+                    out=acc1[e, u][:, t, :],
                     lhsT=w1c[e, g, u][:, t * P : (t + 1) * P].bitcast(FP8X4),
                     lhsT_scale=w1s[e, g, u][:, t * P : (t + 1) * P],
                     rhs=xw[e, g].bitcast(FP8X4),
                     rhs_scale=xs[e][4 * g : P, :],
-                    start=opens,
-                    stop=not opens,
+                    start=opens and t == 0,
+                    stop=(not opens) and t == 1,
                 )
 
         w2b = {}
         w2c = {}
         w2s = {}
 
-        def cast_w2(e, b0, b1, engine):
-            w2b[e, b0] = stream([P, (b1 - b0) * P * PACK], BF16)
+        def cast_w2(e, b0, b1, engine, place=stream):
+            w2b[e, b0] = place([P, (b1 - b0) * P * PACK], BF16)
             dst = w2b[e, b0][:].rearrange("p (c i j) -> p c j i", i=PAIR, j=PACK)
             src = raw2[e][:, :, b0 * P : b1 * P].rearrange("p j (c i) -> p c j i", i=PAIR)
             cast(engine, dst, src)
 
         def quant_w2(e, b0, b1):
-            codes = held([P, (b1 - b0) * P], U32)
+            codes = keep.tile([P, (b1 - b0) * P], U32, name="w2c%d_%d" % (e, b0), align_bytes=64)
             scales = stream([P, (b1 - b0) * P], U8)
             nc.vector.quantize_mx(out=codes[:].bitcast(FP8X4), scales=scales[:], in_=w2b[e, b0][:])
             for b in range(b0, b1):
@@ -180,18 +178,20 @@ def tile_moe_pkd_mlp_relu2_kernel(tc, x_words, x_scales, w1, w2, gate, offs, out
         hc = {}
         hs = {}
 
-        def relu(e):
-            relus[e] = stream([P, PACK, C], F32)
-            for t in range(PACK):
-                nc.scalar.activation(out=relus[e][:, t, :], in_=acc1[e, t][:], func=ACT.Relu)
-
-        def square(e):
+        def relu_square(e):
+            for h in range(2):
+                relus[e, h] = stream([P, PACK, C // 2], F32)
+                for u in range(2):
+                    src = acc1[e, u][:, :, h * C // 2 : (h + 1) * C // 2]
+                    nc.scalar.activation(out=relus[e, h][:, 2 * u : 2 * u + 2, :], in_=src, func=ACT.Relu)
             hb[e] = stream([P, C * PACK], BF16)
-            nc.scalar.activation(
-                out=hb[e][:].rearrange("p (c i t) -> p c t i", i=PAIR, t=PACK),
-                in_=relus[e][:].rearrange("p t (c i) -> p c t i", i=PAIR),
-                func=ACT.Square,
-            )
+            for h in range(2):
+                dst = hb[e][:, h * C * PACK // 2 : (h + 1) * C * PACK // 2]
+                nc.scalar.activation(
+                    out=dst.rearrange("p (c i t) -> p c t i", i=PAIR, t=PACK),
+                    in_=relus[e, h][:].rearrange("p t (c i) -> p c t i", i=PAIR),
+                    func=ACT.Square,
+                )
 
         def quant_h(e):
             hc[e] = held([P, C], U32)
@@ -223,9 +223,31 @@ def tile_moe_pkd_mlp_relu2_kernel(tc, x_words, x_scales, w1, w2, gate, offs, out
             dst = windows[b][:].indirect(slots(e, e + 1))
             nc.vector.tensor_tensor(dst, ys[e, b][:], gates[:, e * C : (e + 1) * C], ALU.mult)
 
+        def weigh(e, b):
+            ys[e, b] = stream([P, C], F32)
+            nc.vector.tensor_tensor(ys[e, b][:], acc2[e, b][:], gates[:, e * C : (e + 1) * C], ALU.mult)
+
+        def scatter_copy(e, b):
+            nc.scalar.activation(windows[b][:].indirect(slots(e, e + 1)), ys[e, b][:], ACT.Copy)
+
         def deliver(e, b):
-            evacuate(e, b)
-            scatter(e, b)
+            weigh(e, b)
+            scatter_copy(e, b)
+
+        def cast_halves(e, g):
+            for u in range(2):
+                cast_w1_half(e, g, u, "vector")
+
+        def first_products(e, g):
+            for u in range(2):
+                first_product(e, g, u)
+
+        def store(b):
+            nc.sync.dma_start(out=out[b * P : (b + 1) * P, :], in_=windows[b][:])
+
+        def second_products(e):
+            for b in range(NB):
+                second_product(e, b)
 
         load_x(0)
         load_scales()
@@ -233,98 +255,90 @@ def tile_moe_pkd_mlp_relu2_kernel(tc, x_words, x_scales, w1, w2, gate, offs, out
         load_w1(0, 0)
         load_w1(0, 1)
         load_x(1)
-        for e in range(E):
-            load_w2(e)
-            if e < LAST:
-                load_w1(e + 1, 0)
-                load_w1(e + 1, 1)
+        load_w2(0)
+        load_w1(1, 0)
+        load_w1(1, 1)
+        load_w2(1)
+        for e in range(2, E):
+            load_w1(e, 0)
+            load_w1(e, 1)
+        load_w2(2)
+        load_w2(LAST)
 
         spread_gate()
         gather_words(0, E // 2, 0, wide)
         gather_words(E // 2, E, 0, wide)
-        gather_scales(0, E // 2)
-        gather_scales(E // 2, E)
-        cast_w1(0, 0, "scalar")
+        gather_scales(0, E // 2, wide)
+        gather_scales(E // 2, E, wide)
+        cast_w1_half(0, 0, 0, "scalar")
+        cast_w1_half(0, 0, 1, "scalar")
+        first_product(0, 0, 0)
         cast_w1_half(0, 1, 0, "vector")
         cast_w1_half(0, 1, 1, "scalar")
-        first_product(0, 0, 0)
         first_product(0, 0, 1)
+        quant_w1(0, 1, 0)
         gather_words(0, 1, 1, held)
-        first_product(0, 1, 0)
-        first_product(0, 1, 1, wide)
-        gather_words(1, E, 1, wide)
-        relu(0)
-        cast_w2(0, 0, 2, "vector")
-        cast_w2(0, 2, NB, "vector")
-        square(0)
-        quant_w2(0, 0, 2)
-        quant_w2(0, 2, NB)
-
-
+        multiply_w1(0, 1, 0)
+        first_product(0, 1, 1)
+        gather_words(1, 2, 1, held)
+        relu_square(0)
+        cast_w2(0, 0, NB, "vector", wide)
+        gather_words(2, LAST, 1, wide)
+        quant_w2(0, 0, NB)
         quant_h(0)
-        for b in range(NB):
-            second_product(0, b)
-        for g in range(PASSES):
-            cast_w1_half(1, g, 0, "scalar")
-            cast_w1_half(1, g, 1, "vector")
-            first_product(1, g, 0)
-            first_product(1, g, 1)
-            deliver(0, g)
-        cast_w2(1, 2, NB, "scalar")
-        cast_w2(1, 0, 2, "scalar")
-        relu(1)
-        cast_w1(2, 0, "vector")
-        square(1)
-        quant_w2(1, 2, NB)
-        quant_w2(1, 0, 2)
+        second_products(0)
 
-        quant_h(1)
-        for b in range(NB):
-            second_product(1, b)
-        first_product(2, 0, 0)
-        first_product(2, 0, 1)
+        cast_w1_half(1, 0, 0, "scalar")
+        cast_w1_half(1, 0, 1, "vector")
+        deliver(0, 0)
+        first_product(1, 0, 1)
+        first_product(1, 0, 0)
+        deliver(0, 1)
+        cast_halves(1, 1)
+        first_products(1, 1)
+        gather_words(LAST, E, 1, held)
+        cast_w2(1, 0, NB, "vector")
+        relu_square(1)
         deliver(0, 2)
-        cast_w1(2, 1, "scalar")
-        first_product(2, 1, 0)
-        first_product(2, 1, 1)
+        quant_w2(1, 0, NB)
+        cast_w1_half(2, 0, 0, "vector")
+        quant_h(1)
+        second_products(1)
+
+        cast_w1_half(2, 0, 1, "vector")
         deliver(1, 0)
+        first_products(2, 0)
         deliver(1, 1)
-        cast_w2(2, 0, 2, "scalar")
-        relu(2)
-        cast_w1_half(LAST, 0, 0, "vector")
-        square(2)
-        quant_w2(2, 0, 2)
-
-        quant_h(2)
-        second_product(2, 0)
-        second_product(2, 1)
-        first_product(LAST, 0, 0)
+        cast_halves(2, 1)
+        first_products(2, 1)
+        cast_halves(LAST, 0)
+        relu_square(2)
+        first_products(LAST, 0)
         deliver(1, 2)
-        cast_w1(LAST, 1, "scalar")
-        cast_w1_half(LAST, 0, 1, "scalar")
-        cast_w2(2, 2, NB, "vector")
-        first_product(LAST, 1, 0)
-        first_product(LAST, 1, 1)
-        first_product(LAST, 0, 1)
+        cast_halves(LAST, 1)
+        first_products(LAST, 1)
+        quant_h(2)
+        cast_w2(2, 0, 1, "vector")
+        cast_w2(2, 1, NB, "vector")
+        quant_w2(2, 0, 1)
+        quant_w2(2, 1, NB)
+        second_products(2)
+        relu_square(LAST)
         deliver(2, 0)
-        quant_w2(2, 2, NB)
-        second_product(2, 2)
-        deliver(2, 1)
-        cast_w2(LAST, 0, 1, "scalar")
-        relu(LAST)
-        square(LAST)
-        quant_w2(LAST, 0, 1)
-
+        cast_w2(LAST, 0, NB, "vector")
         quant_h(LAST)
-        second_product(LAST, 0)
-        deliver(2, 2)
-        cast_w2(LAST, 1, NB, "scalar")
+        quant_w2(LAST, 0, NB)
+        second_products(LAST)
+
         evacuate(LAST, 0)
-        quant_w2(LAST, 1, NB)
-        second_product(LAST, 1)
-        second_product(LAST, 2)
-        for b in range(NB):
-            if b > 0:
-                evacuate(LAST, b)
-            scatter(LAST, b)
-            nc.sync.dma_start(out=out[b * P : (b + 1) * P, :], in_=windows[b][:])
+        evacuate(LAST, 1)
+        deliver(2, 1)
+        weigh(2, 2)
+        scatter(LAST, 0)
+        store(0)
+        weigh(LAST, 2)
+        scatter_copy(2, 2)
+        scatter(LAST, 1)
+        store(1)
+        scatter_copy(LAST, 2)
+        store(2)

@@ -27,7 +27,7 @@ LINE = 4
 PAIR = 2
 LAST = E - 1
 STREAM_BUFS = 28
-HELD_BUFS = 29
+HELD_BUFS = 22
 WIDE_BUFS = 8
 RAW_BUFS = 5
 BANKS = 4
@@ -81,22 +81,33 @@ def tile_moe_pkd_mlp_relu2_kernel(tc, x_words, x_scales, w1, w2, gate, offs, out
             raw2[e] = keep.tile([P, PACK, N], F32, name="raw2_%d" % e)
             nc.sync.dma_start(out=raw2[e][:], in_=w2[e].rearrange("(p j) c -> p j c", j=PACK))
 
-        gate_row = keep.tile([P, RUN], F32, name="gate_row")
-        gates = keep.tile([P, E * C], F32, name="gates")
+        gate_row = keep.tile([P, 2, LINE], F32, name="gate_row")
         identity = keep.tile([P, P], F32, name="identity")
         make_identity(nc, identity[:])
+        gates = {}
 
         def load_gate():
-            nc.sync.dma_start(out=gate_row[:], in_=gate[0].rearrange("(p j) -> p j", j=RUN))
+            nc.sync.dma_start(out=gate_row[:], in_=gate[0].rearrange("(h p j) -> p h j", h=2, j=LINE))
+
+        def early(shape, dtype):
+            return ring.tile(shape, dtype, name="early", align_bytes=64, bufs=3)
+
+        turned = {}
+
+        def turn_gate():
+            for h in range(2):
+                turned[h] = psum.tile([P, LINE, P], F32, name="acc2")
+                for j in range(LINE):
+                    column = gate_row[:, h, j : j + 1].to_broadcast([P, P])
+                    nc.tensor.transpose(turned[h][:, j, :], column, identity[:])
 
         def spread_gate():
-            for j0 in range(0, RUN, LINE):
-                bank = psum.tile([P, LINE, P], F32, name="acc2")
-                for j in range(LINE):
-                    column = gate_row[:, j0 + j : j0 + j + 1].to_broadcast([P, P])
-                    nc.tensor.transpose(bank[:, j, :], column, identity[:])
-                dst = gates[:].rearrange("p (n j) -> p n j", j=RUN)[:, :, j0 : j0 + LINE]
-                nc.scalar.copy(out=dst, in_=bank[:].rearrange("p j n -> p n j"))
+            for h in range(2):
+                tile = early([P, 2 * C], F32)
+                dst = tile[:].rearrange("p (n j) -> p n j", j=LINE)
+                nc.scalar.copy(out=dst, in_=turned[h][:].rearrange("p j n -> p n j"))
+                for e in range(2):
+                    gates[2 * h + e] = tile[:, e * C : (e + 1) * C]
 
         xw = {}
         xs = {}
@@ -123,21 +134,21 @@ def tile_moe_pkd_mlp_relu2_kernel(tc, x_words, x_scales, w1, w2, gate, offs, out
         w1c = {}
         w1s = {}
 
-        def cast_w1_half(e, g, u, engine):
-            w1b[e, g, u] = stream([P, 2 * H], BF16)[:]
+        def cast_w1_half(e, g, u, engine, place=stream):
+            w1b[e, g, u] = place([P, 2 * H], BF16)[:]
             dst = w1b[e, g, u].rearrange("p (t m j) -> p m j t", t=2, j=PACK)
             src = raw1[e, g][:].rearrange("p j (m u t) -> p u m j t", u=2, t=2)
             cast(engine, dst, src[:, u])
 
         acc1 = {}
 
-        def quant_w1(e, g, u):
-            w1c[e, g, u] = held([P, 2 * P], U32)
+        def quant_w1(e, g, u, place=held):
+            w1c[e, g, u] = place([P, 2 * P], U32)
             w1s[e, g, u] = stream([P, 2 * P], U8)
             nc.vector.quantize_mx(out=w1c[e, g, u][:].bitcast(FP8X4), scales=w1s[e, g, u][:], in_=w1b[e, g, u])
 
-        def first_product(e, g, u):
-            quant_w1(e, g, u)
+        def first_product(e, g, u, place=held):
+            quant_w1(e, g, u, place)
             multiply_w1(e, g, u)
 
         def multiply_w1(e, g, u):
@@ -179,9 +190,10 @@ def tile_moe_pkd_mlp_relu2_kernel(tc, x_words, x_scales, w1, w2, gate, offs, out
         hs = {}
 
         def relu_square(e):
-            for h in range(2):
-                relus[e, h] = stream([P, PACK, C // 2], F32)
-                for u in range(2):
+            for u in range(2):
+                for h in range(2):
+                    if u == 0:
+                        relus[e, h] = stream([P, PACK, C // 2], F32)
                     src = acc1[e, u][:, :, h * C // 2 : (h + 1) * C // 2]
                     nc.scalar.activation(out=relus[e, h][:, 2 * u : 2 * u + 2, :], in_=src, func=ACT.Relu)
             hb[e] = stream([P, C * PACK], BF16)
@@ -213,26 +225,22 @@ def tile_moe_pkd_mlp_relu2_kernel(tc, x_words, x_scales, w1, w2, gate, offs, out
                 stop=True,
             )
 
-        def evacuate(e, b):
-            ys[e, b] = stream([P, C], F32)
-            nc.scalar.copy(out=ys[e, b][:], in_=acc2[e, b][:])
-
         windows = [keep.tile([P, T], F32, name="window%d" % b) for b in range(NB)]
-
-        def scatter(e, b):
-            dst = windows[b][:].indirect(slots(e, e + 1))
-            nc.vector.tensor_tensor(dst, ys[e, b][:], gates[:, e * C : (e + 1) * C], ALU.mult)
 
         def weigh(e, b):
             ys[e, b] = stream([P, C], F32)
-            nc.vector.tensor_tensor(ys[e, b][:], acc2[e, b][:], gates[:, e * C : (e + 1) * C], ALU.mult)
+            nc.vector.tensor_tensor(ys[e, b][:], acc2[e, b][:], gates[e], ALU.mult)
 
-        def scatter_copy(e, b):
-            nc.scalar.activation(windows[b][:].indirect(slots(e, e + 1)), ys[e, b][:], ACT.Copy)
+        def scatter(e, b, engine):
+            dst = windows[b][:].indirect(slots(e, e + 1))
+            if engine == "vector":
+                nc.vector.tensor_copy(dst, ys[e, b][:])
+            else:
+                nc.scalar.activation(dst, ys[e, b][:], ACT.Copy)
 
         def deliver(e, b):
             weigh(e, b)
-            scatter_copy(e, b)
+            scatter(e, b, "scalar")
 
         def cast_halves(e, g):
             for u in range(2):
@@ -265,7 +273,7 @@ def tile_moe_pkd_mlp_relu2_kernel(tc, x_words, x_scales, w1, w2, gate, offs, out
         load_w2(2)
         load_w2(LAST)
 
-        spread_gate()
+        turn_gate()
         gather_words(0, E // 2, 0, wide)
         gather_words(E // 2, E, 0, wide)
         gather_scales(0, E // 2, wide)
@@ -274,42 +282,45 @@ def tile_moe_pkd_mlp_relu2_kernel(tc, x_words, x_scales, w1, w2, gate, offs, out
         cast_w1_half(0, 0, 1, "scalar")
         first_product(0, 0, 0)
         cast_w1_half(0, 1, 0, "vector")
-        cast_w1_half(0, 1, 1, "scalar")
+        cast_w1_half(0, 1, 1, "scalar", early)
+        spread_gate()
         first_product(0, 0, 1)
         quant_w1(0, 1, 0)
         gather_words(0, 1, 1, held)
         multiply_w1(0, 1, 0)
-        first_product(0, 1, 1)
-        gather_words(1, 2, 1, held)
+        first_product(0, 1, 1, wide)
+        gather_words(1, 2, 1, wide)
         relu_square(0)
-        cast_w2(0, 0, NB, "vector", wide)
-        gather_words(2, LAST, 1, wide)
-        quant_w2(0, 0, NB)
+        cast_w2(0, 0, 2, "vector", wide)
+        gather_words(2, E, 1, wide)
+        quant_w2(0, 0, 2)
         quant_h(0)
-        second_products(0)
+        second_product(0, 0)
+        second_product(0, 1)
 
+        cast_w2(0, 2, NB, "scalar")
         cast_w1_half(1, 0, 0, "scalar")
         cast_w1_half(1, 0, 1, "vector")
         deliver(0, 0)
         first_product(1, 0, 1)
-        first_product(1, 0, 0)
+        quant_w2(0, 2, NB)
+        second_product(0, 2)
         deliver(0, 1)
+        first_product(1, 0, 0)
         cast_halves(1, 1)
         first_products(1, 1)
-        gather_words(LAST, E, 1, held)
         cast_w2(1, 0, NB, "vector")
         relu_square(1)
         deliver(0, 2)
         quant_w2(1, 0, NB)
-        cast_w1_half(2, 0, 0, "vector")
+        cast_halves(2, 0)
         quant_h(1)
         second_products(1)
 
-        cast_w1_half(2, 0, 1, "vector")
-        deliver(1, 0)
         first_products(2, 0)
-        deliver(1, 1)
+        deliver(1, 0)
         cast_halves(2, 1)
+        deliver(1, 1)
         first_products(2, 1)
         cast_halves(LAST, 0)
         relu_square(2)
@@ -324,21 +335,20 @@ def tile_moe_pkd_mlp_relu2_kernel(tc, x_words, x_scales, w1, w2, gate, offs, out
         quant_w2(2, 1, NB)
         second_products(2)
         relu_square(LAST)
-        deliver(2, 0)
         cast_w2(LAST, 0, NB, "vector")
-        quant_h(LAST)
+        deliver(2, 0)
         quant_w2(LAST, 0, NB)
+        quant_h(LAST)
         second_products(LAST)
 
-        evacuate(LAST, 0)
-        evacuate(LAST, 1)
         deliver(2, 1)
-        weigh(2, 2)
-        scatter(LAST, 0)
+        deliver(2, 2)
+        weigh(LAST, 0)
+        weigh(LAST, 1)
+        scatter(LAST, 0, "vector")
         store(0)
         weigh(LAST, 2)
-        scatter_copy(2, 2)
-        scatter(LAST, 1)
+        scatter(LAST, 1, "vector")
         store(1)
-        scatter_copy(LAST, 2)
+        scatter(LAST, 2, "scalar")
         store(2)

@@ -26,10 +26,10 @@ RUN = E * C // P
 LINE = 4
 PAIR = 2
 LAST = E - 1
-STREAM_BUFS = 28
-HELD_BUFS = 22
+STREAM_BUFS = 24
+HELD_BUFS = 18
 WIDE_BUFS = 8
-RAW_BUFS = 5
+RAW_BUFS = 4
 BANKS = 4
 
 
@@ -140,6 +140,25 @@ def tile_moe_pkd_mlp_relu2_kernel(tc, x_words, x_scales, w1, w2, gate, offs, out
             src = raw1[e, g][:].rearrange("p j (m u t) -> p u m j t", u=2, t=2)
             cast(engine, dst, src[:, u])
 
+        def cast_w1(e, g):
+            tile = stream([P, PACK * H], BF16)
+            dst = tile[:].rearrange("p (t m j) -> p m j t", t=PACK, j=PACK)
+            src = raw1[e, g][:].rearrange("p j (m t) -> p m j t", t=PACK)
+            nc.vector.tensor_copy(out=dst, in_=src)
+            whole[e, g] = tile
+            for u in range(2):
+                w1b[e, g, u] = tile[:, u * 2 * H : (u + 1) * 2 * H]
+
+        def first_pass(e):
+            codes = ring.tile([P, H], U32, name="codes", align_bytes=64, bufs=2)
+            scales = stream([P, H], U8)
+            nc.vector.quantize_mx(out=codes[:].bitcast(FP8X4), scales=scales[:], in_=whole[e, 0][:])
+            for u in range(2):
+                w1c[e, 0, u] = codes[:, u * 2 * P : (u + 1) * 2 * P]
+                w1s[e, 0, u] = scales[:, u * 2 * P : (u + 1) * 2 * P]
+                multiply_w1(e, 0, u)
+
+        whole = {}
         acc1 = {}
 
         def quant_w1(e, g, u, place=held):
@@ -172,8 +191,9 @@ def tile_moe_pkd_mlp_relu2_kernel(tc, x_words, x_scales, w1, w2, gate, offs, out
 
         def cast_w2(e, b0, b1, engine, place=stream):
             w2b[e, b0] = place([P, (b1 - b0) * P * PACK], BF16)
-            dst = w2b[e, b0][:].rearrange("p (c i j) -> p c j i", i=PAIR, j=PACK)
-            src = raw2[e][:, :, b0 * P : b1 * P].rearrange("p j (c i) -> p c j i", i=PAIR)
+            run = LINE if engine == "vector" else PAIR
+            dst = w2b[e, b0][:].rearrange("p (c i j) -> p c j i", i=run, j=PACK)
+            src = raw2[e][:, :, b0 * P : b1 * P].rearrange("p j (c i) -> p c j i", i=run)
             cast(engine, dst, src)
 
         def quant_w2(e, b0, b1):
@@ -242,10 +262,6 @@ def tile_moe_pkd_mlp_relu2_kernel(tc, x_words, x_scales, w1, w2, gate, offs, out
             weigh(e, b)
             scatter(e, b, "scalar")
 
-        def cast_halves(e, g):
-            for u in range(2):
-                cast_w1_half(e, g, u, "vector")
-
         def first_products(e, g):
             for u in range(2):
                 first_product(e, g, u)
@@ -303,30 +319,30 @@ def tile_moe_pkd_mlp_relu2_kernel(tc, x_words, x_scales, w1, w2, gate, offs, out
         cast_w1_half(1, 0, 1, "vector")
         deliver(0, 0)
         first_product(1, 0, 1)
-        quant_w2(0, 2, NB)
-        second_product(0, 2)
         deliver(0, 1)
         first_product(1, 0, 0)
-        cast_halves(1, 1)
+        cast_w1(1, 1)
+        quant_w2(0, 2, NB)
+        second_product(0, 2)
         first_products(1, 1)
         cast_w2(1, 0, NB, "vector")
         relu_square(1)
         deliver(0, 2)
         quant_w2(1, 0, NB)
-        cast_halves(2, 0)
+        cast_w1(2, 0)
         quant_h(1)
         second_products(1)
 
-        first_products(2, 0)
+        first_pass(2)
         deliver(1, 0)
-        cast_halves(2, 1)
+        cast_w1(2, 1)
         deliver(1, 1)
         first_products(2, 1)
-        cast_halves(LAST, 0)
+        cast_w1(LAST, 0)
         relu_square(2)
-        first_products(LAST, 0)
         deliver(1, 2)
-        cast_halves(LAST, 1)
+        first_pass(LAST)
+        cast_w1(LAST, 1)
         first_products(LAST, 1)
         quant_h(2)
         cast_w2(2, 0, 1, "vector")

@@ -23,6 +23,7 @@ PASSES = K // K_PASS
 NB = N // P
 GROUP = 16
 RUN = E * C // P
+BURST = 256
 LINE = 4
 PAIR = 2
 LAST = E - 1
@@ -55,7 +56,7 @@ def tile_moe_pkd_mlp_relu2_kernel(tc, x_words, x_scales, w1, w2, gate, offs, out
         def slots(e0, e1):
             return offsets[:, e0 * C // GROUP : e1 * C // GROUP]
 
-        xs_win = keep.tile([P, T], U8, name="xs_win", align_bytes=64)
+        xs_win = keep.tile([P, T], U8, name="xs_win", align_bytes=BURST)
         nc.gpsimd.memset(xs_win[:].bitcast(I32), 0)
 
         def load_scales():
@@ -65,7 +66,7 @@ def tile_moe_pkd_mlp_relu2_kernel(tc, x_words, x_scales, w1, w2, gate, offs, out
                     in_=x_scales[:, 4 * q : 4 * q + 4, :].bitcast(I32),
                 )
 
-        xw_win = [keep.tile([P, T], I32, name="xw_win%d" % g, align_bytes=64) for g in range(PASSES)]
+        xw_win = [keep.tile([P, T], I32, name="xw_win%d" % g, align_bytes=BURST) for g in range(PASSES)]
         raw1 = {}
         raw2 = {}
 
@@ -74,11 +75,11 @@ def tile_moe_pkd_mlp_relu2_kernel(tc, x_words, x_scales, w1, w2, gate, offs, out
 
         def load_w1(e, g):
             rows = w1[e, g * K_PASS : (g + 1) * K_PASS, :].rearrange("(p j) c -> p j c", j=PACK)
-            raw1[e, g] = ring.tile([P, PACK, H], F32, name="raw1", bufs=RAW_BUFS)
+            raw1[e, g] = ring.tile([P, PACK, H], F32, name="raw1", bufs=RAW_BUFS, align_bytes=BURST)
             nc.sync.dma_start(out=raw1[e, g][:], in_=rows)
 
         def load_w2(e):
-            raw2[e] = keep.tile([P, PACK, N], F32, name="raw2_%d" % e)
+            raw2[e] = keep.tile([P, PACK, N], F32, name="raw2_%d" % e, align_bytes=BURST)
             nc.sync.dma_start(out=raw2[e][:], in_=w2[e].rearrange("(p j) c -> p j c", j=PACK))
 
         gate_row = keep.tile([P, 2, LINE], F32, name="gate_row")
@@ -245,7 +246,7 @@ def tile_moe_pkd_mlp_relu2_kernel(tc, x_words, x_scales, w1, w2, gate, offs, out
                 stop=True,
             )
 
-        windows = [keep.tile([P, T], F32, name="window%d" % b) for b in range(NB)]
+        windows = [keep.tile([P, T], F32, name="window%d" % b, align_bytes=BURST) for b in range(NB)]
 
         def weigh(e, b):
             ys[e, b] = stream([P, C], F32)

@@ -28,7 +28,7 @@ LINE = 4
 PAIR = 2
 LAST = E - 1
 STREAM_BUFS = 24
-HELD_BUFS = 18
+HELD_BUFS = 20
 WIDE_BUFS = 8
 RAW_BUFS = 4
 BANKS = 4
@@ -42,7 +42,6 @@ def tile_moe_pkd_mlp_relu2_kernel(tc, x_words, x_scales, w1, w2, gate, offs, out
         psum = ctx.enter_context(tc.psum_pool(name="psum", bufs=BANKS))
 
         offsets = keep.tile([P, E * C // GROUP], U16, name="offsets")
-        nc.sync.dma_start(offsets[:], offs)
 
         def stream(shape, dtype):
             return ring.tile(shape, dtype, name="stream", align_bytes=64)
@@ -82,16 +81,16 @@ def tile_moe_pkd_mlp_relu2_kernel(tc, x_words, x_scales, w1, w2, gate, offs, out
             raw2[e] = keep.tile([P, PACK, N], F32, name="raw2_%d" % e, align_bytes=BURST)
             nc.sync.dma_start(out=raw2[e][:], in_=w2[e].rearrange("(p j) c -> p j c", j=PACK))
 
-        gate_row = keep.tile([P, 2, LINE], F32, name="gate_row")
+        gate_row = keep.tile([P, RUN], F32, name="gate_row")
         identity = keep.tile([P, P], F32, name="identity")
         make_identity(nc, identity[:])
         gates = {}
 
         def load_gate():
-            nc.sync.dma_start(out=gate_row[:], in_=gate[0].rearrange("(h p j) -> p h j", h=2, j=LINE))
+            nc.sync.dma_start(out=gate_row[:], in_=gate[0].rearrange("(p j) -> p j", j=RUN))
 
         def early(shape, dtype):
-            return ring.tile(shape, dtype, name="early", align_bytes=64, bufs=3)
+            return ring.tile(shape, dtype, name="early", align_bytes=64, bufs=2)
 
         turned = {}
 
@@ -99,16 +98,16 @@ def tile_moe_pkd_mlp_relu2_kernel(tc, x_words, x_scales, w1, w2, gate, offs, out
             for h in range(2):
                 turned[h] = psum.tile([P, LINE, P], F32, name="acc2")
                 for j in range(LINE):
-                    column = gate_row[:, h, j : j + 1].to_broadcast([P, P])
+                    column = gate_row[:, h * LINE + j : h * LINE + j + 1].to_broadcast([P, P])
                     nc.tensor.transpose(turned[h][:, j, :], column, identity[:])
 
         def spread_gate():
+            tile = early([P, E * C], F32)
             for h in range(2):
-                tile = early([P, 2 * C], F32)
-                dst = tile[:].rearrange("p (n j) -> p n j", j=LINE)
-                nc.scalar.copy(out=dst, in_=turned[h][:].rearrange("p j n -> p n j"))
-                for e in range(2):
-                    gates[2 * h + e] = tile[:, e * C : (e + 1) * C]
+                dst = tile[:].rearrange("p (n h j) -> p h n j", h=2, j=LINE)
+                nc.scalar.copy(out=dst[:, h], in_=turned[h][:].rearrange("p j n -> p n j"))
+            for e in range(E):
+                gates[e] = tile[:, e * C : (e + 1) * C]
 
         xw = {}
         xs = {}
@@ -231,8 +230,29 @@ def tile_moe_pkd_mlp_relu2_kernel(tc, x_words, x_scales, w1, w2, gate, offs, out
             hs[e] = stream([P, C], U8)
             nc.vector.quantize_mx(out=hc[e][:].bitcast(FP8X4), scales=hs[e][:], in_=hb[e][:])
 
+        def quant_h_half(e, h):
+            if h == 0:
+                hc[e] = held([P, C], U32)
+                hs[e] = stream([P, C], U8)
+            cols = slice(h * P, (h + 1) * P)
+            src = hb[e][:, h * P * PACK : (h + 1) * P * PACK]
+            nc.vector.quantize_mx(out=hc[e][:, cols].bitcast(FP8X4), scales=hs[e][:, cols], in_=src)
+
         acc2 = {}
         ys = {}
+
+        def first_block_half(e, h):
+            acc2[e, 0, h] = psum.tile([P, P], F32, name="acc2")
+            cols = slice(h * P, (h + 1) * P)
+            nc.tensor.matmul_mx(
+                out=acc2[e, 0, h][:],
+                lhsT=w2c[e, 0].bitcast(FP8X4),
+                lhsT_scale=w2s[e, 0],
+                rhs=hc[e][:, cols].bitcast(FP8X4),
+                rhs_scale=hs[e][:, cols],
+                start=True,
+                stop=True,
+            )
 
         def second_product(e, b):
             acc2[e, b] = psum.tile([P, C], F32, name="acc2")
@@ -263,6 +283,12 @@ def tile_moe_pkd_mlp_relu2_kernel(tc, x_words, x_scales, w1, w2, gate, offs, out
             weigh(e, b)
             scatter(e, b, "scalar")
 
+        def deliver_first_half(e, h):
+            y = stream([P, P], F32)
+            nc.vector.tensor_tensor(y[:], acc2[e, 0, h][:], gates[e][:, h * P : (h + 1) * P], ALU.mult)
+            first = (e * C + h * P) // GROUP
+            nc.scalar.activation(windows[0][:].indirect(offsets[:, first : first + P // GROUP]), y[:], ACT.Copy)
+
         def first_products(e, g):
             for u in range(2):
                 first_product(e, g, u)
@@ -275,6 +301,7 @@ def tile_moe_pkd_mlp_relu2_kernel(tc, x_words, x_scales, w1, w2, gate, offs, out
                 second_product(e, b)
 
         load_x(0)
+        nc.sync.dma_start(offsets[:], offs)
         load_scales()
         load_gate()
         load_w1(0, 0)
@@ -330,20 +357,30 @@ def tile_moe_pkd_mlp_relu2_kernel(tc, x_words, x_scales, w1, w2, gate, offs, out
         relu_square(1)
         deliver(0, 2)
         quant_w2(1, 0, NB)
-        cast_w1(2, 0)
-        quant_h(1)
-        second_products(1)
+        cast_w1_half(2, 0, 0, "vector")
+        quant_h_half(1, 0)
+        first_block_half(1, 0)
+        cast_w1_half(2, 0, 1, "vector")
+        quant_h_half(1, 1)
+        second_product(1, 1)
+        first_block_half(1, 1)
+        second_product(1, 2)
 
-        first_pass(2)
-        deliver(1, 0)
-        cast_w1(2, 1)
+        deliver_first_half(1, 0)
+        quant_w1(2, 0, 0)
+        quant_w1(2, 0, 1)
         deliver(1, 1)
+        multiply_w1(2, 0, 0)
+        multiply_w1(2, 0, 1)
+        cast_w1(2, 1)
+        deliver_first_half(1, 1)
         first_products(2, 1)
         cast_w1(LAST, 0)
         relu_square(2)
         deliver(1, 2)
         first_pass(LAST)
-        cast_w1(LAST, 1)
+        cast_w1_half(LAST, 1, 0, "vector")
+        cast_w1_half(LAST, 1, 1, "vector")
         first_products(LAST, 1)
         quant_h(2)
         cast_w2(2, 0, 1, "vector")
@@ -352,19 +389,23 @@ def tile_moe_pkd_mlp_relu2_kernel(tc, x_words, x_scales, w1, w2, gate, offs, out
         quant_w2(2, 1, NB)
         second_products(2)
         relu_square(LAST)
-        cast_w2(LAST, 0, NB, "vector")
+        cast_w2(LAST, 0, 1, "vector")
         deliver(2, 0)
-        quant_w2(LAST, 0, NB)
+        cast_w2(LAST, 1, NB, "vector")
+        quant_w2(LAST, 0, 1)
         quant_h(LAST)
-        second_products(LAST)
+        second_product(LAST, 0)
+        quant_w2(LAST, 1, NB)
+        second_product(LAST, 1)
+        second_product(LAST, 2)
 
         deliver(2, 1)
         deliver(2, 2)
         weigh(LAST, 0)
         weigh(LAST, 1)
+        weigh(LAST, 2)
         scatter(LAST, 0, "vector")
         store(0)
-        weigh(LAST, 2)
         scatter(LAST, 1, "vector")
         store(1)
         scatter(LAST, 2, "scalar")

@@ -149,14 +149,13 @@ def tile_moe_pkd_mlp_relu2_kernel(tc, x_words, x_scales, w1, w2, gate, offs, out
             for u in range(2):
                 w1b[e, g, u] = tile[:, u * 2 * H : (u + 1) * 2 * H]
 
-        def first_pass(e):
+        def quant_first_pass(e):
             codes = ring.tile([P, H], U32, name="codes", align_bytes=64, bufs=2)
             scales = stream([P, H], U8)
             nc.vector.quantize_mx(out=codes[:].bitcast(FP8X4), scales=scales[:], in_=whole[e, 0][:])
             for u in range(2):
                 w1c[e, 0, u] = codes[:, u * 2 * P : (u + 1) * 2 * P]
                 w1s[e, 0, u] = scales[:, u * 2 * P : (u + 1) * 2 * P]
-                multiply_w1(e, 0, u)
 
         whole = {}
         acc1 = {}
@@ -165,6 +164,10 @@ def tile_moe_pkd_mlp_relu2_kernel(tc, x_words, x_scales, w1, w2, gate, offs, out
             w1c[e, g, u] = place([P, 2 * P], U32)
             w1s[e, g, u] = stream([P, 2 * P], U8)
             nc.vector.quantize_mx(out=w1c[e, g, u][:].bitcast(FP8X4), scales=w1s[e, g, u][:], in_=w1b[e, g, u])
+
+        def multiply_first_pass(e):
+            for u in range(2):
+                multiply_w1(e, 0, u)
 
         def first_product(e, g, u, place=held):
             quant_w1(e, g, u, place)
@@ -204,24 +207,23 @@ def tile_moe_pkd_mlp_relu2_kernel(tc, x_words, x_scales, w1, w2, gate, offs, out
                 w2c[e, b] = codes[:, (b - b0) * P : (b - b0 + 1) * P]
                 w2s[e, b] = scales[:, (b - b0) * P : (b - b0 + 1) * P]
 
-        relus = {}
         hb = {}
         hc = {}
         hs = {}
 
         def relu_square(e):
-            for u in range(2):
-                for h in range(2):
-                    if u == 0:
-                        relus[e, h] = stream([P, PACK, C // 2], F32)
-                    src = acc1[e, u][:, :, h * C // 2 : (h + 1) * C // 2]
-                    nc.scalar.activation(out=relus[e, h][:, 2 * u : 2 * u + 2, :], in_=src, func=ACT.Relu)
+            relus = stream([P, 2, PACK, C // 2], F32)
+            src = acc1[e, 0][:].rearrange("p t (h c) -> p h t c", h=2)
+            nc.scalar.activation(out=relus[:, :, 0:2, :], in_=src, func=ACT.Relu)
+            for h in range(2):
+                src = acc1[e, 1][:, :, h * C // 2 : (h + 1) * C // 2]
+                nc.scalar.activation(out=relus[:, h, 2:PACK, :], in_=src, func=ACT.Relu)
             hb[e] = stream([P, C * PACK], BF16)
             for h in range(2):
                 dst = hb[e][:, h * C * PACK // 2 : (h + 1) * C * PACK // 2]
                 nc.scalar.activation(
                     out=dst.rearrange("p (c i t) -> p c t i", i=PAIR, t=PACK),
-                    in_=relus[e, h][:].rearrange("p t (c i) -> p c t i", i=PAIR),
+                    in_=relus[:, h].rearrange("p t (c i) -> p c t i", i=PAIR),
                     func=ACT.Square,
                 )
 
@@ -266,18 +268,37 @@ def tile_moe_pkd_mlp_relu2_kernel(tc, x_words, x_scales, w1, w2, gate, offs, out
                 stop=True,
             )
 
+        def last_blocks(e):
+            acc2[e] = psum.tile([P, 2, C], F32, name="acc2")
+            for b in range(1, NB):
+                nc.tensor.matmul_mx(
+                    out=acc2[e][:, b - 1, :],
+                    lhsT=w2c[e, b].bitcast(FP8X4),
+                    lhsT_scale=w2s[e, b],
+                    rhs=hc[e][:].bitcast(FP8X4),
+                    rhs_scale=hs[e][:],
+                    start=True,
+                    stop=True,
+                )
+
         windows = [keep.tile([P, T], F32, name="window%d" % b, align_bytes=BURST) for b in range(NB)]
 
         def weigh(e, b):
-            ys[e, b] = stream([P, C], F32)
-            nc.vector.tensor_tensor(ys[e, b][:], acc2[e, b][:], gates[e], ALU.mult)
+            ys[e, b] = stream([P, C], F32)[:]
+            nc.vector.tensor_tensor(ys[e, b], acc2[e, b][:], gates[e], ALU.mult)
+
+        def weigh_last_blocks(e):
+            both = stream([P, 2, C], F32)
+            nc.vector.tensor_tensor(both[:], acc2[e][:], gates[e].unsqueeze(1).to_broadcast([P, 2, C]), ALU.mult)
+            for b in range(1, NB):
+                ys[e, b] = both[:, b - 1, :]
 
         def scatter(e, b, engine):
             dst = windows[b][:].indirect(slots(e, e + 1))
             if engine == "vector":
-                nc.vector.tensor_copy(dst, ys[e, b][:])
+                nc.vector.tensor_copy(dst, ys[e, b])
             else:
-                nc.scalar.activation(dst, ys[e, b][:], ACT.Copy)
+                nc.scalar.activation(dst, ys[e, b], ACT.Copy)
 
         def deliver(e, b):
             weigh(e, b)
@@ -295,10 +316,6 @@ def tile_moe_pkd_mlp_relu2_kernel(tc, x_words, x_scales, w1, w2, gate, offs, out
 
         def store(b):
             nc.sync.dma_start(out=out[b * P : (b + 1) * P, :], in_=windows[b][:])
-
-        def second_products(e):
-            for b in range(NB):
-                second_product(e, b)
 
         load_x(0)
         nc.sync.dma_start(offsets[:], offs)
@@ -338,18 +355,21 @@ def tile_moe_pkd_mlp_relu2_kernel(tc, x_words, x_scales, w1, w2, gate, offs, out
         cast_w2(0, 0, 2, "vector", wide)
         gather_words(2, E, 1, wide)
         quant_w2(0, 0, 2)
-        quant_h(0)
-        second_product(0, 0)
-        second_product(0, 1)
-
-        cast_w2(0, 2, NB, "scalar")
+        quant_h_half(0, 0)
+        first_block_half(0, 0)
         cast_w1_half(1, 0, 0, "scalar")
         cast_w1_half(1, 0, 1, "vector")
-        deliver(0, 0)
+        quant_h_half(0, 1)
+        second_product(0, 1)
+        first_block_half(0, 1)
+
+        deliver_first_half(0, 0)
+        cast_w2(0, 2, NB, "scalar")
         first_product(1, 0, 1)
-        deliver(0, 1)
         first_product(1, 0, 0)
+        deliver(0, 1)
         cast_w1(1, 1)
+        deliver_first_half(0, 1)
         quant_w2(0, 2, NB)
         second_product(0, 2)
         first_products(1, 1)
@@ -357,53 +377,48 @@ def tile_moe_pkd_mlp_relu2_kernel(tc, x_words, x_scales, w1, w2, gate, offs, out
         relu_square(1)
         deliver(0, 2)
         quant_w2(1, 0, NB)
-        cast_w1_half(2, 0, 0, "vector")
+        cast_w1(2, 0)
         quant_h_half(1, 0)
         first_block_half(1, 0)
-        cast_w1_half(2, 0, 1, "vector")
+        quant_first_pass(2)
         quant_h_half(1, 1)
         second_product(1, 1)
         first_block_half(1, 1)
         second_product(1, 2)
+        multiply_first_pass(2)
 
         deliver_first_half(1, 0)
-        quant_w1(2, 0, 0)
-        quant_w1(2, 0, 1)
+        cast_w1_half(2, 1, 0, "vector")
         deliver(1, 1)
-        multiply_w1(2, 0, 0)
-        multiply_w1(2, 0, 1)
-        cast_w1(2, 1)
+        cast_w1_half(2, 1, 1, "vector")
         deliver_first_half(1, 1)
         first_products(2, 1)
         cast_w1(LAST, 0)
         relu_square(2)
         deliver(1, 2)
-        first_pass(LAST)
+        quant_first_pass(LAST)
+        multiply_first_pass(LAST)
         cast_w1_half(LAST, 1, 0, "vector")
         cast_w1_half(LAST, 1, 1, "vector")
         first_products(LAST, 1)
+        cast_w2(2, 0, NB, "vector")
         quant_h(2)
-        cast_w2(2, 0, 1, "vector")
-        cast_w2(2, 1, NB, "vector")
-        quant_w2(2, 0, 1)
-        quant_w2(2, 1, NB)
-        second_products(2)
+        quant_w2(2, 0, NB)
+        second_product(2, 0)
+        last_blocks(2)
         relu_square(LAST)
-        cast_w2(LAST, 0, 1, "vector")
+        cast_w2(LAST, 0, NB, "vector")
         deliver(2, 0)
-        cast_w2(LAST, 1, NB, "vector")
-        quant_w2(LAST, 0, 1)
+        quant_w2(LAST, 0, NB)
         quant_h(LAST)
         second_product(LAST, 0)
-        quant_w2(LAST, 1, NB)
-        second_product(LAST, 1)
-        second_product(LAST, 2)
+        last_blocks(LAST)
 
-        deliver(2, 1)
-        deliver(2, 2)
+        weigh_last_blocks(2)
+        scatter(2, 1, "scalar")
+        scatter(2, 2, "scalar")
         weigh(LAST, 0)
-        weigh(LAST, 1)
-        weigh(LAST, 2)
+        weigh_last_blocks(LAST)
         scatter(LAST, 0, "vector")
         store(0)
         scatter(LAST, 1, "vector")

@@ -140,6 +140,12 @@ def tile_moe_pkd_mlp_relu2_kernel(tc, x_words, x_scales, w1, w2, gate, offs, out
             src = raw1[e, g][:].rearrange("p j (m u t) -> p u m j t", u=2, t=2)
             cast(engine, dst, src[:, u])
 
+        def shared(shape, dtype):
+            first = (2, 0) not in whole
+            if first:
+                whole[2, 0] = stream([P, 2 * shape[1]], dtype)
+            return whole[2, 0][:, : shape[1]] if first else whole[2, 0][:, shape[1] :]
+
         def cast_w1(e, g):
             tile = stream([P, PACK * H], BF16)
             dst = tile[:].rearrange("p (t m j) -> p m j t", t=PACK, j=PACK)
@@ -212,20 +218,17 @@ def tile_moe_pkd_mlp_relu2_kernel(tc, x_words, x_scales, w1, w2, gate, offs, out
         hs = {}
 
         def relu_square(e):
-            relus = stream([P, 2, PACK, C // 2], F32)
-            src = acc1[e, 0][:].rearrange("p t (h c) -> p h t c", h=2)
-            nc.scalar.activation(out=relus[:, :, 0:2, :], in_=src, func=ACT.Relu)
+            relus = stream([P, 2, C, 2], F32)
+            nc.scalar.activation(out=relus[:, 0], in_=acc1[e, 0][:].rearrange("p t s -> p s t"), func=ACT.Relu)
             for h in range(2):
-                src = acc1[e, 1][:, :, h * C // 2 : (h + 1) * C // 2]
-                nc.scalar.activation(out=relus[:, h, 2:PACK, :], in_=src, func=ACT.Relu)
+                cols = slice(h * P, (h + 1) * P)
+                src = acc1[e, 1][:, :, cols].rearrange("p t s -> p s t")
+                nc.scalar.activation(out=relus[:, 1, cols, :], in_=src, func=ACT.Relu)
             hb[e] = stream([P, C * PACK], BF16)
             for h in range(2):
-                dst = hb[e][:, h * C * PACK // 2 : (h + 1) * C * PACK // 2]
-                nc.scalar.activation(
-                    out=dst.rearrange("p (c i t) -> p c t i", i=PAIR, t=PACK),
-                    in_=relus[:, h].rearrange("p t (c i) -> p c t i", i=PAIR),
-                    func=ACT.Square,
-                )
+                dst = hb[e][:, h * P * PACK : (h + 1) * P * PACK].rearrange("p (s u t) -> p s u t", u=2, t=2)
+                src = relus[:, :, h * P : (h + 1) * P, :].rearrange("p u s t -> p s u t")
+                nc.scalar.activation(out=dst, in_=src, func=ACT.Square)
 
         def quant_h(e):
             hc[e] = held([P, C], U32)
@@ -377,20 +380,20 @@ def tile_moe_pkd_mlp_relu2_kernel(tc, x_words, x_scales, w1, w2, gate, offs, out
         relu_square(1)
         deliver(0, 2)
         quant_w2(1, 0, NB)
-        cast_w1(2, 0)
+        cast_w1_half(2, 0, 0, "vector", shared)
         quant_h_half(1, 0)
         first_block_half(1, 0)
-        quant_first_pass(2)
+        cast_w1_half(2, 0, 1, "vector", shared)
         quant_h_half(1, 1)
         second_product(1, 1)
         first_block_half(1, 1)
         second_product(1, 2)
-        multiply_first_pass(2)
 
         deliver_first_half(1, 0)
-        cast_w1_half(2, 1, 0, "vector")
+        quant_first_pass(2)
+        multiply_first_pass(2)
         deliver(1, 1)
-        cast_w1_half(2, 1, 1, "vector")
+        cast_w1(2, 1)
         deliver_first_half(1, 1)
         first_products(2, 1)
         cast_w1(LAST, 0)
@@ -411,14 +414,14 @@ def tile_moe_pkd_mlp_relu2_kernel(tc, x_words, x_scales, w1, w2, gate, offs, out
         deliver(2, 0)
         quant_w2(LAST, 0, NB)
         quant_h(LAST)
-        second_product(LAST, 0)
-        last_blocks(LAST)
+        for b in range(NB):
+            second_product(LAST, b)
 
         weigh_last_blocks(2)
         scatter(2, 1, "scalar")
         scatter(2, 2, "scalar")
-        weigh(LAST, 0)
-        weigh_last_blocks(LAST)
+        for b in range(NB):
+            weigh(LAST, b)
         scatter(LAST, 0, "vector")
         store(0)
         scatter(LAST, 1, "vector")

from contextlib import ExitStack

import concourse.mybir as mybir
from concourse.masks import make_identity

K, T, E, C, H, N = 1024, 1024, 4, 256, 512, 384
FLOPS = 2 * E * C * (K * H + H * N)

F32 = mybir.dt.float32
BF16 = mybir.dt.bfloat16
I32 = mybir.dt.int32
U32 = mybir.dt.uint32
U16 = mybir.dt.uint16
U8 = mybir.dt.uint8
FP8X4 = mybir.dt.float8_e4m3fn_x4
ACT = mybir.ActivationFunctionType
ALU = mybir.AluOpType

P = 128
PACK = 4
K_PASS = P * PACK
PASSES = K // K_PASS
NB = N // P
GROUP = 16
RUN = E * C // P
BURST = 256
LINE = 4
PAIR = 2
LAST = E - 1
STREAM_BUFS = 24
HELD_BUFS = 20
WIDE_BUFS = 8
RAW_BUFS = 4
BANKS = 4


def tile_moe_pkd_mlp_relu2_kernel(tc, x_words, x_scales, w1, w2, gate, offs, out):
    nc = tc.nc
    with ExitStack() as ctx:
        keep = ctx.enter_context(tc.tile_pool(name="keep", bufs=1))
        ring = ctx.enter_context(tc.tile_pool(name="ring", bufs=STREAM_BUFS))
        psum = ctx.enter_context(tc.psum_pool(name="psum", bufs=BANKS))

        offsets = keep.tile([P, E * C // GROUP], U16, name="offsets")

        def stream(shape, dtype):
            return ring.tile(shape, dtype, name="stream", align_bytes=64)

        def held(shape, dtype):
            return ring.tile(shape, dtype, name="held", align_bytes=64, bufs=HELD_BUFS)

        def wide(shape, dtype):
            return ring.tile(shape, dtype, name="wide", align_bytes=64, bufs=WIDE_BUFS)

        def slots(e0, e1):
            return offsets[:, e0 * C // GROUP : e1 * C // GROUP]

        xs_win = keep.tile([P, T], U8, name="xs_win", align_bytes=BURST)
        nc.gpsimd.memset(xs_win[:].bitcast(I32), 0)

        def load_scales():
            for q in range(4):
                nc.sync.dma_start(
                    out=xs_win[32 * q : 32 * q + 4 * PASSES, :].bitcast(I32),
                    in_=x_scales[:, 4 * q : 4 * q + 4, :].bitcast(I32),
                )

        xw_win = [keep.tile([P, T], I32, name="xw_win%d" % g, align_bytes=BURST) for g in range(PASSES)]
        raw1 = {}
        raw2 = {}

        def load_x(g):
            nc.sync.dma_start(out=xw_win[g][:], in_=x_words[g].rearrange("p t r -> p (t r)").bitcast(I32))

        def load_w1(e, g):
            rows = w1[e, g * K_PASS : (g + 1) * K_PASS, :].rearrange("(p j) c -> p j c", j=PACK)
            raw1[e, g] = ring.tile([P, PACK, H], F32, name="raw1", bufs=RAW_BUFS, align_bytes=BURST)
            nc.sync.dma_start(out=raw1[e, g][:], in_=rows)

        def load_w2(e):
            raw2[e] = keep.tile([P, PACK, N], F32, name="raw2_%d" % e, align_bytes=BURST)
            nc.sync.dma_start(out=raw2[e][:], in_=w2[e].rearrange("(p j) c -> p j c", j=PACK))

        gate_row = keep.tile([P, RUN], F32, name="gate_row")
        identity = keep.tile([P, P], F32, name="identity")
        make_identity(nc, identity[:])
        gates = {}

        def load_gate():
            nc.sync.dma_start(out=gate_row[:], in_=gate[0].rearrange("(p j) -> p j", j=RUN))

        def early(shape, dtype):
            return ring.tile(shape, dtype, name="early", align_bytes=64, bufs=2)

        turned = {}

        def turn_gate():
            for h in range(2):
                turned[h] = psum.tile([P, LINE, P], F32, name="acc2")
                for j in range(LINE):
                    column = gate_row[:, h * LINE + j : h * LINE + j + 1].to_broadcast([P, P])
                    nc.tensor.transpose(turned[h][:, j, :], column, identity[:])

        def spread_gate():
            tile = early([P, E * C], F32)
            for h in range(2):
                dst = tile[:].rearrange("p (n h j) -> p h n j", h=2, j=LINE)
                nc.scalar.copy(out=dst[:, h], in_=turned[h][:].rearrange("p j n -> p n j"))
            for e in range(E):
                gates[e] = tile[:, e * C : (e + 1) * C]

        xw = {}
        xs = {}

        def gather_scales(e0, e1, place):
            tile = place([P, (e1 - e0) * C], U8)
            nc.vector.tensor_copy(tile[:], xs_win[:].indirect(slots(e0, e1)))
            for e in range(e0, e1):
                xs[e] = tile[:, (e - e0) * C : (e - e0 + 1) * C]

        def gather_words(e0, e1, g, place):
            tile = place([P, (e1 - e0) * C], U32)
            nc.vector.tensor_copy(tile[:], xw_win[g][:].bitcast(U32).indirect(slots(e0, e1)))
            for e in range(e0, e1):
                xw[e, g] = tile[:, (e - e0) * C : (e - e0 + 1) * C]

        def cast(engine, dst, src):
            if engine == "vector":
                nc.vector.tensor_copy(out=dst, in_=src)
            else:
                nc.scalar.copy(out=dst, in_=src)

        w1b = {}
        w1c = {}
        w1s = {}

        def cast_w1_half(e, g, u, engine, place=stream):
            w1b[e, g, u] = place([P, 2 * H], BF16)[:]
            dst = w1b[e, g, u].rearrange("p (t m j) -> p m j t", t=2, j=PACK)
            src = raw1[e, g][:].rearrange("p j (m u t) -> p u m j t", u=2, t=2)
            cast(engine, dst, src[:, u])

        def shared(shape, dtype):
            first = (2, 0) not in whole
            if first:
                whole[2, 0] = stream([P, 2 * shape[1]], dtype)
            return whole[2, 0][:, : shape[1]] if first else whole[2, 0][:, shape[1] :]

        def cast_w1(e, g):
            tile = stream([P, PACK * H], BF16)
            dst = tile[:].rearrange("p (t m j) -> p m j t", t=PACK, j=PACK)
            src = raw1[e, g][:].rearrange("p j (m t) -> p m j t", t=PACK)
            nc.vector.tensor_copy(out=dst, in_=src)
            whole[e, g] = tile
            for u in range(2):
                w1b[e, g, u] = tile[:, u * 2 * H : (u + 1) * 2 * H]

        def quant_first_pass(e):
            codes = ring.tile([P, H], U32, name="codes", align_bytes=64, bufs=2)
            scales = stream([P, H], U8)
            nc.vector.quantize_mx(out=codes[:].bitcast(FP8X4), scales=scales[:], in_=whole[e, 0][:])
            for u in range(2):
                w1c[e, 0, u] = codes[:, u * 2 * P : (u + 1) * 2 * P]
                w1s[e, 0, u] = scales[:, u * 2 * P : (u + 1) * 2 * P]

        whole = {}
        acc1 = {}

        def quant_w1(e, g, u, place=held):
            w1c[e, g, u] = place([P, 2 * P], U32)
            w1s[e, g, u] = stream([P, 2 * P], U8)
            nc.vector.quantize_mx(out=w1c[e, g, u][:].bitcast(FP8X4), scales=w1s[e, g, u][:], in_=w1b[e, g, u])

        def multiply_first_pass(e):
            for u in range(2):
                multiply_w1(e, 0, u)

        def first_product(e, g, u, place=held):
            quant_w1(e, g, u, place)
            multiply_w1(e, g, u)

        def multiply_w1(e, g, u):
            opens = (e, u) not in acc1
            if opens:
                acc1[e, u] = psum.tile([P, 2, C], F32, name="acc1")
            for t in range(2):
                nc.tensor.matmul_mx(
                    out=acc1[e, u][:, t, :],
                    lhsT=w1c[e, g, u][:, t * P : (t + 1) * P].bitcast(FP8X4),
                    lhsT_scale=w1s[e, g, u][:, t * P : (t + 1) * P],
                    rhs=xw[e, g].bitcast(FP8X4),
                    rhs_scale=xs[e][4 * g : P, :],
                    start=opens and t == 0,
                    stop=(not opens) and t == 1,
                )

        w2b = {}
        w2c = {}
        w2s = {}

        def cast_w2(e, b0, b1, engine, place=stream):
            w2b[e, b0] = place([P, (b1 - b0) * P * PACK], BF16)
            run = LINE if engine == "vector" else PAIR
            dst = w2b[e, b0][:].rearrange("p (c i j) -> p c j i", i=run, j=PACK)
            src = raw2[e][:, :, b0 * P : b1 * P].rearrange("p j (c i) -> p c j i", i=run)
            cast(engine, dst, src)

        def quant_w2(e, b0, b1):
            codes = keep.tile([P, (b1 - b0) * P], U32, name="w2c%d_%d" % (e, b0), align_bytes=64)
            scales = stream([P, (b1 - b0) * P], U8)
            nc.vector.quantize_mx(out=codes[:].bitcast(FP8X4), scales=scales[:], in_=w2b[e, b0][:])
            for b in range(b0, b1):
                w2c[e, b] = codes[:, (b - b0) * P : (b - b0 + 1) * P]
                w2s[e, b] = scales[:, (b - b0) * P : (b - b0 + 1) * P]

        hb = {}
        hc = {}
        hs = {}

        def relu_square(e):
            relus = stream([P, 2, C, 2], F32)
            nc.scalar.activation(out=relus[:, 0], in_=acc1[e, 0][:].rearrange("p t s -> p s t"), func=ACT.Relu)
            for h in range(2):
                cols = slice(h * P, (h + 1) * P)
                src = acc1[e, 1][:, :, cols].rearrange("p t s -> p s t")
                nc.scalar.activation(out=relus[:, 1, cols, :], in_=src, func=ACT.Relu)
            hb[e] = stream([P, C * PACK], BF16)
            for h in range(2):
                dst = hb[e][:, h * P * PACK : (h + 1) * P * PACK].rearrange("p (s u t) -> p s u t", u=2, t=2)
                src = relus[:, :, h * P : (h + 1) * P, :].rearrange("p u s t -> p s u t")
                nc.scalar.activation(out=dst, in_=src, func=ACT.Square)

        def quant_h(e):
            hc[e] = held([P, C], U32)
            hs[e] = stream([P, C], U8)
            nc.vector.quantize_mx(out=hc[e][:].bitcast(FP8X4), scales=hs[e][:], in_=hb[e][:])

        def quant_h_half(e, h):
            if h == 0:
                hc[e] = held([P, C], U32)
                hs[e] = stream([P, C], U8)
            cols = slice(h * P, (h + 1) * P)
            src = hb[e][:, h * P * PACK : (h + 1) * P * PACK]
            nc.vector.quantize_mx(out=hc[e][:, cols].bitcast(FP8X4), scales=hs[e][:, cols], in_=src)

        acc2 = {}
        ys = {}

        def first_block_half(e, h):
            acc2[e, 0, h] = psum.tile([P, P], F32, name="acc2")
            cols = slice(h * P, (h + 1) * P)
            nc.tensor.matmul_mx(
                out=acc2[e, 0, h][:],
                lhsT=w2c[e, 0].bitcast(FP8X4),
                lhsT_scale=w2s[e, 0],
                rhs=hc[e][:, cols].bitcast(FP8X4),
                rhs_scale=hs[e][:, cols],
                start=True,
                stop=True,
            )

        def second_product(e, b):
            acc2[e, b] = psum.tile([P, C], F32, name="acc2")
            nc.tensor.matmul_mx(
                out=acc2[e, b][:],
                lhsT=w2c[e, b].bitcast(FP8X4),
                lhsT_scale=w2s[e, b],
                rhs=hc[e][:].bitcast(FP8X4),
                rhs_scale=hs[e][:],
                start=True,
                stop=True,
            )

        def last_blocks(e):
            acc2[e] = psum.tile([P, 2, C], F32, name="acc2")
            for b in range(1, NB):
                nc.tensor.matmul_mx(
                    out=acc2[e][:, b - 1, :],
                    lhsT=w2c[e, b].bitcast(FP8X4),
                    lhsT_scale=w2s[e, b],
                    rhs=hc[e][:].bitcast(FP8X4),
                    rhs_scale=hs[e][:],
                    start=True,
                    stop=True,
                )

        windows = [keep.tile([P, T], F32, name="window%d" % b, align_bytes=BURST) for b in range(NB)]

        def weigh(e, b):
            ys[e, b] = stream([P, C], F32)[:]
            nc.vector.tensor_tensor(ys[e, b], acc2[e, b][:], gates[e], ALU.mult)

        def weigh_last_blocks(e):
            both = stream([P, 2, C], F32)
            nc.vector.tensor_tensor(both[:], acc2[e][:], gates[e].unsqueeze(1).to_broadcast([P, 2, C]), ALU.mult)
            for b in range(1, NB):
                ys[e, b] = both[:, b - 1, :]

        def scatter(e, b, engine):
            dst = windows[b][:].indirect(slots(e, e + 1))
            if engine == "vector":
                nc.vector.tensor_copy(dst, ys[e, b])
            else:
                nc.scalar.activation(dst, ys[e, b], ACT.Copy)

        def deliver(e, b):
            weigh(e, b)
            scatter(e, b, "scalar")

        def deliver_first_half(e, h):
            y = stream([P, P], F32)
            nc.vector.tensor_tensor(y[:], acc2[e, 0, h][:], gates[e][:, h * P : (h + 1) * P], ALU.mult)
            first = (e * C + h * P) // GROUP
            nc.scalar.activation(windows[0][:].indirect(offsets[:, first : first + P // GROUP]), y[:], ACT.Copy)

        def first_products(e, g):
            for u in range(2):
                first_product(e, g, u)

        def store(b):
            nc.sync.dma_start(out=out[b * P : (b + 1) * P, :], in_=windows[b][:])

        load_x(0)
        nc.sync.dma_start(offsets[:], offs)
        load_scales()
        load_gate()
        load_w1(0, 0)
        load_w1(0, 1)
        load_x(1)
        load_w2(0)
        load_w1(1, 0)
        load_w1(1, 1)
        load_w2(1)
        for e in range(2, E):
            load_w1(e, 0)
            load_w1(e, 1)
        load_w2(2)
        load_w2(LAST)

        turn_gate()
        gather_words(0, E // 2, 0, wide)
        gather_words(E // 2, E, 0, wide)
        gather_scales(0, E // 2, wide)
        gather_scales(E // 2, E, wide)
        cast_w1_half(0, 0, 0, "scalar")
        cast_w1_half(0, 0, 1, "scalar")
        first_product(0, 0, 0)
        cast_w1_half(0, 1, 0, "vector")
        cast_w1_half(0, 1, 1, "scalar", early)
        spread_gate()
        first_product(0, 0, 1)
        quant_w1(0, 1, 0)
        gather_words(0, 1, 1, held)
        multiply_w1(0, 1, 0)
        first_product(0, 1, 1, wide)
        gather_words(1, 2, 1, wide)
        relu_square(0)
        cast_w2(0, 0, 2, "vector", wide)
        gather_words(2, E, 1, wide)
        quant_w2(0, 0, 2)
        quant_h_half(0, 0)
        first_block_half(0, 0)
        cast_w1_half(1, 0, 0, "scalar")
        cast_w1_half(1, 0, 1, "vector")
        quant_h_half(0, 1)
        second_product(0, 1)
        first_block_half(0, 1)

        deliver_first_half(0, 0)
        cast_w2(0, 2, NB, "scalar")
        first_product(1, 0, 1)
        first_product(1, 0, 0)
        deliver(0, 1)
        cast_w1(1, 1)
        deliver_first_half(0, 1)
        quant_w2(0, 2, NB)
        second_product(0, 2)
        first_products(1, 1)
        cast_w2(1, 0, NB, "vector")
        relu_square(1)
        deliver(0, 2)
        quant_w2(1, 0, NB)
        cast_w1_half(2, 0, 0, "vector", shared)
        quant_h_half(1, 0)
        first_block_half(1, 0)
        cast_w1_half(2, 0, 1, "vector", shared)
        quant_h_half(1, 1)
        second_product(1, 1)
        first_block_half(1, 1)
        second_product(1, 2)

        deliver_first_half(1, 0)
        quant_first_pass(2)
        multiply_first_pass(2)
        deliver(1, 1)
        cast_w1(2, 1)
        deliver_first_half(1, 1)
        first_products(2, 1)
        cast_w1(LAST, 0)
        relu_square(2)
        deliver(1, 2)
        quant_first_pass(LAST)
        multiply_first_pass(LAST)
        cast_w1_half(LAST, 1, 0, "vector")
        cast_w1_half(LAST, 1, 1, "vector")
        first_products(LAST, 1)
        cast_w2(2, 0, NB, "vector")
        quant_h(2)
        quant_w2(2, 0, NB)
        second_product(2, 0)
        last_blocks(2)
        relu_square(LAST)
        cast_w2(LAST, 0, NB, "vector")
        deliver(2, 0)
        quant_w2(LAST, 0, NB)
        quant_h(LAST)
        for b in range(NB):
            second_product(LAST, b)

        weigh_last_blocks(2)
        scatter(2, 1, "scalar")
        scatter(2, 2, "scalar")
        for b in range(NB):
            weigh(LAST, b)
        scatter(LAST, 0, "vector")
        store(0)
        scatter(LAST, 1, "vector")
        store(1)
        scatter(LAST, 2, "scalar")
        store(2)
